import numpy as np
import ml_dtypes


def mxq(x, axis, fmt="e4m3"):
    dtype, down = {"e4m3": (ml_dtypes.float8_e4m3fn, 7), "e5m2": (ml_dtypes.float8_e5m2, 14)}[fmt]
    v = np.moveaxis(np.asarray(x, np.float32).astype(ml_dtypes.bfloat16).astype(np.float64), axis, -1)
    blocks = v.reshape(v.shape[:-1] + (-1, 32))
    amax = np.abs(blocks).max(-1, keepdims=True)
    byte = np.maximum(np.where(amax > 0, np.frexp(amax)[1] - 1 + 127, 0) - down, 1)
    scale = np.exp2(byte - 127.0)
    codes = (blocks / scale).astype(np.float32).astype(dtype).astype(np.float64)
    return np.moveaxis((codes * scale).reshape(v.shape), -1, axis)


WIDE = False


def mx_kscale(k):
    if not WIDE:
        return np.ones(k)
    levels = np.array([10, -10, 5, -5, 0])
    if k % 512:
        return np.exp2(np.random.permutation(np.resize(levels, k // 32))).repeat(32)
    a = np.empty((k // 512, 16))
    for p in range(k // 512):
        a[p, :8] = np.random.permutation(np.resize(levels, 8))
        for g in range(8):
            far = levels[np.abs(levels - a[p, g]) >= 10]
            a[p, g + 8] = far[np.random.randint(len(far))]
    return np.exp2(a.ravel()).repeat(32)


def f64(x):
    return np.asarray(x).astype(np.float64)


def striped(idx):
    return np.tile(idx.reshape(-1, 16).T, (8, 1)).astype(np.uint16)


def unstriped(offs):
    return offs[:16].T.reshape(-1).astype(np.int64)


E2M1 = np.array([0.0, 0.5, 1.0, 1.5, 2.0, 3.0, 4.0, 6.0, -0.0, -0.5, -1.0, -1.5, -2.0, -3.0, -4.0, -6.0])


def pack_weight(w, fmt):
    k, n = w.shape
    w = f64(np.asarray(w, np.float32).astype(ml_dtypes.bfloat16)).reshape(k // 32, 32, n)
    amax = np.abs(w).max(1)
    if fmt == "e4m3":
        byte = np.frexp(amax)[1] - 1 + 127 - 7
    else:
        mant, ex = np.frexp(amax / 6.0)
        byte = np.where(mant > 0.5, ex, ex - 1) + 127
    byte = np.clip(np.where(amax > 0, byte, 1), 1, 254)
    scaled = (w * np.exp2(127.0 - byte)[:, None, :]).reshape(k, n).astype(np.float32)
    by_word = np.ascontiguousarray(scaled.reshape(k // 512, 128, 4, n).transpose(0, 1, 3, 2))
    if fmt == "e4m3":
        words = by_word.astype(ml_dtypes.float8_e4m3fn).view(np.uint8)
    else:
        c = by_word.astype(ml_dtypes.float4_e2m1fn).view(np.uint8) & 0xF
        words = (c[..., 0::2] | (c[..., 1::2] << 4)).reshape(k // 512, 128, 2 * n)
    return np.ascontiguousarray(words), np.ascontiguousarray(byte.astype(np.uint8).reshape(k // 512, 16, n))


def unpack_weight(words, scales, fmt):
    g, _, n = scales.shape
    words = np.ascontiguousarray(words).reshape(g, 128, n, -1)
    if fmt == "e4m3":
        vals = words.view(ml_dtypes.float8_e4m3fn).astype(np.float64)
    else:
        nib = np.empty((g, 128, n, 4), np.uint8)
        nib[..., 0::2] = words & 0xF
        nib[..., 1::2] = words >> 4
        vals = E2M1[nib]
    vals = vals * np.repeat(np.exp2(scales.astype(np.float64) - 127.0), 8, axis=1)[..., None]
    return vals.transpose(0, 1, 3, 2).reshape(g * 512, n)


def relu2(v):
    return np.maximum(v, 0.0) ** 2


K, T, E, C, H, N = 1536, 768, 12, 128, 512, 128


def by_expert(wq, xq):
    return np.concatenate([wq[e].T @ xq[:, e * C:(e + 1) * C] for e in range(E)], axis=1)


def setup_inputs():
    n = np.random.standard_normal
    s = mx_kscale(K)
    u = mx_kscale(H)
    first = np.random.permutation(np.repeat(np.arange(E), T // E))
    second = (first + 1 + np.random.permutation(np.repeat(np.arange(E - 1), -(-T // (E - 1)))[:T])) % E
    while np.bincount(second, minlength=E).max() != T // E:
        load = np.bincount(second, minlength=E); hi, lo = int(load.argmax()), int(load.argmin())
        t = np.flatnonzero((second == hi) & (first != lo))[0]; second[t] = lo
    slot_token = np.empty(E * C, np.int64); pos = np.empty((2, T), np.int64); fill = np.zeros(E, np.int64)
    place = np.stack([np.random.permutation(C) for _ in range(E)])
    for r, deal in enumerate((first, second)):
        for t in np.random.permutation(T):
            e = deal[t]; j = e * C + place[e, fill[e]]; fill[e] += 1; slot_token[j] = t; pos[r, t] = j
    g = np.random.uniform(0.2, 0.8, T)
    x = pack_weight(n((K, T)) * s[:, None], "e4m3")
    w1 = pack_weight(n((K, H)) / np.sqrt(K) / s[:, None] * u, "e2m1")
    return {
        "x_words": x[0],
        "x_scales": x[1],
        "w1_words": w1[0],
        "w1_scales": w1[1],
        "w2": (n((E, H, N)) / np.sqrt(H) / u[None, :, None] ** 2).astype(np.float32),
        "gate": np.stack([np.tile(g, (128, 1)), np.tile(1.0 - g, (128, 1))]).astype(np.float32),
        "offs": striped(slot_token),
        "pos1": striped(pos[0]),
        "pos2": striped(pos[1]),
    }


def reference(x_words, x_scales, w1_words, w1_scales, w2, gate, offs, pos1, pos2):
    w1 = unpack_weight(w1_words, w1_scales, "e2m1")
    w2q = mxq(f64(w2), 1, "e4m3")
    idx = unstriped(offs)
    x = unpack_weight(x_words, x_scales, "e4m3")
    h = relu2(w1.T @ x)
    y = by_expert(w2q, mxq(h[:, idx], 0, "e4m3"))
    out = sum(f64(gate[r, :1]) * y[:, unstriped(p)] for r, p in enumerate((pos1, pos2)))
    return out

@@ -1,0 +1,192 @@
+from contextlib import ExitStack
+
+import concourse.mybir as mybir
+
+K, T, E, C, H, N = 1536, 768, 12, 128, 512, 128
+P = 128
+PASSES = K // 512
+S = E * C
+FLOPS = 2 * K * H * T + 2 * H * N * S
+
+F32 = mybir.dt.float32
+BF16 = mybir.dt.bfloat16
+I32 = mybir.dt.int32
+U32 = mybir.dt.uint32
+U16 = mybir.dt.uint16
+U8 = mybir.dt.uint8
+FP8X4 = mybir.dt.float8_e4m3fn_x4
+FP4X4 = mybir.dt.float4_e2m1fn_x4
+ALU = mybir.AluOpType
+ACT = mybir.ActivationFunctionType
+
+WIDE = 512
+SLOT_CHUNKS = (4, 4, 2, 2)
+TOKEN_CHUNKS = (320, 320, 128)
+VECTOR_PAIRS = (0, 5)
+
+
+def tile_moe_sup_lin_relu2_kernel(tc, x_words, x_scales, w1_words, w1_scales, w2, gate, offs, pos1, pos2, out):
+    nc = tc.nc
+    with ExitStack() as ctx:
+        keep = ctx.enter_context(tc.tile_pool(name="keep", bufs=1))
+        psum = ctx.enter_context(tc.psum_pool(name="psum", bufs=1))
+        ypsum = ctx.enter_context(tc.psum_pool(name="ypsum", bufs=2))
+
+        w1_raw = keep.tile([P, PASSES, 2 * H], U8, align_bytes=64)
+        w1s_raw = keep.tile([P, PASSES, H], U8, align_bytes=64)
+        xs = keep.tile([P, PASSES, T], U8, align_bytes=64)
+        xw = [keep.tile([P, 4 * T], U8, align_bytes=64, name=f"xw{s}") for s in range(PASSES)]
+        nc.gpsimd.memset(w1s_raw[:].bitcast(I32), 0)
+        nc.vector.memset(xs[:].bitcast(I32), 0)
+        warm = keep.tile([P, 8], F32)
+        warm2 = keep.tile([P, 8], F32)
+        nc.vector.memset(warm[:], 0.0)
+        nc.scalar.activation(warm2[:], warm[:], ACT.Square)
+
+        offs_sb = keep.tile([P, S // 16], U16)
+        nc.sync.dma_start(offs_sb[:], offs)
+        pos1_sb = keep.tile([P, T // 16], U16)
+        nc.sync.dma_start(pos1_sb[:], pos1)
+        pos2_sb = keep.tile([P, T // 16], U16)
+        nc.sync.dma_start(pos2_sb[:], pos2)
+        nc.sync.dma_start(out=w1_raw[:].bitcast(I32), in_=w1_words.rearrange("s p b -> p s b").bitcast(I32))
+        x_rows = x_words.rearrange("s p t d -> s p (t d)")
+        w1s_rows = w1_scales.rearrange("s (q r) i -> r q s i", r=4)
+        xs_rows = x_scales.rearrange("s (q r) t -> r q s t", r=4)
+        for r in range(4):
+            nc.sync.dma_start(out=w1s_raw[r:P:32, :, :].bitcast(I32), in_=w1s_rows[r].bitcast(I32))
+        for r in range(4):
+            queue = nc.sync
+            queue.dma_start(out=xs[r:P:32, :, :].bitcast(I32), in_=xs_rows[r].bitcast(I32))
+        for s in range(PASSES):
+            nc.sync.dma_start(out=xw[s][:].bitcast(I32), in_=x_rows[s].bitcast(I32))
+
+        w1w = [[keep.tile([P, H], U8, align_bytes=64, name=f"w1w{u}{s}") for s in range(PASSES)] for u in range(2)]
+        w1s = [[keep.tile([P, H // 2], U8, align_bytes=64, name=f"w1s{u}{s}") for s in range(PASSES)] for u in range(2)]
+        for u in range(2):
+            for s in range(PASSES):
+                nc.vector.tensor_copy(
+                    out=w1w[u][s][:].bitcast(U16).rearrange("p (b m) -> p b m", b=2),
+                    in_=w1_raw[:, s, :].bitcast(U16).rearrange("p (m j) -> p j m", j=4)[:, 2 * u : 2 * u + 2, :],
+                )
+                nc.vector.tensor_copy(
+                    out=w1s[u][s][:].rearrange("p (b m) -> p b m", b=2),
+                    in_=w1s_raw[:, s, :].rearrange("p (m j) -> p j m", j=4)[:, 2 * u : 2 * u + 2, :],
+                )
+        w2_raw = [keep.tile([P, 2, 4 * N], F32, name=f"w2_raw{g}") for g in range(E // 2)]
+        for g in range(E // 2):
+            nc.sync.dma_start(out=w2_raw[g][:], in_=w2[2 * g : 2 * g + 2].rearrange("e (p j) n -> p e (j n)", j=4))
+        gate_sb = keep.tile([P, 2, T], F32)
+        nc.sync.dma_start(out=gate_sb[:], in_=gate.rearrange("r p t -> p r t"))
+
+        def first_layer(acc, u, b, s, t0, t1):
+            nc.tensor.matmul_mx(
+                out=acc,
+                lhsT=w1w[u][s][:, 2 * P * b : 2 * P * (b + 1)].bitcast(FP4X4),
+                lhsT_scale=w1s[u][s][:, P * b : P * (b + 1)],
+                rhs=xw[s][:, 4 * t0 : 4 * t1].bitcast(FP8X4),
+                rhs_scale=xs[:, s, t0:t1],
+                start=(s == 0),
+                stop=(s == PASSES - 1),
+            )
+
+        w2_codes = [keep.tile([P, 2 * N], U32, align_bytes=64, name=f"w2_codes{g}") for g in range(E // 2)]
+        w2_scales = [keep.tile([P, 2 * N], U8, align_bytes=64, name=f"w2_scales{g}") for g in range(E // 2)]
+        w2_bf = [keep.tile([P, 2 * N * 4], BF16, align_bytes=64, name=f"w2_bf{g}") for g in range(E // 2)]
+
+        def cast_w2(g):
+            src = w2_raw[g][:].rearrange("p e (j c i) -> p e c j i", j=4, i=4)
+            dst = w2_bf[g][:].rearrange("p (e c i j) -> p e c j i", e=2, i=4, j=4)
+            if g in VECTOR_PAIRS:
+                nc.vector.tensor_copy(out=dst, in_=src)
+            else:
+                nc.scalar.copy(out=dst, in_=src)
+
+        def quantize_w2(g):
+            nc.vector.quantize_mx(out=w2_codes[g][:].bitcast(FP8X4), scales=w2_scales[g][:], in_=w2_bf[g][:])
+
+        h_pairs = [keep.tile([P, 2 * T], BF16, align_bytes=64, name=f"h_pairs{u}") for u in range(2)]
+        for u in range(2):
+            wide = [psum.tile([P, WIDE], F32, name=f"wide{b}") for b in range(2)]
+            rest = psum.tile([P, 2, T - WIDE], F32, name="rest")
+            for s in range(PASSES):
+                for b in range(2):
+                    first_layer(wide[b][:], u, b, s, 0, WIDE)
+            for b in range(2):
+                for t0 in range(WIDE, T, P):
+                    for s in range(PASSES):
+                        first_layer(rest[:, b, t0 - WIDE : t0 - WIDE + P], u, b, s, t0, t0 + P)
+            relu_wide = keep.tile([P, 2, WIDE], F32, name=f"relu_wide{u}")
+            relu_rest = keep.tile([P, T - WIDE, 2], F32, name=f"relu_rest{u}")
+            if u == 0:
+                for b in range(2):
+                    nc.vector.tensor_scalar_max(relu_wide[:, b, :], wide[b][:], 0.0)
+                nc.vector.tensor_scalar_max(relu_rest[:], rest[:].rearrange("p b t -> p t b"), 0.0)
+            else:
+                for b in range(2):
+                    nc.scalar.activation(relu_wide[:, b, :], wide[b][:], ACT.Relu)
+                nc.scalar.activation(relu_rest[:], rest[:].rearrange("p b t -> p t b"), ACT.Relu)
+            nc.scalar.activation(
+                h_pairs[u][:, : 2 * WIDE].rearrange("p (t b) -> p t b", b=2),
+                relu_wide[:].rearrange("p b t -> p t b"),
+                ACT.Square,
+            )
+            nc.scalar.activation(h_pairs[u][:, 2 * WIDE :], relu_rest[:].rearrange("p t b -> p (t b)"), ACT.Square)
+
+        firsts = [sum(SLOT_CHUNKS[:c]) for c in range(len(SLOT_CHUNKS))]
+        gathered = [keep.tile([P, 2, n * C], U32, name=f"gathered{c}") for c, n in enumerate(SLOT_CHUNKS)]
+
+        def gather_h(c, u):
+            cols = slice(firsts[c] * C // 16, (firsts[c] + SLOT_CHUNKS[c]) * C // 16)
+            nc.vector.tensor_copy(out=gathered[c][:, u, :], in_=h_pairs[u][:].bitcast(U32).indirect(offs_sb[:, cols]))
+
+        for c in range(len(SLOT_CHUNKS)):
+            gather_h(c, 0)
+        for g in range(E // 2):
+            cast_w2(g)
+            quantize_w2(g)
+
+        y = keep.tile([P, S], F32)
+        for c, n in enumerate(SLOT_CHUNKS):
+            gather_h(c, 1)
+            woven = keep.tile([P, n * C * 4], BF16, align_bytes=64, name=f"woven{c}")
+            if c < len(SLOT_CHUNKS) - 1:
+                nc.scalar.copy(
+                    out=woven[:].bitcast(U32).rearrange("p (s u) -> p s u", u=2),
+                    in_=gathered[c][:].rearrange("p u s -> p s u"),
+                )
+            else:
+                nc.vector.tensor_copy(
+                    out=woven[:].bitcast(I32).rearrange("p (s u) -> p s u", u=2),
+                    in_=gathered[c][:].bitcast(I32).rearrange("p u s -> p s u"),
+                )
+            h_codes = keep.tile([P, n * C], U32, align_bytes=64, name=f"h_codes{c}")
+            h_scales = keep.tile([P, n * C], U8, align_bytes=64, name=f"h_scales{c}")
+            nc.vector.quantize_mx(out=h_codes[:].bitcast(FP8X4), scales=h_scales[:], in_=woven[:])
+            acc = ypsum.tile([P, WIDE], F32, name="acc")
+            for m in range(n):
+                e = firsts[c] + m
+                w_cols = slice((e % 2) * N, (e % 2 + 1) * N)
+                cols = slice(m * C, (m + 1) * C)
+                nc.tensor.matmul_mx(
+                    out=acc[:, cols],
+                    lhsT=w2_codes[e // 2][:, w_cols].bitcast(FP8X4),
+                    lhsT_scale=w2_scales[e // 2][:, w_cols],
+                    rhs=h_codes[:, cols].bitcast(FP8X4),
+                    rhs_scale=h_scales[:, cols],
+                    start=True,
+                    stop=True,
+                )
+            nc.scalar.copy(out=y[:, firsts[c] * C : (firsts[c] + n) * C], in_=acc[:, : n * C])
+
+        t0 = 0
+        for c, n in enumerate(TOKEN_CHUNKS):
+            cols = slice(t0 // 16, (t0 + n) // 16)
+            first = keep.tile([P, n], F32, name=f"first{c}")
+            second = keep.tile([P, n], F32, name=f"second{c}")
+            total = keep.tile([P, n], F32, name=f"total{c}")
+            nc.vector.tensor_tensor(first[:], y[:].indirect(pos1_sb[:, cols]), gate_sb[:, 0, t0 : t0 + n], ALU.mult)
+            nc.vector.tensor_tensor(second[:], y[:].indirect(pos2_sb[:, cols]), gate_sb[:, 1, t0 : t0 + n], ALU.mult)
+            nc.vector.tensor_tensor(total[:], first[:], second[:], ALU.add)
+            nc.sync.dma_start(out=out[:, t0 : t0 + n], in_=total[:])
+            t0 = t0 + n

@@ -21,8 +21,7 @@ ACT = mybir.ActivationFunctionType
 
 WIDE = 512
 SLOT_CHUNKS = (4, 4, 2, 2)
-TOKEN_CHUNKS = (320, 320, 128)
-VECTOR_PAIRS = (0, 5)
+TOKEN_CHUNKS = (384, 256, 128)
 
 
 def tile_moe_sup_lin_relu2_kernel(tc, x_words, x_scales, w1_words, w1_scales, w2, gate, offs, pos1, pos2, out):
@@ -30,36 +29,37 @@ def tile_moe_sup_lin_relu2_kernel(tc, x_words, x_scales, w1_words, w1_scales, w2
     with ExitStack() as ctx:
         keep = ctx.enter_context(tc.tile_pool(name="keep", bufs=1))
         psum = ctx.enter_context(tc.psum_pool(name="psum", bufs=1))
-        ypsum = ctx.enter_context(tc.psum_pool(name="ypsum", bufs=2))
+        ypsum = ctx.enter_context(tc.psum_pool(name="ypsum", bufs=4))
 
         w1_raw = keep.tile([P, PASSES, 2 * H], U8, align_bytes=64)
         w1s_raw = keep.tile([P, PASSES, H], U8, align_bytes=64)
         xs = keep.tile([P, PASSES, T], U8, align_bytes=64)
         xw = [keep.tile([P, 4 * T], U8, align_bytes=64, name=f"xw{s}") for s in range(PASSES)]
-        nc.gpsimd.memset(w1s_raw[:].bitcast(I32), 0)
-        nc.vector.memset(xs[:].bitcast(I32), 0)
         warm = keep.tile([P, 8], F32)
         warm2 = keep.tile([P, 8], F32)
+        w1s_rows = keep.tile([P, PASSES * H // 4], I32)
+        nc.vector.memset(xs[:].bitcast(I32), 0)
         nc.vector.memset(warm[:], 0.0)
-        nc.scalar.activation(warm2[:], warm[:], ACT.Square)
+        nc.vector.memset(w1s_raw[:].bitcast(I32), 0)
 
-        offs_sb = keep.tile([P, S // 16], U16)
-        nc.sync.dma_start(offs_sb[:], offs)
-        pos1_sb = keep.tile([P, T // 16], U16)
-        nc.sync.dma_start(pos1_sb[:], pos1)
-        pos2_sb = keep.tile([P, T // 16], U16)
-        nc.sync.dma_start(pos2_sb[:], pos2)
-        nc.sync.dma_start(out=w1_raw[:].bitcast(I32), in_=w1_words.rearrange("s p b -> p s b").bitcast(I32))
+        w1s_hbm = w1_scales.rearrange("s (q r) i -> q r s i", r=4)
+        for q in range(4):
+            queue = nc.sync if q < 2 else nc.scalar
+            queue.dma_start(
+                out=w1s_rows[32 * q : 32 * q + 4, :].rearrange("p (s i) -> p s i", s=PASSES), in_=w1s_hbm[q].bitcast(I32)
+            )
+        nc.scalar.dma_start(out=w1_raw[:].bitcast(I32), in_=w1_words.rearrange("s p b -> p s b").bitcast(I32))
         x_rows = x_words.rearrange("s p t d -> s p (t d)")
-        w1s_rows = w1_scales.rearrange("s (q r) i -> r q s i", r=4)
         xs_rows = x_scales.rearrange("s (q r) t -> r q s t", r=4)
+        nc.scalar.dma_start(out=xw[0][:].bitcast(I32), in_=x_rows[0].bitcast(I32))
+        nc.scalar.activation(warm2[:], warm[:], ACT.Square)
         for r in range(4):
-            nc.sync.dma_start(out=w1s_raw[r:P:32, :, :].bitcast(I32), in_=w1s_rows[r].bitcast(I32))
-        for r in range(4):
-            queue = nc.sync
-            queue.dma_start(out=xs[r:P:32, :, :].bitcast(I32), in_=xs_rows[r].bitcast(I32))
-        for s in range(PASSES):
+            nc.sync.dma_start(out=xs[r:P:32, :, :].bitcast(I32), in_=xs_rows[r].bitcast(I32))
+        for s in range(1, PASSES):
             nc.sync.dma_start(out=xw[s][:].bitcast(I32), in_=x_rows[s].bitcast(I32))
+        for q in range(4):
+            rows = slice(32 * q, 32 * q + 4)
+            nc.vector.tensor_copy(out=w1s_raw[rows].rearrange("p s i -> p (s i)").bitcast(I32), in_=w1s_rows[rows, :])
 
         w1w = [[keep.tile([P, H], U8, align_bytes=64, name=f"w1w{u}{s}") for s in range(PASSES)] for u in range(2)]
         w1s = [[keep.tile([P, H // 2], U8, align_bytes=64, name=f"w1s{u}{s}") for s in range(PASSES)] for u in range(2)]
@@ -73,9 +73,15 @@ def tile_moe_sup_lin_relu2_kernel(tc, x_words, x_scales, w1_words, w1_scales, w2
                     out=w1s[u][s][:].rearrange("p (b m) -> p b m", b=2),
                     in_=w1s_raw[:, s, :].rearrange("p (m j) -> p j m", j=4)[:, 2 * u : 2 * u + 2, :],
                 )
+        offs_sb = keep.tile([P, S // 16], U16)
+        nc.sync.dma_start(offs_sb[:], offs)
         w2_raw = [keep.tile([P, 2, 4 * N], F32, name=f"w2_raw{g}") for g in range(E // 2)]
         for g in range(E // 2):
             nc.sync.dma_start(out=w2_raw[g][:], in_=w2[2 * g : 2 * g + 2].rearrange("e (p j) n -> p e (j n)", j=4))
+        pos1_sb = keep.tile([P, T // 16], U16)
+        nc.sync.dma_start(pos1_sb[:], pos1)
+        pos2_sb = keep.tile([P, T // 16], U16)
+        nc.sync.dma_start(pos2_sb[:], pos2)
         gate_sb = keep.tile([P, 2, T], F32)
         nc.sync.dma_start(out=gate_sb[:], in_=gate.rearrange("r p t -> p r t"))
 
@@ -90,21 +96,6 @@ def tile_moe_sup_lin_relu2_kernel(tc, x_words, x_scales, w1_words, w1_scales, w2
                 stop=(s == PASSES - 1),
             )
 
-        w2_codes = [keep.tile([P, 2 * N], U32, align_bytes=64, name=f"w2_codes{g}") for g in range(E // 2)]
-        w2_scales = [keep.tile([P, 2 * N], U8, align_bytes=64, name=f"w2_scales{g}") for g in range(E // 2)]
-        w2_bf = [keep.tile([P, 2 * N * 4], BF16, align_bytes=64, name=f"w2_bf{g}") for g in range(E // 2)]
-
-        def cast_w2(g):
-            src = w2_raw[g][:].rearrange("p e (j c i) -> p e c j i", j=4, i=4)
-            dst = w2_bf[g][:].rearrange("p (e c i j) -> p e c j i", e=2, i=4, j=4)
-            if g in VECTOR_PAIRS:
-                nc.vector.tensor_copy(out=dst, in_=src)
-            else:
-                nc.scalar.copy(out=dst, in_=src)
-
-        def quantize_w2(g):
-            nc.vector.quantize_mx(out=w2_codes[g][:].bitcast(FP8X4), scales=w2_scales[g][:], in_=w2_bf[g][:])
-
         h_pairs = [keep.tile([P, 2 * T], BF16, align_bytes=64, name=f"h_pairs{u}") for u in range(2)]
         for u in range(2):
             wide = [psum.tile([P, WIDE], F32, name=f"wide{b}") for b in range(2)]
@@ -116,11 +107,11 @@ def tile_moe_sup_lin_relu2_kernel(tc, x_words, x_scales, w1_words, w1_scales, w2
                 for t0 in range(WIDE, T, P):
                     for s in range(PASSES):
                         first_layer(rest[:, b, t0 - WIDE : t0 - WIDE + P], u, b, s, t0, t0 + P)
-            relu_wide = keep.tile([P, 2, WIDE], F32, name=f"relu_wide{u}")
-            relu_rest = keep.tile([P, T - WIDE, 2], F32, name=f"relu_rest{u}")
+            relu_wide = keep.tile([P, 2, WIDE], F32, name=f"relu_wide{u}", tag=f"relu_wide{u}", align_bytes=64)
+            relu_rest = keep.tile([P, T - WIDE, 2], F32, name=f"relu_rest{u}", tag=f"relu_rest{u}", align_bytes=64)
             if u == 0:
-                for b in range(2):
-                    nc.vector.tensor_scalar_max(relu_wide[:, b, :], wide[b][:], 0.0)
+                nc.scalar.activation(relu_wide[:, 0, :], wide[0][:], ACT.Relu)
+                nc.vector.tensor_scalar_max(relu_wide[:, 1, :], wide[1][:], 0.0)
                 nc.vector.tensor_scalar_max(relu_rest[:], rest[:].rearrange("p b t -> p t b"), 0.0)
             else:
                 for b in range(2):
@@ -132,6 +123,25 @@ def tile_moe_sup_lin_relu2_kernel(tc, x_words, x_scales, w1_words, w1_scales, w2
                 ACT.Square,
             )
             nc.scalar.activation(h_pairs[u][:, 2 * WIDE :], relu_rest[:].rearrange("p t b -> p (t b)"), ACT.Square)
+
+        own_bf = [keep.tile([P, 8 * N], BF16, align_bytes=64, name=f"own_bf{g}") for g in range(2)]
+        late_bf = keep.tile([P, E // 2 - 2, 8 * N], BF16, align_bytes=64, tag="relu_rest1")
+        w2_bf = [own_bf[0][:]] + [late_bf[:, g, :] for g in range(E // 2 - 2)] + [own_bf[1][:]]
+        first_codes = keep.tile([P, 2 * N], U32, align_bytes=64)
+        late_codes = keep.tile([P, E // 2 - 1, 2 * N], U32, align_bytes=64, tag="relu_rest0")
+        w2_codes = [first_codes[:]] + [late_codes[:, g, :] for g in range(E // 2 - 1)]
+        w2_scales = [keep.tile([P, 2 * N], U8, align_bytes=64, name=f"w2_scales{g}") for g in range(E // 2)]
+
+        def cast_w2(g):
+            src = w2_raw[g][:].rearrange("p e (j c i) -> p e c j i", j=4, i=4)
+            dst = w2_bf[g].rearrange("p (e c i j) -> p e c j i", e=2, i=4, j=4)
+            if g in (0, E // 2 - 1):
+                nc.vector.tensor_copy(out=dst, in_=src)
+            else:
+                nc.scalar.copy(out=dst, in_=src)
+
+        def quantize_w2(g):
+            nc.vector.quantize_mx(out=w2_codes[g].bitcast(FP8X4), scales=w2_scales[g][:], in_=w2_bf[g])
 
         firsts = [sum(SLOT_CHUNKS[:c]) for c in range(len(SLOT_CHUNKS))]
         gathered = [keep.tile([P, 2, n * C], U32, name=f"gathered{c}") for c, n in enumerate(SLOT_CHUNKS)]
@@ -150,16 +160,10 @@ def tile_moe_sup_lin_relu2_kernel(tc, x_words, x_scales, w1_words, w1_scales, w2
         for c, n in enumerate(SLOT_CHUNKS):
             gather_h(c, 1)
             woven = keep.tile([P, n * C * 4], BF16, align_bytes=64, name=f"woven{c}")
-            if c < len(SLOT_CHUNKS) - 1:
-                nc.scalar.copy(
-                    out=woven[:].bitcast(U32).rearrange("p (s u) -> p s u", u=2),
-                    in_=gathered[c][:].rearrange("p u s -> p s u"),
-                )
-            else:
-                nc.vector.tensor_copy(
-                    out=woven[:].bitcast(I32).rearrange("p (s u) -> p s u", u=2),
-                    in_=gathered[c][:].bitcast(I32).rearrange("p u s -> p s u"),
-                )
+            nc.scalar.copy(
+                out=woven[:].bitcast(U32).rearrange("p (s u) -> p s u", u=2),
+                in_=gathered[c][:].rearrange("p u s -> p s u"),
+            )
             h_codes = keep.tile([P, n * C], U32, align_bytes=64, name=f"h_codes{c}")
             h_scales = keep.tile([P, n * C], U8, align_bytes=64, name=f"h_scales{c}")
             nc.vector.quantize_mx(out=h_codes[:].bitcast(FP8X4), scales=h_scales[:], in_=woven[:])
@@ -177,7 +181,10 @@ def tile_moe_sup_lin_relu2_kernel(tc, x_words, x_scales, w1_words, w1_scales, w2
                     start=True,
                     stop=True,
                 )
-            nc.scalar.copy(out=y[:, firsts[c] * C : (firsts[c] + n) * C], in_=acc[:, : n * C])
+            if c % 2 == 0:
+                nc.scalar.copy(out=y[:, firsts[c] * C : (firsts[c] + n) * C], in_=acc[:, : n * C])
+            else:
+                nc.vector.tensor_copy(out=y[:, firsts[c] * C : (firsts[c] + n) * C], in_=acc[:, : n * C])
 
         t0 = 0
         for c, n in enumerate(TOKEN_CHUNKS):

@@ -34,7 +34,8 @@ def tile_moe_sup_lin_relu2_kernel(tc, x_words, x_scales, w1_words, w1_scales, w2
         w1_raw = keep.tile([P, PASSES, 2 * H], U8, align_bytes=64)
         w1s_raw = keep.tile([P, PASSES, H], U8, align_bytes=64)
         xs = keep.tile([P, PASSES, T], U8, align_bytes=64)
-        xw = [keep.tile([P, 4 * T], U8, align_bytes=64, name=f"xw{s}") for s in range(PASSES)]
+        x_wide = [keep.tile([P, 4 * WIDE], U8, align_bytes=64, name=f"x_wide{s}") for s in range(PASSES)]
+        x_rest = keep.tile([P, PASSES, 4 * (T - WIDE)], U8, align_bytes=64)
         warm = keep.tile([P, 8], F32)
         warm2 = keep.tile([P, 8], F32)
         w1s_rows = keep.tile([P, PASSES * H // 4], I32)
@@ -51,12 +52,13 @@ def tile_moe_sup_lin_relu2_kernel(tc, x_words, x_scales, w1_words, w1_scales, w2
         nc.scalar.dma_start(out=w1_raw[:].bitcast(I32), in_=w1_words.rearrange("s p b -> p s b").bitcast(I32))
         x_rows = x_words.rearrange("s p t d -> s p (t d)")
         xs_rows = x_scales.rearrange("s (q r) t -> r q s t", r=4)
-        nc.scalar.dma_start(out=xw[0][:].bitcast(I32), in_=x_rows[0].bitcast(I32))
+        nc.scalar.dma_start(out=x_wide[0][:].bitcast(I32), in_=x_rows[0, :, : 4 * WIDE].bitcast(I32))
         nc.scalar.activation(warm2[:], warm[:], ACT.Square)
         for r in range(4):
             nc.sync.dma_start(out=xs[r:P:32, :, :].bitcast(I32), in_=xs_rows[r].bitcast(I32))
         for s in range(1, PASSES):
-            nc.sync.dma_start(out=xw[s][:].bitcast(I32), in_=x_rows[s].bitcast(I32))
+            nc.sync.dma_start(out=x_wide[s][:].bitcast(I32), in_=x_rows[s, :, : 4 * WIDE].bitcast(I32))
+        nc.sync.dma_start(out=x_rest[:].bitcast(I32), in_=x_rows[:, :, 4 * WIDE :].rearrange("s p b -> p s b").bitcast(I32))
         for q in range(4):
             rows = slice(32 * q, 32 * q + 4)
             nc.vector.tensor_copy(out=w1s_raw[rows].rearrange("p s i -> p (s i)").bitcast(I32), in_=w1s_rows[rows, :])
@@ -86,14 +88,32 @@ def tile_moe_sup_lin_relu2_kernel(tc, x_words, x_scales, w1_words, w1_scales, w2
         nc.sync.dma_start(out=gate_sb[:], in_=gate.rearrange("r p t -> p r t"))
 
         def first_layer(acc, u, b, s, t0, t1):
+            words = x_wide[s][:] if t0 == 0 else x_rest[:, s, 4 * (t0 - WIDE) : 4 * (t1 - WIDE)]
             nc.tensor.matmul_mx(
                 out=acc,
                 lhsT=w1w[u][s][:, 2 * P * b : 2 * P * (b + 1)].bitcast(FP4X4),
                 lhsT_scale=w1s[u][s][:, P * b : P * (b + 1)],
-                rhs=xw[s][:, 4 * t0 : 4 * t1].bitcast(FP8X4),
+                rhs=words.bitcast(FP8X4),
                 rhs_scale=xs[:, s, t0:t1],
                 start=(s == 0),
                 stop=(s == PASSES - 1),
+            )
+
+        zeros = keep.tile([P, 4 * P], BF16, align_bytes=64)
+        zero_codes = keep.tile([P, P], U32, align_bytes=64)
+        zero_scales = keep.tile([P, P], U8, align_bytes=64)
+        nc.vector.memset(zeros[:].bitcast(I32), 0)
+        nc.vector.quantize_mx(out=zero_codes[:].bitcast(FP8X4), scales=zero_scales[:], in_=zeros[:])
+        idle = psum.tile([P, WIDE], F32)
+        for i in range(8):
+            nc.tensor.matmul_mx(
+                out=idle[:, (i % 4) * P : (i % 4 + 1) * P],
+                lhsT=w1_raw[:, 0, : 2 * P].bitcast(FP4X4),
+                lhsT_scale=w1s_raw[:, 0, :P],
+                rhs=zero_codes[:].bitcast(FP8X4),
+                rhs_scale=zero_scales[:],
+                start=True,
+                stop=True,
             )
 
         h_pairs = [keep.tile([P, 2 * T], BF16, align_bytes=64, name=f"h_pairs{u}") for u in range(2)]
@@ -181,7 +201,7 @@ def tile_moe_sup_lin_relu2_kernel(tc, x_words, x_scales, w1_words, w1_scales, w2
                     start=True,
                     stop=True,
                 )
-            if c % 2 == 0:
+            if c < len(SLOT_CHUNKS) - 1:
                 nc.scalar.copy(out=y[:, firsts[c] * C : (firsts[c] + n) * C], in_=acc[:, : n * C])
             else:
                 nc.vector.tensor_copy(out=y[:, firsts[c] * C : (firsts[c] + n) * C], in_=acc[:, : n * C])

@@ -1,12 +1,16 @@
 from contextlib import ExitStack
 
 import concourse.mybir as mybir
+from concourse.masks import make_identity
 
 K, T, E, C, H, N = 1536, 768, 12, 128, 512, 128
 P = 128
-PASSES = K // 512
-S = E * C
-FLOPS = 2 * K * H * T + 2 * H * N * S
+PACK = 4
+PASSES = K // (P * PACK)
+SLOTS = E * C
+PAIRS = E // 2
+PER_COLUMN = 16
+FLOPS = 2 * K * H * T + 2 * H * N * SLOTS
 
 F32 = mybir.dt.float32
 BF16 = mybir.dt.bfloat16
@@ -21,199 +25,233 @@ ACT = mybir.ActivationFunctionType
 
 WIDE = 512
 SLOT_CHUNKS = (4, 4, 2, 2)
-TOKEN_CHUNKS = (384, 256, 128)
+VECTOR_PAIRS = (0, PAIRS - 1)
+TURNED_CHUNKS = (256, 256)
+WARM_PASSES = 8
 
 
 def tile_moe_sup_lin_relu2_kernel(tc, x_words, x_scales, w1_words, w1_scales, w2, gate, offs, pos1, pos2, out):
     nc = tc.nc
     with ExitStack() as ctx:
         keep = ctx.enter_context(tc.tile_pool(name="keep", bufs=1))
-        psum = ctx.enter_context(tc.psum_pool(name="psum", bufs=1))
-        ypsum = ctx.enter_context(tc.psum_pool(name="ypsum", bufs=4))
 
-        w1_raw = keep.tile([P, PASSES, 2 * H], U8, align_bytes=64)
-        w1s_raw = keep.tile([P, PASSES, H], U8, align_bytes=64)
-        xs = keep.tile([P, PASSES, T], U8, align_bytes=64)
-        x_wide = [keep.tile([P, 4 * WIDE], U8, align_bytes=64, name=f"x_wide{s}") for s in range(PASSES)]
-        x_rest = keep.tile([P, PASSES, 4 * (T - WIDE)], U8, align_bytes=64)
-        warm = keep.tile([P, 8], F32)
-        warm2 = keep.tile([P, 8], F32)
-        w1s_rows = keep.tile([P, PASSES * H // 4], I32)
-        nc.vector.memset(xs[:].bitcast(I32), 0)
-        nc.vector.memset(warm[:], 0.0)
-        nc.vector.memset(w1s_raw[:].bitcast(I32), 0)
+        with tc.psum_pool(name="psum", bufs=1) as psum, tc.psum_pool(name="y_psum", bufs=len(SLOT_CHUNKS)) as y_psum:
+            w1_raw = keep.tile([P, PASSES, 2 * H], U8, align_bytes=64)
+            w1_plane = keep.tile([P, PASSES, H], U8, align_bytes=64)
+            x_plane = keep.tile([P, PASSES, T], U8, align_bytes=64)
+            x_wide = [keep.tile([P, PACK * WIDE], U8, align_bytes=64, name=f"x_wide{s}") for s in range(PASSES)]
+            x_rest = keep.tile([P, PASSES, PACK * (T - WIDE)], U8, align_bytes=64)
+            table_in = keep.tile([P, 8], F32)
+            table_out = keep.tile([P, 8], F32)
+            w1_rows = keep.tile([P, PASSES * H // 4], I32)
+            nc.vector.memset(x_plane[:].bitcast(I32), 0)
+            nc.vector.memset(table_in[:], 0.0)
+            nc.vector.memset(w1_plane[:].bitcast(I32), 0)
 
-        w1s_hbm = w1_scales.rearrange("s (q r) i -> q r s i", r=4)
-        for q in range(4):
-            queue = nc.sync if q < 2 else nc.scalar
-            queue.dma_start(
-                out=w1s_rows[32 * q : 32 * q + 4, :].rearrange("p (s i) -> p s i", s=PASSES), in_=w1s_hbm[q].bitcast(I32)
-            )
-        nc.scalar.dma_start(out=w1_raw[:].bitcast(I32), in_=w1_words.rearrange("s p b -> p s b").bitcast(I32))
-        x_rows = x_words.rearrange("s p t d -> s p (t d)")
-        xs_rows = x_scales.rearrange("s (q r) t -> r q s t", r=4)
-        nc.scalar.dma_start(out=x_wide[0][:].bitcast(I32), in_=x_rows[0, :, : 4 * WIDE].bitcast(I32))
-        nc.scalar.activation(warm2[:], warm[:], ACT.Square)
-        for r in range(4):
-            nc.sync.dma_start(out=xs[r:P:32, :, :].bitcast(I32), in_=xs_rows[r].bitcast(I32))
-        for s in range(1, PASSES):
-            nc.sync.dma_start(out=x_wide[s][:].bitcast(I32), in_=x_rows[s, :, : 4 * WIDE].bitcast(I32))
-        nc.sync.dma_start(out=x_rest[:].bitcast(I32), in_=x_rows[:, :, 4 * WIDE :].rearrange("s p b -> p s b").bitcast(I32))
-        for q in range(4):
-            rows = slice(32 * q, 32 * q + 4)
-            nc.vector.tensor_copy(out=w1s_raw[rows].rearrange("p s i -> p (s i)").bitcast(I32), in_=w1s_rows[rows, :])
-
-        w1w = [[keep.tile([P, H], U8, align_bytes=64, name=f"w1w{u}{s}") for s in range(PASSES)] for u in range(2)]
-        w1s = [[keep.tile([P, H // 2], U8, align_bytes=64, name=f"w1s{u}{s}") for s in range(PASSES)] for u in range(2)]
-        for u in range(2):
-            for s in range(PASSES):
-                nc.vector.tensor_copy(
-                    out=w1w[u][s][:].bitcast(U16).rearrange("p (b m) -> p b m", b=2),
-                    in_=w1_raw[:, s, :].bitcast(U16).rearrange("p (m j) -> p j m", j=4)[:, 2 * u : 2 * u + 2, :],
+            w1_scale_rows = w1_scales.rearrange("s (q r) i -> q r s i", r=4)
+            for q in range(4):
+                queue = nc.sync if q < 2 else nc.scalar
+                queue.dma_start(
+                    out=w1_rows[32 * q : 32 * q + 4, :].rearrange("p (s i) -> p s i", s=PASSES),
+                    in_=w1_scale_rows[q].bitcast(I32),
                 )
-                nc.vector.tensor_copy(
-                    out=w1s[u][s][:].rearrange("p (b m) -> p b m", b=2),
-                    in_=w1s_raw[:, s, :].rearrange("p (m j) -> p j m", j=4)[:, 2 * u : 2 * u + 2, :],
-                )
-        offs_sb = keep.tile([P, S // 16], U16)
-        nc.sync.dma_start(offs_sb[:], offs)
-        w2_raw = [keep.tile([P, 2, 4 * N], F32, name=f"w2_raw{g}") for g in range(E // 2)]
-        for g in range(E // 2):
-            nc.sync.dma_start(out=w2_raw[g][:], in_=w2[2 * g : 2 * g + 2].rearrange("e (p j) n -> p e (j n)", j=4))
-        pos1_sb = keep.tile([P, T // 16], U16)
-        nc.sync.dma_start(pos1_sb[:], pos1)
-        pos2_sb = keep.tile([P, T // 16], U16)
-        nc.sync.dma_start(pos2_sb[:], pos2)
-        gate_sb = keep.tile([P, 2, T], F32)
-        nc.sync.dma_start(out=gate_sb[:], in_=gate.rearrange("r p t -> p r t"))
-
-        def first_layer(acc, u, b, s, t0, t1):
-            words = x_wide[s][:] if t0 == 0 else x_rest[:, s, 4 * (t0 - WIDE) : 4 * (t1 - WIDE)]
-            nc.tensor.matmul_mx(
-                out=acc,
-                lhsT=w1w[u][s][:, 2 * P * b : 2 * P * (b + 1)].bitcast(FP4X4),
-                lhsT_scale=w1s[u][s][:, P * b : P * (b + 1)],
-                rhs=words.bitcast(FP8X4),
-                rhs_scale=xs[:, s, t0:t1],
-                start=(s == 0),
-                stop=(s == PASSES - 1),
+            nc.scalar.dma_start(out=w1_raw[:].bitcast(I32), in_=w1_words.rearrange("s p b -> p s b").bitcast(I32))
+            x_rows = x_words.rearrange("s p t d -> s p (t d)")
+            x_scale_rows = x_scales.rearrange("s (q r) t -> r q s t", r=4)
+            nc.scalar.dma_start(out=x_wide[0][:].bitcast(I32), in_=x_rows[0, :, : PACK * WIDE].bitcast(I32))
+            nc.scalar.activation(table_out[:], table_in[:], ACT.Square)
+            for r in range(4):
+                nc.sync.dma_start(out=x_plane[r:P:32, :, :].bitcast(I32), in_=x_scale_rows[r].bitcast(I32))
+            for s in range(1, PASSES):
+                nc.sync.dma_start(out=x_wide[s][:].bitcast(I32), in_=x_rows[s, :, : PACK * WIDE].bitcast(I32))
+            nc.sync.dma_start(
+                out=x_rest[:].bitcast(I32), in_=x_rows[:, :, PACK * WIDE :].rearrange("s p b -> p s b").bitcast(I32)
             )
+            for q in range(4):
+                rows = slice(32 * q, 32 * q + 4)
+                nc.vector.tensor_copy(out=w1_plane[rows].rearrange("p s i -> p (s i)").bitcast(I32), in_=w1_rows[rows, :])
 
-        zeros = keep.tile([P, 4 * P], BF16, align_bytes=64)
-        zero_codes = keep.tile([P, P], U32, align_bytes=64)
-        zero_scales = keep.tile([P, P], U8, align_bytes=64)
-        nc.vector.memset(zeros[:].bitcast(I32), 0)
-        nc.vector.quantize_mx(out=zero_codes[:].bitcast(FP8X4), scales=zero_scales[:], in_=zeros[:])
-        idle = psum.tile([P, WIDE], F32)
-        for i in range(8):
-            nc.tensor.matmul_mx(
-                out=idle[:, (i % 4) * P : (i % 4 + 1) * P],
-                lhsT=w1_raw[:, 0, : 2 * P].bitcast(FP4X4),
-                lhsT_scale=w1s_raw[:, 0, :P],
-                rhs=zero_codes[:].bitcast(FP8X4),
-                rhs_scale=zero_scales[:],
-                start=True,
-                stop=True,
-            )
+            w1_codes = [[keep.tile([P, H], U8, align_bytes=64, name=f"w1_codes{u}{s}") for s in range(PASSES)] for u in range(2)]
+            w1_bytes = [[keep.tile([P, H // 2], U8, align_bytes=64, name=f"w1_bytes{u}{s}") for s in range(PASSES)] for u in range(2)]
+            for u in range(2):
+                for s in range(PASSES):
+                    nc.vector.tensor_copy(
+                        out=w1_codes[u][s][:].bitcast(U16).rearrange("p (b m) -> p b m", b=2),
+                        in_=w1_raw[:, s, :].bitcast(U16).rearrange("p (m j) -> p j m", j=PACK)[:, 2 * u : 2 * u + 2, :],
+                    )
+                    nc.vector.tensor_copy(
+                        out=w1_bytes[u][s][:].rearrange("p (b m) -> p b m", b=2),
+                        in_=w1_plane[:, s, :].rearrange("p (m j) -> p j m", j=PACK)[:, 2 * u : 2 * u + 2, :],
+                    )
 
-        h_pairs = [keep.tile([P, 2 * T], BF16, align_bytes=64, name=f"h_pairs{u}") for u in range(2)]
-        for u in range(2):
-            wide = [psum.tile([P, WIDE], F32, name=f"wide{b}") for b in range(2)]
-            rest = psum.tile([P, 2, T - WIDE], F32, name="rest")
-            for s in range(PASSES):
-                for b in range(2):
-                    first_layer(wide[b][:], u, b, s, 0, WIDE)
-            for b in range(2):
-                for t0 in range(WIDE, T, P):
-                    for s in range(PASSES):
-                        first_layer(rest[:, b, t0 - WIDE : t0 - WIDE + P], u, b, s, t0, t0 + P)
-            relu_wide = keep.tile([P, 2, WIDE], F32, name=f"relu_wide{u}", tag=f"relu_wide{u}", align_bytes=64)
-            relu_rest = keep.tile([P, T - WIDE, 2], F32, name=f"relu_rest{u}", tag=f"relu_rest{u}", align_bytes=64)
-            if u == 0:
-                nc.scalar.activation(relu_wide[:, 0, :], wide[0][:], ACT.Relu)
-                nc.vector.tensor_scalar_max(relu_wide[:, 1, :], wide[1][:], 0.0)
-                nc.vector.tensor_scalar_max(relu_rest[:], rest[:].rearrange("p b t -> p t b"), 0.0)
-            else:
-                for b in range(2):
-                    nc.scalar.activation(relu_wide[:, b, :], wide[b][:], ACT.Relu)
-                nc.scalar.activation(relu_rest[:], rest[:].rearrange("p b t -> p t b"), ACT.Relu)
-            nc.scalar.activation(
-                h_pairs[u][:, : 2 * WIDE].rearrange("p (t b) -> p t b", b=2),
-                relu_wide[:].rearrange("p b t -> p t b"),
-                ACT.Square,
-            )
-            nc.scalar.activation(h_pairs[u][:, 2 * WIDE :], relu_rest[:].rearrange("p t b -> p (t b)"), ACT.Square)
+            offs_sb = keep.tile([P, SLOTS // PER_COLUMN], U16)
+            nc.sync.dma_start(offs_sb[:], offs)
+            w2_raw = [keep.tile([P, 2, PACK * N], F32, name=f"w2_raw{g}") for g in range(PAIRS)]
+            for g in range(PAIRS):
+                nc.sync.dma_start(out=w2_raw[g][:], in_=w2[2 * g : 2 * g + 2].rearrange("e (p j) n -> p e (j n)", j=PACK))
+            pos1_sb = keep.tile([P, T // PER_COLUMN], U16)
+            nc.sync.dma_start(pos1_sb[:], pos1)
+            pos2_sb = keep.tile([P, T // PER_COLUMN], U16)
+            nc.sync.dma_start(pos2_sb[:], pos2)
+            gate_sb = keep.tile([P, 2, T], F32)
+            nc.sync.dma_start(out=gate_sb[:], in_=gate.rearrange("r p t -> p r t"))
 
-        own_bf = [keep.tile([P, 8 * N], BF16, align_bytes=64, name=f"own_bf{g}") for g in range(2)]
-        late_bf = keep.tile([P, E // 2 - 2, 8 * N], BF16, align_bytes=64, tag="relu_rest1")
-        w2_bf = [own_bf[0][:]] + [late_bf[:, g, :] for g in range(E // 2 - 2)] + [own_bf[1][:]]
-        first_codes = keep.tile([P, 2 * N], U32, align_bytes=64)
-        late_codes = keep.tile([P, E // 2 - 1, 2 * N], U32, align_bytes=64, tag="relu_rest0")
-        w2_codes = [first_codes[:]] + [late_codes[:, g, :] for g in range(E // 2 - 1)]
-        w2_scales = [keep.tile([P, 2 * N], U8, align_bytes=64, name=f"w2_scales{g}") for g in range(E // 2)]
-
-        def cast_w2(g):
-            src = w2_raw[g][:].rearrange("p e (j c i) -> p e c j i", j=4, i=4)
-            dst = w2_bf[g].rearrange("p (e c i j) -> p e c j i", e=2, i=4, j=4)
-            if g in (0, E // 2 - 1):
-                nc.vector.tensor_copy(out=dst, in_=src)
-            else:
-                nc.scalar.copy(out=dst, in_=src)
-
-        def quantize_w2(g):
-            nc.vector.quantize_mx(out=w2_codes[g].bitcast(FP8X4), scales=w2_scales[g][:], in_=w2_bf[g])
-
-        firsts = [sum(SLOT_CHUNKS[:c]) for c in range(len(SLOT_CHUNKS))]
-        gathered = [keep.tile([P, 2, n * C], U32, name=f"gathered{c}") for c, n in enumerate(SLOT_CHUNKS)]
-
-        def gather_h(c, u):
-            cols = slice(firsts[c] * C // 16, (firsts[c] + SLOT_CHUNKS[c]) * C // 16)
-            nc.vector.tensor_copy(out=gathered[c][:, u, :], in_=h_pairs[u][:].bitcast(U32).indirect(offs_sb[:, cols]))
-
-        for c in range(len(SLOT_CHUNKS)):
-            gather_h(c, 0)
-        for g in range(E // 2):
-            cast_w2(g)
-            quantize_w2(g)
-
-        y = keep.tile([P, S], F32)
-        for c, n in enumerate(SLOT_CHUNKS):
-            gather_h(c, 1)
-            woven = keep.tile([P, n * C * 4], BF16, align_bytes=64, name=f"woven{c}")
-            nc.scalar.copy(
-                out=woven[:].bitcast(U32).rearrange("p (s u) -> p s u", u=2),
-                in_=gathered[c][:].rearrange("p u s -> p s u"),
-            )
-            h_codes = keep.tile([P, n * C], U32, align_bytes=64, name=f"h_codes{c}")
-            h_scales = keep.tile([P, n * C], U8, align_bytes=64, name=f"h_scales{c}")
-            nc.vector.quantize_mx(out=h_codes[:].bitcast(FP8X4), scales=h_scales[:], in_=woven[:])
-            acc = ypsum.tile([P, WIDE], F32, name="acc")
-            for m in range(n):
-                e = firsts[c] + m
-                w_cols = slice((e % 2) * N, (e % 2 + 1) * N)
-                cols = slice(m * C, (m + 1) * C)
+            zeros = keep.tile([P, PACK * P], BF16, align_bytes=64)
+            zero_codes = keep.tile([P, P], U32, align_bytes=64)
+            zero_bytes = keep.tile([P, P], U8, align_bytes=64)
+            nc.vector.memset(zeros[:].bitcast(I32), 0)
+            nc.vector.quantize_mx(out=zero_codes[:].bitcast(FP8X4), scales=zero_bytes[:], in_=zeros[:])
+            idle = psum.tile([P, WIDE], F32)
+            for w in range(WARM_PASSES):
+                place = w % (WIDE // P) * P
                 nc.tensor.matmul_mx(
-                    out=acc[:, cols],
-                    lhsT=w2_codes[e // 2][:, w_cols].bitcast(FP8X4),
-                    lhsT_scale=w2_scales[e // 2][:, w_cols],
-                    rhs=h_codes[:, cols].bitcast(FP8X4),
-                    rhs_scale=h_scales[:, cols],
+                    out=idle[:, place : place + P],
+                    lhsT=w1_raw[:, 0, : 2 * P].bitcast(FP4X4),
+                    lhsT_scale=w1_plane[:, 0, :P],
+                    rhs=zero_codes[:].bitcast(FP8X4),
+                    rhs_scale=zero_bytes[:],
                     start=True,
                     stop=True,
                 )
-            if c < len(SLOT_CHUNKS) - 1:
-                nc.scalar.copy(out=y[:, firsts[c] * C : (firsts[c] + n) * C], in_=acc[:, : n * C])
-            else:
-                nc.vector.tensor_copy(out=y[:, firsts[c] * C : (firsts[c] + n) * C], in_=acc[:, : n * C])
 
+            def first_layer(acc, u, b, s, t0, t1):
+                words = x_wide[s][:] if t0 == 0 else x_rest[:, s, PACK * (t0 - WIDE) : PACK * (t1 - WIDE)]
+                nc.tensor.matmul_mx(
+                    out=acc,
+                    lhsT=w1_codes[u][s][:, 2 * P * b : 2 * P * (b + 1)].bitcast(FP4X4),
+                    lhsT_scale=w1_bytes[u][s][:, P * b : P * (b + 1)],
+                    rhs=words.bitcast(FP8X4),
+                    rhs_scale=x_plane[:, s, t0:t1],
+                    start=(s == 0),
+                    stop=(s == PASSES - 1),
+                )
+
+            h_pairs = [keep.tile([P, 2 * T], BF16, align_bytes=64, name=f"h_pairs{u}") for u in range(2)]
+            for u in range(2):
+                wide = [psum.tile([P, WIDE], F32, name=f"wide{b}") for b in range(2)]
+                rest = psum.tile([P, 2, T - WIDE], F32, name="rest")
+                for s in range(PASSES):
+                    for b in range(2):
+                        first_layer(wide[b][:], u, b, s, 0, WIDE)
+                for b in range(2):
+                    for t0 in range(WIDE, T, P):
+                        for s in range(PASSES):
+                            first_layer(rest[:, b, t0 - WIDE : t0 - WIDE + P], u, b, s, t0, t0 + P)
+                relu_wide = keep.tile([P, 2, WIDE], F32, name=f"relu_wide{u}", tag=f"relu_wide{u}", align_bytes=64)
+                relu_rest = keep.tile([P, T - WIDE, 2], F32, name=f"relu_rest{u}", tag=f"relu_rest{u}", align_bytes=64)
+                nc.scalar.activation(relu_wide[:, 0, :], wide[0][:], ACT.Relu)
+                if u == 0:
+                    nc.vector.tensor_scalar_max(relu_wide[:, 1, :], wide[1][:], 0.0)
+                    nc.vector.tensor_scalar_max(relu_rest[:], rest[:].rearrange("p b t -> p t b"), 0.0)
+                else:
+                    nc.scalar.activation(relu_wide[:, 1, :], wide[1][:], ACT.Relu)
+                    nc.scalar.activation(relu_rest[:], rest[:].rearrange("p b t -> p t b"), ACT.Relu)
+                nc.scalar.activation(
+                    h_pairs[u][:, : 2 * WIDE].rearrange("p (t b) -> p t b", b=2),
+                    relu_wide[:].rearrange("p b t -> p t b"),
+                    ACT.Square,
+                )
+                nc.scalar.activation(h_pairs[u][:, 2 * WIDE :], relu_rest[:].rearrange("p t b -> p (t b)"), ACT.Square)
+
+            scalar_pairs = [g for g in range(PAIRS) if g not in VECTOR_PAIRS]
+            vector_bf = [keep.tile([P, 2 * N * PACK], BF16, align_bytes=64, name=f"vector_bf{g}") for g in VECTOR_PAIRS]
+            scalar_bf = keep.tile([P, len(scalar_pairs), 2 * N * PACK], BF16, align_bytes=64, tag="relu_rest1")
+            first_codes = keep.tile([P, 2 * N], U32, align_bytes=64)
+            later_codes = keep.tile([P, PAIRS - 1, 2 * N], U32, align_bytes=64, tag="relu_rest0")
+            w2_codes = [first_codes[:]] + [later_codes[:, g, :] for g in range(PAIRS - 1)]
+            w2_bytes = [keep.tile([P, 2 * N], U8, align_bytes=64, name=f"w2_bytes{g}") for g in range(PAIRS)]
+
+            first_expert = [sum(SLOT_CHUNKS[:c]) for c in range(len(SLOT_CHUNKS))]
+            gathered = [keep.tile([P, 2, n * C], U32, name=f"gathered{c}") for c, n in enumerate(SLOT_CHUNKS)]
+
+            def gather_h(c, u):
+                entries = slice(first_expert[c] * C // PER_COLUMN, (first_expert[c] + SLOT_CHUNKS[c]) * C // PER_COLUMN)
+                nc.vector.tensor_copy(out=gathered[c][:, u, :], in_=h_pairs[u][:].bitcast(U32).indirect(offs_sb[:, entries]))
+
+            for c in range(len(SLOT_CHUNKS)):
+                gather_h(c, 0)
+            for g in range(PAIRS):
+                src = w2_raw[g][:].rearrange("p e (j c i) -> p e c j i", j=PACK, i=4)
+                rounded = vector_bf[VECTOR_PAIRS.index(g)][:] if g in VECTOR_PAIRS else scalar_bf[:, scalar_pairs.index(g), :]
+                dst = rounded.rearrange("p (e c i j) -> p e c j i", e=2, i=4, j=PACK)
+                if g in VECTOR_PAIRS:
+                    nc.vector.tensor_copy(out=dst, in_=src)
+                else:
+                    nc.scalar.copy(out=dst, in_=src)
+                nc.vector.quantize_mx(out=w2_codes[g].bitcast(FP8X4), scales=w2_bytes[g][:], in_=rounded)
+
+            identity = keep.tile([P, P], F32)
+            make_identity(nc, identity[:])
+            turned_blocks = sum(TURNED_CHUNKS) // P
+            gate_cols = keep.tile([P, 2, turned_blocks], F32)
+            for r in range(2):
+                gate_turned = psum.tile([P, turned_blocks, P], F32, name=f"wide{r}")
+                for k in range(turned_blocks):
+                    nc.tensor.transpose(gate_turned[:, k, :], gate_sb[:, r, k * P : (k + 1) * P], identity[:])
+                nc.scalar.copy(out=gate_cols[:, r, :], in_=gate_turned[:, :, 0])
+
+            y = keep.tile([P, SLOTS], F32)
+            for c, n in enumerate(SLOT_CHUNKS):
+                gather_h(c, 1)
+                slot_h = keep.tile([P, n * C * PACK], BF16, align_bytes=64, name=f"slot_h{c}")
+                nc.scalar.copy(
+                    out=slot_h[:].bitcast(U32).rearrange("p (s u) -> p s u", u=2),
+                    in_=gathered[c][:].rearrange("p u s -> p s u"),
+                )
+                h_codes = keep.tile([P, n * C], U32, align_bytes=64, name=f"h_codes{c}")
+                h_bytes = keep.tile([P, n * C], U8, align_bytes=64, name=f"h_bytes{c}")
+                nc.vector.quantize_mx(out=h_codes[:].bitcast(FP8X4), scales=h_bytes[:], in_=slot_h[:])
+                y_acc = y_psum.tile([P, WIDE], F32, name="y_acc")
+                for m in range(n):
+                    e = first_expert[c] + m
+                    w_cols = slice((e % 2) * N, (e % 2 + 1) * N)
+                    slots = slice(m * C, (m + 1) * C)
+                    nc.tensor.matmul_mx(
+                        out=y_acc[:, slots],
+                        lhsT=w2_codes[e // 2][:, w_cols].bitcast(FP8X4),
+                        lhsT_scale=w2_bytes[e // 2][:, w_cols],
+                        rhs=h_codes[:, slots].bitcast(FP8X4),
+                        rhs_scale=h_bytes[:, slots],
+                        start=True,
+                        stop=True,
+                    )
+                y_cols = slice(first_expert[c] * C, (first_expert[c] + n) * C)
+                if c < len(SLOT_CHUNKS) - 1:
+                    nc.scalar.copy(out=y[:, y_cols], in_=y_acc[:, : n * C])
+                else:
+                    nc.vector.tensor_copy(out=y[:, y_cols], in_=y_acc[:, : n * C])
+
+        banks = ctx.enter_context(tc.psum_pool(name="banks", bufs=8))
+        pos_sb = (pos1_sb, pos2_sb)
         t0 = 0
-        for c, n in enumerate(TOKEN_CHUNKS):
-            cols = slice(t0 // 16, (t0 + n) // 16)
-            first = keep.tile([P, n], F32, name=f"first{c}")
-            second = keep.tile([P, n], F32, name=f"second{c}")
+        for c, n in enumerate(TURNED_CHUNKS):
+            picked = keep.tile([P, 2, n], F32, name=f"picked{c}")
+            weighted = keep.tile([P, 2, n], F32, name=f"weighted{c}")
+            for r in range(2):
+                entries = slice(t0 // PER_COLUMN, (t0 + n) // PER_COLUMN)
+                nc.vector.tensor_copy(out=picked[:, r, :], in_=y[:].indirect(pos_sb[r][:, entries]))
+                for k in range(n // P):
+                    cols = slice(k * P, (k + 1) * P)
+                    block = t0 // P + k
+                    turned = banks.tile([P, P], F32, name="bank")
+                    nc.tensor.transpose(turned[:], picked[:, r, cols], identity[:])
+                    nc.scalar.activation(weighted[:, r, cols], turned[:], ACT.Copy, scale=gate_cols[:, r, block : block + 1])
             total = keep.tile([P, n], F32, name=f"total{c}")
-            nc.vector.tensor_tensor(first[:], y[:].indirect(pos1_sb[:, cols]), gate_sb[:, 0, t0 : t0 + n], ALU.mult)
-            nc.vector.tensor_tensor(second[:], y[:].indirect(pos2_sb[:, cols]), gate_sb[:, 1, t0 : t0 + n], ALU.mult)
-            nc.vector.tensor_tensor(total[:], first[:], second[:], ALU.add)
+            for k in range(n // P):
+                cols = slice(k * P, (k + 1) * P)
+                summed = banks.tile([P, P], F32, name="bank")
+                for r in range(2):
+                    nc.tensor.matmul(
+                        summed[:], lhsT=weighted[:, r, cols], rhs=identity[:], start=(r == 0), stop=(r == 1), is_transpose=True
+                    )
+                nc.scalar.copy(out=total[:, cols], in_=summed[:])
             nc.sync.dma_start(out=out[:, t0 : t0 + n], in_=total[:])
             t0 = t0 + n
+
+        first_term = keep.tile([P, T - t0], F32)
+        second_term = keep.tile([P, T - t0], F32)
+        last_total = keep.tile([P, T - t0], F32)
+        nc.vector.tensor_tensor(first_term[:], y[:].indirect(pos1_sb[:, t0 // PER_COLUMN :]), gate_sb[:, 0, t0:], ALU.mult)
+        nc.vector.tensor_tensor(second_term[:], y[:].indirect(pos2_sb[:, t0 // PER_COLUMN :]), gate_sb[:, 1, t0:], ALU.mult)
+        nc.vector.tensor_tensor(last_total[:], first_term[:], second_term[:], ALU.add)
+        nc.sync.dma_start(out=out[:, t0:], in_=last_total[:])

@@ -25,9 +25,10 @@ ACT = mybir.ActivationFunctionType
 
 WIDE = 512
 SLOT_CHUNKS = (4, 4, 2, 2)
-VECTOR_PAIRS = (0, PAIRS - 1)
-TURNED_CHUNKS = (256, 256)
-WARM_PASSES = 8
+VECTOR_PAIRS = ()
+GPSIMD_PAIRS = (0, 1, 2, 3)
+TURNED_CHUNKS = (256, 128)
+WARM_PASSES = 2
 
 
 def tile_moe_sup_lin_relu2_kernel(tc, x_words, x_scales, w1_words, w1_scales, w2, gate, offs, pos1, pos2, out):
@@ -56,39 +57,37 @@ def tile_moe_sup_lin_relu2_kernel(tc, x_words, x_scales, w1_words, w1_scales, w2
                     in_=w1_scale_rows[q].bitcast(I32),
                 )
             nc.scalar.dma_start(out=w1_raw[:].bitcast(I32), in_=w1_words.rearrange("s p b -> p s b").bitcast(I32))
-            x_rows = x_words.rearrange("s p t d -> s p (t d)")
+            x_rows = x_words.rearrange("s p t d -> p s (t d)")
             x_scale_rows = x_scales.rearrange("s (q r) t -> r q s t", r=4)
-            nc.scalar.dma_start(out=x_wide[0][:].bitcast(I32), in_=x_rows[0, :, : PACK * WIDE].bitcast(I32))
+            nc.scalar.dma_start(out=x_wide[0][:].bitcast(I32), in_=x_rows[:, 0, : PACK * WIDE].bitcast(I32))
             nc.scalar.activation(table_out[:], table_in[:], ACT.Square)
             for r in range(4):
                 nc.sync.dma_start(out=x_plane[r:P:32, :, :].bitcast(I32), in_=x_scale_rows[r].bitcast(I32))
             for s in range(1, PASSES):
-                nc.sync.dma_start(out=x_wide[s][:].bitcast(I32), in_=x_rows[s, :, : PACK * WIDE].bitcast(I32))
-            nc.sync.dma_start(
-                out=x_rest[:].bitcast(I32), in_=x_rows[:, :, PACK * WIDE :].rearrange("s p b -> p s b").bitcast(I32)
-            )
+                nc.sync.dma_start(out=x_wide[s][:].bitcast(I32), in_=x_rows[:, s, : PACK * WIDE].bitcast(I32))
+            nc.sync.dma_start(out=x_rest[:].bitcast(I32), in_=x_rows[:, :, PACK * WIDE :].bitcast(I32))
             for q in range(4):
                 rows = slice(32 * q, 32 * q + 4)
                 nc.vector.tensor_copy(out=w1_plane[rows].rearrange("p s i -> p (s i)").bitcast(I32), in_=w1_rows[rows, :])
 
-            w1_codes = [[keep.tile([P, H], U8, align_bytes=64, name=f"w1_codes{u}{s}") for s in range(PASSES)] for u in range(2)]
-            w1_bytes = [[keep.tile([P, H // 2], U8, align_bytes=64, name=f"w1_bytes{u}{s}") for s in range(PASSES)] for u in range(2)]
+            w1_codes = [keep.tile([P, PASSES, H], U8, align_bytes=64, name=f"w1_codes{u}") for u in range(2)]
+            w1_bytes = [keep.tile([P, PASSES, H // 2], U8, align_bytes=64, name=f"w1_bytes{u}") for u in range(2)]
             for u in range(2):
-                for s in range(PASSES):
-                    nc.vector.tensor_copy(
-                        out=w1_codes[u][s][:].bitcast(U16).rearrange("p (b m) -> p b m", b=2),
-                        in_=w1_raw[:, s, :].bitcast(U16).rearrange("p (m j) -> p j m", j=PACK)[:, 2 * u : 2 * u + 2, :],
-                    )
-                    nc.vector.tensor_copy(
-                        out=w1_bytes[u][s][:].rearrange("p (b m) -> p b m", b=2),
-                        in_=w1_plane[:, s, :].rearrange("p (m j) -> p j m", j=PACK)[:, 2 * u : 2 * u + 2, :],
-                    )
+                nc.vector.tensor_copy(
+                    out=w1_bytes[u][:].rearrange("p s (b m) -> p b s m", b=2),
+                    in_=w1_plane[:].rearrange("p s (m j) -> p j s m", j=PACK)[:, 2 * u : 2 * u + 2, :, :],
+                )
+                nc.vector.tensor_copy(
+                    out=w1_codes[u][:].bitcast(U16).rearrange("p s (b m) -> p b s m", b=2),
+                    in_=w1_raw[:].bitcast(U16).rearrange("p s (m j) -> p j s m", j=PACK)[:, 2 * u : 2 * u + 2, :, :],
+                )
 
             offs_sb = keep.tile([P, SLOTS // PER_COLUMN], U16)
-            nc.sync.dma_start(offs_sb[:], offs)
             w2_raw = [keep.tile([P, 2, PACK * N], F32, name=f"w2_raw{g}") for g in range(PAIRS)]
             for g in range(PAIRS):
                 nc.sync.dma_start(out=w2_raw[g][:], in_=w2[2 * g : 2 * g + 2].rearrange("e (p j) n -> p e (j n)", j=PACK))
+                if g == 0:
+                    nc.sync.dma_start(offs_sb[:], offs)
             pos1_sb = keep.tile([P, T // PER_COLUMN], U16)
             nc.sync.dma_start(pos1_sb[:], pos1)
             pos2_sb = keep.tile([P, T // PER_COLUMN], U16)
@@ -96,70 +95,83 @@ def tile_moe_sup_lin_relu2_kernel(tc, x_words, x_scales, w1_words, w1_scales, w2
             gate_sb = keep.tile([P, 2, T], F32)
             nc.sync.dma_start(out=gate_sb[:], in_=gate.rearrange("r p t -> p r t"))
 
-            zeros = keep.tile([P, PACK * P], BF16, align_bytes=64)
-            zero_codes = keep.tile([P, P], U32, align_bytes=64)
-            zero_bytes = keep.tile([P, P], U8, align_bytes=64)
-            nc.vector.memset(zeros[:].bitcast(I32), 0)
+            zeros = keep.tile([P, PACK * WIDE], BF16, align_bytes=64)
+            zero_codes = keep.tile([P, WIDE], U32, align_bytes=64)
+            zero_bytes = keep.tile([P, WIDE], U8, align_bytes=64)
+            nc.gpsimd.memset(zeros[:].bitcast(I32), 0)
             nc.vector.quantize_mx(out=zero_codes[:].bitcast(FP8X4), scales=zero_bytes[:], in_=zeros[:])
             idle = psum.tile([P, WIDE], F32)
             for w in range(WARM_PASSES):
-                place = w % (WIDE // P) * P
                 nc.tensor.matmul_mx(
-                    out=idle[:, place : place + P],
-                    lhsT=w1_raw[:, 0, : 2 * P].bitcast(FP4X4),
-                    lhsT_scale=w1_plane[:, 0, :P],
+                    out=idle[:],
+                    lhsT=zero_codes[:, :P].bitcast(FP8X4),
+                    lhsT_scale=zero_bytes[:, :P],
                     rhs=zero_codes[:].bitcast(FP8X4),
                     rhs_scale=zero_bytes[:],
                     start=True,
                     stop=True,
                 )
 
-            def first_layer(acc, u, b, s, t0, t1):
-                words = x_wide[s][:] if t0 == 0 else x_rest[:, s, PACK * (t0 - WIDE) : PACK * (t1 - WIDE)]
-                nc.tensor.matmul_mx(
-                    out=acc,
-                    lhsT=w1_codes[u][s][:, 2 * P * b : 2 * P * (b + 1)].bitcast(FP4X4),
-                    lhsT_scale=w1_bytes[u][s][:, P * b : P * (b + 1)],
-                    rhs=words.bitcast(FP8X4),
-                    rhs_scale=x_plane[:, s, t0:t1],
-                    start=(s == 0),
-                    stop=(s == PASSES - 1),
-                )
+            def first_layer(acc, u, b, t0, t1, passes=range(PASSES)):
+                for s in passes:
+                    words = x_wide[s][:] if t0 == 0 else x_rest[:, s, PACK * (t0 - WIDE) : PACK * (t1 - WIDE)]
+                    nc.tensor.matmul_mx(
+                        out=acc,
+                        lhsT=w1_codes[u][:, s, 2 * P * b : 2 * P * (b + 1)].bitcast(FP4X4),
+                        lhsT_scale=w1_bytes[u][:, s, P * b : P * (b + 1)],
+                        rhs=words.bitcast(FP8X4),
+                        rhs_scale=x_plane[:, s, t0:t1],
+                        start=(s == 0),
+                        stop=(s == PASSES - 1),
+                    )
 
             h_pairs = [keep.tile([P, 2 * T], BF16, align_bytes=64, name=f"h_pairs{u}") for u in range(2)]
             for u in range(2):
+                relu_wide = keep.tile([P, 2, WIDE], F32, name=f"relu_wide{u}", align_bytes=64)
                 wide = [psum.tile([P, WIDE], F32, name=f"wide{b}") for b in range(2)]
-                rest = psum.tile([P, 2, T - WIDE], F32, name="rest")
-                for s in range(PASSES):
-                    for b in range(2):
-                        first_layer(wide[b][:], u, b, s, 0, WIDE)
-                for b in range(2):
-                    for t0 in range(WIDE, T, P):
-                        for s in range(PASSES):
-                            first_layer(rest[:, b, t0 - WIDE : t0 - WIDE + P], u, b, s, t0, t0 + P)
-                relu_wide = keep.tile([P, 2, WIDE], F32, name=f"relu_wide{u}", tag=f"relu_wide{u}", align_bytes=64)
-                relu_rest = keep.tile([P, T - WIDE, 2], F32, name=f"relu_rest{u}", tag=f"relu_rest{u}", align_bytes=64)
-                nc.scalar.activation(relu_wide[:, 0, :], wide[0][:], ACT.Relu)
                 if u == 0:
+                    for s in range(PASSES):
+                        for b in range(2):
+                            first_layer(wide[b][:], u, b, 0, WIDE, [s])
+                    nc.scalar.activation(relu_wide[:, 0, :], wide[0][:], ACT.Relu)
                     nc.vector.tensor_scalar_max(relu_wide[:, 1, :], wide[1][:], 0.0)
-                    nc.vector.tensor_scalar_max(relu_rest[:], rest[:].rearrange("p b t -> p t b"), 0.0)
                 else:
-                    nc.scalar.activation(relu_wide[:, 1, :], wide[1][:], ACT.Relu)
-                    nc.scalar.activation(relu_rest[:], rest[:].rearrange("p b t -> p t b"), ACT.Relu)
+                    for b in range(2):
+                        first_layer(wide[b][:], u, b, 0, WIDE)
+                        nc.scalar.activation(relu_wide[:, b, :], wide[b][:], ACT.Relu)
                 nc.scalar.activation(
                     h_pairs[u][:, : 2 * WIDE].rearrange("p (t b) -> p t b", b=2),
                     relu_wide[:].rearrange("p b t -> p t b"),
                     ACT.Square,
                 )
-                nc.scalar.activation(h_pairs[u][:, 2 * WIDE :], relu_rest[:].rearrange("p t b -> p (t b)"), ACT.Square)
+                rest = psum.tile([P, 2, T - WIDE], F32, name="rest")
+                for b in range(2):
+                    for t0 in range(WIDE, T, P):
+                        first_layer(rest[:, b, t0 - WIDE : t0 - WIDE + P], u, b, t0, t0 + P)
+                relu_rest = keep.tile([P, 2 * (T - WIDE)], F32, name=f"relu_rest{u}", tag=f"relu_rest{u}", align_bytes=64)
+                by_token = relu_rest[:].rearrange("p (t b) -> p t b", b=2)
+                if u == 0:
+                    nc.vector.tensor_scalar_max(by_token, rest[:].rearrange("p b t -> p t b"), 0.0)
+                    nc.scalar.activation(h_pairs[u][:, 2 * WIDE :], relu_rest[:], ACT.Square)
+                else:
+                    nc.scalar.activation(by_token, rest[:].rearrange("p b t -> p t b"), ACT.Relu)
+                    nc.scalar.activation(h_pairs[u][:, 2 * WIDE :], relu_rest[:], ACT.Square)
 
-            scalar_pairs = [g for g in range(PAIRS) if g not in VECTOR_PAIRS]
-            vector_bf = [keep.tile([P, 2 * N * PACK], BF16, align_bytes=64, name=f"vector_bf{g}") for g in VECTOR_PAIRS]
+            scalar_pairs = [g for g in range(PAIRS) if g not in VECTOR_PAIRS + GPSIMD_PAIRS]
             scalar_bf = keep.tile([P, len(scalar_pairs), 2 * N * PACK], BF16, align_bytes=64, tag="relu_rest1")
-            first_codes = keep.tile([P, 2 * N], U32, align_bytes=64)
-            later_codes = keep.tile([P, PAIRS - 1, 2 * N], U32, align_bytes=64, tag="relu_rest0")
-            w2_codes = [first_codes[:]] + [later_codes[:, g, :] for g in range(PAIRS - 1)]
-            w2_bytes = [keep.tile([P, 2 * N], U8, align_bytes=64, name=f"w2_bytes{g}") for g in range(PAIRS)]
+            side_bf = keep.tile([P, len(GPSIMD_PAIRS) * 2 * N * PACK], BF16, align_bytes=64)
+            side_codes = keep.tile([P, len(GPSIMD_PAIRS) * 2 * N], U32, align_bytes=64)
+            side_bytes = keep.tile([P, len(GPSIMD_PAIRS) * 2 * N], U8, align_bytes=64)
+            rounded = [
+                scalar_bf[:, scalar_pairs.index(g), :]
+                if g in scalar_pairs
+                else side_bf[:, GPSIMD_PAIRS.index(g) * 2 * N * PACK : (GPSIMD_PAIRS.index(g) + 1) * 2 * N * PACK]
+                if g in GPSIMD_PAIRS
+                else keep.tile([P, 2 * N * PACK], BF16, align_bytes=64, name=f"rounded{g}", tag=f"rounded{g}")[:]
+                for g in range(PAIRS)
+            ]
+            w2_codes = [keep.tile([P, 2 * N], U32, align_bytes=64, name=f"w2_codes{g}")[:] if g not in GPSIMD_PAIRS else side_codes[:, GPSIMD_PAIRS.index(g) * 2 * N : (GPSIMD_PAIRS.index(g) + 1) * 2 * N] for g in range(PAIRS)]
+            w2_bytes = [keep.tile([P, 2 * N], U8, align_bytes=64, name=f"w2_bytes{g}")[:] if g not in GPSIMD_PAIRS else side_bytes[:, GPSIMD_PAIRS.index(g) * 2 * N : (GPSIMD_PAIRS.index(g) + 1) * 2 * N] for g in range(PAIRS)]
 
             first_expert = [sum(SLOT_CHUNKS[:c]) for c in range(len(SLOT_CHUNKS))]
             gathered = [keep.tile([P, 2, n * C], U32, name=f"gathered{c}") for c, n in enumerate(SLOT_CHUNKS)]
@@ -168,39 +180,50 @@ def tile_moe_sup_lin_relu2_kernel(tc, x_words, x_scales, w1_words, w1_scales, w2
                 entries = slice(first_expert[c] * C // PER_COLUMN, (first_expert[c] + SLOT_CHUNKS[c]) * C // PER_COLUMN)
                 nc.vector.tensor_copy(out=gathered[c][:, u, :], in_=h_pairs[u][:].bitcast(U32).indirect(offs_sb[:, entries]))
 
+            def prepare_w2(g):
+                if g in GPSIMD_PAIRS:
+                    nc.gpsimd.tensor_scalar(
+                        rounded[g].rearrange("p (e n j) -> p e n j", e=2, j=PACK),
+                        w2_raw[g][:].rearrange("p e (j n) -> p e n j", j=PACK),
+                        1.0,
+                        0.0,
+                        ALU.mult,
+                        ALU.add,
+                    )
+                else:
+                    copy = nc.vector.tensor_copy if g in VECTOR_PAIRS else nc.scalar.copy
+                    copy(
+                        out=rounded[g].rearrange("p (e c i j) -> p e c j i", e=2, i=4, j=PACK),
+                        in_=w2_raw[g][:].rearrange("p e (j c i) -> p e c j i", j=PACK, i=4),
+                    )
+                if g not in GPSIMD_PAIRS:
+                    nc.vector.quantize_mx(out=w2_codes[g].bitcast(FP8X4), scales=w2_bytes[g], in_=rounded[g])
+                elif g == GPSIMD_PAIRS[-1]:
+                    nc.vector.quantize_mx(out=side_codes[:].bitcast(FP8X4), scales=side_bytes[:], in_=side_bf[:])
+
+            early = 0
+            for g in range(early):
+                prepare_w2(g)
             for c in range(len(SLOT_CHUNKS)):
                 gather_h(c, 0)
-            for g in range(PAIRS):
-                src = w2_raw[g][:].rearrange("p e (j c i) -> p e c j i", j=PACK, i=4)
-                rounded = vector_bf[VECTOR_PAIRS.index(g)][:] if g in VECTOR_PAIRS else scalar_bf[:, scalar_pairs.index(g), :]
-                dst = rounded.rearrange("p (e c i j) -> p e c j i", e=2, i=4, j=PACK)
-                if g in VECTOR_PAIRS:
-                    nc.vector.tensor_copy(out=dst, in_=src)
-                else:
-                    nc.scalar.copy(out=dst, in_=src)
-                nc.vector.quantize_mx(out=w2_codes[g].bitcast(FP8X4), scales=w2_bytes[g][:], in_=rounded)
+            for g in range(early, PAIRS):
+                prepare_w2(g)
 
             identity = keep.tile([P, P], F32)
             make_identity(nc, identity[:])
-            turned_blocks = sum(TURNED_CHUNKS) // P
-            gate_cols = keep.tile([P, 2, turned_blocks], F32)
-            for r in range(2):
-                gate_turned = psum.tile([P, turned_blocks, P], F32, name=f"wide{r}")
-                for k in range(turned_blocks):
-                    nc.tensor.transpose(gate_turned[:, k, :], gate_sb[:, r, k * P : (k + 1) * P], identity[:])
-                nc.scalar.copy(out=gate_cols[:, r, :], in_=gate_turned[:, :, 0])
 
-            y = keep.tile([P, SLOTS], F32)
-            for c, n in enumerate(SLOT_CHUNKS):
+            slot_h = [keep.tile([P, n * C * PACK], BF16, align_bytes=64, name=f"slot_h{c}") for c, n in enumerate(SLOT_CHUNKS)]
+            for c in range(len(SLOT_CHUNKS)):
                 gather_h(c, 1)
-                slot_h = keep.tile([P, n * C * PACK], BF16, align_bytes=64, name=f"slot_h{c}")
                 nc.scalar.copy(
-                    out=slot_h[:].bitcast(U32).rearrange("p (s u) -> p s u", u=2),
+                    out=slot_h[c][:].bitcast(U32).rearrange("p (s u) -> p s u", u=2),
                     in_=gathered[c][:].rearrange("p u s -> p s u"),
                 )
+            y = keep.tile([P, SLOTS], F32)
+            for c, n in enumerate(SLOT_CHUNKS):
                 h_codes = keep.tile([P, n * C], U32, align_bytes=64, name=f"h_codes{c}")
                 h_bytes = keep.tile([P, n * C], U8, align_bytes=64, name=f"h_bytes{c}")
-                nc.vector.quantize_mx(out=h_codes[:].bitcast(FP8X4), scales=h_bytes[:], in_=slot_h[:])
+                nc.vector.quantize_mx(out=h_codes[:].bitcast(FP8X4), scales=h_bytes[:], in_=slot_h[c][:])
                 y_acc = y_psum.tile([P, WIDE], F32, name="y_acc")
                 for m in range(n):
                     e = first_expert[c] + m
@@ -225,17 +248,11 @@ def tile_moe_sup_lin_relu2_kernel(tc, x_words, x_scales, w1_words, w1_scales, w2
         pos_sb = (pos1_sb, pos2_sb)
         t0 = 0
         for c, n in enumerate(TURNED_CHUNKS):
-            picked = keep.tile([P, 2, n], F32, name=f"picked{c}")
             weighted = keep.tile([P, 2, n], F32, name=f"weighted{c}")
             for r in range(2):
                 entries = slice(t0 // PER_COLUMN, (t0 + n) // PER_COLUMN)
-                nc.vector.tensor_copy(out=picked[:, r, :], in_=y[:].indirect(pos_sb[r][:, entries]))
-                for k in range(n // P):
-                    cols = slice(k * P, (k + 1) * P)
-                    block = t0 // P + k
-                    turned = banks.tile([P, P], F32, name="bank")
-                    nc.tensor.transpose(turned[:], picked[:, r, cols], identity[:])
-                    nc.scalar.activation(weighted[:, r, cols], turned[:], ACT.Copy, scale=gate_cols[:, r, block : block + 1])
+                nc.vector.tensor_tensor(weighted[:, r, :], y[:].indirect(pos_sb[r][:, entries]), gate_sb[:, r, t0 : t0 + n], ALU.mult)
+            turned = keep.tile([P, n], F32, name=f"turned{c}")
             total = keep.tile([P, n], F32, name=f"total{c}")
             for k in range(n // P):
                 cols = slice(k * P, (k + 1) * P)
@@ -244,7 +261,12 @@ def tile_moe_sup_lin_relu2_kernel(tc, x_words, x_scales, w1_words, w1_scales, w2
                     nc.tensor.matmul(
                         summed[:], lhsT=weighted[:, r, cols], rhs=identity[:], start=(r == 0), stop=(r == 1), is_transpose=True
                     )
-                nc.scalar.copy(out=total[:, cols], in_=summed[:])
+                nc.scalar.copy(out=turned[:, cols], in_=summed[:])
+            for k in range(n // P):
+                cols = slice(k * P, (k + 1) * P)
+                back = banks.tile([P, P], F32, name="bank")
+                nc.tensor.transpose(back[:], turned[:, cols], identity[:])
+                nc.scalar.copy(out=total[:, cols], in_=back[:])
             nc.sync.dma_start(out=out[:, t0 : t0 + n], in_=total[:])
             t0 = t0 + n
 

@@ -26,7 +26,7 @@ ACT = mybir.ActivationFunctionType
 WIDE = 512
 SLOT_CHUNKS = (4, 4, 2, 2)
 VECTOR_PAIRS = ()
-GPSIMD_PAIRS = (0, 1, 2, 3)
+GPSIMD_PAIRS = (0, 1, 2)
 TURNED_CHUNKS = (256, 128)
 WARM_PASSES = 2
 
@@ -36,7 +36,7 @@ def tile_moe_sup_lin_relu2_kernel(tc, x_words, x_scales, w1_words, w1_scales, w2
     with ExitStack() as ctx:
         keep = ctx.enter_context(tc.tile_pool(name="keep", bufs=1))
 
-        with tc.psum_pool(name="psum", bufs=1) as psum, tc.psum_pool(name="y_psum", bufs=len(SLOT_CHUNKS)) as y_psum:
+        with tc.psum_pool(name="psum", bufs=1) as psum, tc.psum_pool(name="y_psum", bufs=3) as y_psum:
             w1_raw = keep.tile([P, PASSES, 2 * H], U8, align_bytes=64)
             w1_plane = keep.tile([P, PASSES, H], U8, align_bytes=64)
             x_plane = keep.tile([P, PASSES, T], U8, align_bytes=64)
@@ -100,7 +100,7 @@ def tile_moe_sup_lin_relu2_kernel(tc, x_words, x_scales, w1_words, w1_scales, w2
             zero_bytes = keep.tile([P, WIDE], U8, align_bytes=64)
             nc.gpsimd.memset(zeros[:].bitcast(I32), 0)
             nc.vector.quantize_mx(out=zero_codes[:].bitcast(FP8X4), scales=zero_bytes[:], in_=zeros[:])
-            idle = psum.tile([P, WIDE], F32)
+            idle = psum.tile([P, WIDE], F32, tag="idle")
             for w in range(WARM_PASSES):
                 nc.tensor.matmul_mx(
                     out=idle[:],
@@ -125,42 +125,50 @@ def tile_moe_sup_lin_relu2_kernel(tc, x_words, x_scales, w1_words, w1_scales, w2
                         stop=(s == PASSES - 1),
                     )
 
-            h_pairs = [keep.tile([P, 2 * T], BF16, align_bytes=64, name=f"h_pairs{u}") for u in range(2)]
-            for u in range(2):
-                relu_wide = keep.tile([P, 2, WIDE], F32, name=f"relu_wide{u}", align_bytes=64)
-                wide = [psum.tile([P, WIDE], F32, name=f"wide{b}") for b in range(2)]
-                if u == 0:
-                    for s in range(PASSES):
-                        for b in range(2):
-                            first_layer(wide[b][:], u, b, 0, WIDE, [s])
-                    nc.scalar.activation(relu_wide[:, 0, :], wide[0][:], ACT.Relu)
-                    nc.vector.tensor_scalar_max(relu_wide[:, 1, :], wide[1][:], 0.0)
-                else:
-                    for b in range(2):
-                        first_layer(wide[b][:], u, b, 0, WIDE)
-                        nc.scalar.activation(relu_wide[:, b, :], wide[b][:], ACT.Relu)
+            h_pairs = [keep.tile([P, 2 * T], BF16, align_bytes=64, name=f"h_pairs{u}", tag=f"h_pairs{u}") for u in range(2)]
+            def rest_tokens(u, t0, t1, tag):
+                sums = psum.tile([P, 2, t1 - t0], F32, name=f"rest{u}_{t0}", tag=tag)
+                for b in range(2):
+                    for t in range(t0, t1, P):
+                        first_layer(sums[:, b, t - t0 : t - t0 + P], u, b, t, t + P)
+                relu = keep.tile([P, t1 - t0, 2], F32, name=f"relu_rest{u}_{t0}", align_bytes=64)
+                return sums[:].rearrange("p b t -> p t b"), relu[:], h_pairs[u][:, 2 * t0 : 2 * t1].rearrange("p (t b) -> p t b", b=2)
+
+            relu_wide = [keep.tile([P, 2, WIDE], F32, name=f"relu_wide{u}", tag=f"relu_wide{u}", align_bytes=64) for u in range(2)]
+
+            def square_wide(u):
                 nc.scalar.activation(
                     h_pairs[u][:, : 2 * WIDE].rearrange("p (t b) -> p t b", b=2),
-                    relu_wide[:].rearrange("p b t -> p t b"),
+                    relu_wide[u][:].rearrange("p b t -> p t b"),
                     ACT.Square,
                 )
-                rest = psum.tile([P, 2, T - WIDE], F32, name="rest")
+
+            wide = [psum.tile([P, WIDE], F32, name=f"wide{b}", tag=f"wide{b}") for b in range(2)]
+            for s in range(PASSES):
                 for b in range(2):
-                    for t0 in range(WIDE, T, P):
-                        first_layer(rest[:, b, t0 - WIDE : t0 - WIDE + P], u, b, t0, t0 + P)
-                relu_rest = keep.tile([P, 2 * (T - WIDE)], F32, name=f"relu_rest{u}", tag=f"relu_rest{u}", align_bytes=64)
-                by_token = relu_rest[:].rearrange("p (t b) -> p t b", b=2)
-                if u == 0:
-                    nc.vector.tensor_scalar_max(by_token, rest[:].rearrange("p b t -> p t b"), 0.0)
-                    nc.scalar.activation(h_pairs[u][:, 2 * WIDE :], relu_rest[:], ACT.Square)
-                else:
-                    nc.scalar.activation(by_token, rest[:].rearrange("p b t -> p t b"), ACT.Relu)
-                    nc.scalar.activation(h_pairs[u][:, 2 * WIDE :], relu_rest[:], ACT.Square)
+                    first_layer(wide[b][:], 0, b, 0, WIDE, [s])
+            nc.scalar.activation(relu_wide[0][:, 0, :], wide[0][:], ACT.Relu)
+            nc.vector.tensor_scalar_max(relu_wide[0][:, 1, :], wide[1][:], 0.0)
+            square_wide(0)
+            blocks = [rest_tokens(0, t0, t1, f"rest{t0}") for t0, t1 in ((WIDE, WIDE + P), (WIDE + P, T))]
+            for sums, relu, pairs in blocks:
+                nc.vector.tensor_scalar_max(relu, sums, 0.0)
+            for sums, relu, pairs in blocks:
+                nc.vector.tensor_tensor(pairs, sums, relu, ALU.mult)
+
+            sums, relu, pairs = rest_tokens(1, WIDE, T, "idle")
+            nc.scalar.activation(relu, sums, ACT.Relu)
+            nc.scalar.activation(pairs, relu, ACT.Square)
+            for b in range(2):
+                wide = psum.tile([P, WIDE], F32, name=f"wide{b}", tag=f"wide{b}")
+                first_layer(wide[:], 1, b, 0, WIDE)
+                nc.scalar.activation(relu_wide[1][:, b, :], wide[:], ACT.Relu)
+            square_wide(1)
 
             scalar_pairs = [g for g in range(PAIRS) if g not in VECTOR_PAIRS + GPSIMD_PAIRS]
-            scalar_bf = keep.tile([P, len(scalar_pairs), 2 * N * PACK], BF16, align_bytes=64, tag="relu_rest1")
+            scalar_bf = keep.tile([P, len(scalar_pairs), 2 * N * PACK], BF16, align_bytes=64, tag="relu_wide1")
             side_bf = keep.tile([P, len(GPSIMD_PAIRS) * 2 * N * PACK], BF16, align_bytes=64)
-            side_codes = keep.tile([P, len(GPSIMD_PAIRS) * 2 * N], U32, align_bytes=64)
+            side_codes = keep.tile([P, len(GPSIMD_PAIRS) * 2 * N], U32, align_bytes=64, tag="h_pairs1")
             side_bytes = keep.tile([P, len(GPSIMD_PAIRS) * 2 * N], U8, align_bytes=64)
             rounded = [
                 scalar_bf[:, scalar_pairs.index(g), :]
@@ -198,8 +206,7 @@ def tile_moe_sup_lin_relu2_kernel(tc, x_words, x_scales, w1_words, w1_scales, w2
                     )
                 if g not in GPSIMD_PAIRS:
                     nc.vector.quantize_mx(out=w2_codes[g].bitcast(FP8X4), scales=w2_bytes[g], in_=rounded[g])
-                elif g == GPSIMD_PAIRS[-1]:
-                    nc.vector.quantize_mx(out=side_codes[:].bitcast(FP8X4), scales=side_bytes[:], in_=side_bf[:])
+
 
             early = 0
             for g in range(early):
@@ -218,6 +225,12 @@ def tile_moe_sup_lin_relu2_kernel(tc, x_words, x_scales, w1_words, w1_scales, w2
                 nc.scalar.copy(
                     out=slot_h[c][:].bitcast(U32).rearrange("p (s u) -> p s u", u=2),
                     in_=gathered[c][:].rearrange("p u s -> p s u"),
+                )
+            for a, b in ((0, 2), (2, 3)):
+                nc.vector.quantize_mx(
+                    out=side_codes[:, a * 2 * N : b * 2 * N].bitcast(FP8X4),
+                    scales=side_bytes[:, a * 2 * N : b * 2 * N],
+                    in_=side_bf[:, a * 2 * N * PACK : b * 2 * N * PACK],
                 )
             y = keep.tile([P, SLOTS], F32)
             for c, n in enumerate(SLOT_CHUNKS):

@@ -25,9 +25,9 @@ ACT = mybir.ActivationFunctionType
 
 WIDE = 512
 SLOT_CHUNKS = (4, 4, 2, 2)
-VECTOR_PAIRS = ()
-GPSIMD_PAIRS = (0, 1, 2)
-TURNED_CHUNKS = (256, 128)
+GATHER = 512
+GPSIMD_PAIRS = 4
+TURNED_CHUNKS = (256,)
 WARM_PASSES = 2
 
 
@@ -40,12 +40,14 @@ def tile_moe_sup_lin_relu2_kernel(tc, x_words, x_scales, w1_words, w1_scales, w2
             w1_raw = keep.tile([P, PASSES, 2 * H], U8, align_bytes=64)
             w1_plane = keep.tile([P, PASSES, H], U8, align_bytes=64)
             x_plane = keep.tile([P, PASSES, T], U8, align_bytes=64)
-            x_wide = [keep.tile([P, PACK * WIDE], U8, align_bytes=64, name=f"x_wide{s}") for s in range(PASSES)]
-            x_rest = keep.tile([P, PASSES, PACK * (T - WIDE)], U8, align_bytes=64)
+            x_first = keep.tile([P, PACK * T], U8, align_bytes=64)
+            x_wide = [x_first[:, : PACK * WIDE]] + [keep.tile([P, PACK * WIDE], U8, align_bytes=64, name=f"x_wide{s}")[:] for s in range(1, PASSES)]
+            x_later = keep.tile([P, PASSES - 1, PACK * (T - WIDE)], U8, align_bytes=64)
+            x_rest = [x_first[:, PACK * WIDE :]] + [x_later[:, s, :] for s in range(PASSES - 1)]
             table_in = keep.tile([P, 8], F32)
             table_out = keep.tile([P, 8], F32)
             w1_rows = keep.tile([P, PASSES * H // 4], I32)
-            nc.vector.memset(x_plane[:].bitcast(I32), 0)
+            nc.gpsimd.memset(x_plane[:].bitcast(I32), 0)
             nc.vector.memset(table_in[:], 0.0)
             nc.vector.memset(w1_plane[:].bitcast(I32), 0)
 
@@ -59,13 +61,13 @@ def tile_moe_sup_lin_relu2_kernel(tc, x_words, x_scales, w1_words, w1_scales, w2
             nc.scalar.dma_start(out=w1_raw[:].bitcast(I32), in_=w1_words.rearrange("s p b -> p s b").bitcast(I32))
             x_rows = x_words.rearrange("s p t d -> p s (t d)")
             x_scale_rows = x_scales.rearrange("s (q r) t -> r q s t", r=4)
-            nc.scalar.dma_start(out=x_wide[0][:].bitcast(I32), in_=x_rows[:, 0, : PACK * WIDE].bitcast(I32))
+            nc.scalar.dma_start(out=x_first[:].bitcast(I32), in_=x_rows[:, 0, :].bitcast(I32))
             nc.scalar.activation(table_out[:], table_in[:], ACT.Square)
             for r in range(4):
                 nc.sync.dma_start(out=x_plane[r:P:32, :, :].bitcast(I32), in_=x_scale_rows[r].bitcast(I32))
             for s in range(1, PASSES):
-                nc.sync.dma_start(out=x_wide[s][:].bitcast(I32), in_=x_rows[:, s, : PACK * WIDE].bitcast(I32))
-            nc.sync.dma_start(out=x_rest[:].bitcast(I32), in_=x_rows[:, :, PACK * WIDE :].bitcast(I32))
+                nc.sync.dma_start(out=x_wide[s].bitcast(I32), in_=x_rows[:, s, : PACK * WIDE].bitcast(I32))
+            nc.sync.dma_start(out=x_later[:].bitcast(I32), in_=x_rows[:, 1:, PACK * WIDE :].bitcast(I32))
             for q in range(4):
                 rows = slice(32 * q, 32 * q + 4)
                 nc.vector.tensor_copy(out=w1_plane[rows].rearrange("p s i -> p (s i)").bitcast(I32), in_=w1_rows[rows, :])
@@ -95,26 +97,26 @@ def tile_moe_sup_lin_relu2_kernel(tc, x_words, x_scales, w1_words, w1_scales, w2
             gate_sb = keep.tile([P, 2, T], F32)
             nc.sync.dma_start(out=gate_sb[:], in_=gate.rearrange("r p t -> p r t"))
 
-            zeros = keep.tile([P, PACK * WIDE], BF16, align_bytes=64)
-            zero_codes = keep.tile([P, WIDE], U32, align_bytes=64)
-            zero_bytes = keep.tile([P, WIDE], U8, align_bytes=64)
-            nc.gpsimd.memset(zeros[:].bitcast(I32), 0)
+            zeros = keep.tile([P, PACK * P], BF16, align_bytes=64)
+            zero_codes = keep.tile([P, P], U32, align_bytes=64)
+            zero_bytes = keep.tile([P, P], U8, align_bytes=64)
+            nc.vector.memset(zeros[:].bitcast(I32), 0)
             nc.vector.quantize_mx(out=zero_codes[:].bitcast(FP8X4), scales=zero_bytes[:], in_=zeros[:])
             idle = psum.tile([P, WIDE], F32, tag="idle")
             for w in range(WARM_PASSES):
                 nc.tensor.matmul_mx(
                     out=idle[:],
-                    lhsT=zero_codes[:, :P].bitcast(FP8X4),
-                    lhsT_scale=zero_bytes[:, :P],
-                    rhs=zero_codes[:].bitcast(FP8X4),
-                    rhs_scale=zero_bytes[:],
+                    lhsT=zero_codes[:].bitcast(FP8X4),
+                    lhsT_scale=zero_bytes[:],
+                    rhs=w1_raw[:, 0, :].bitcast(FP4X4),
+                    rhs_scale=w1_plane[:, 0, :],
                     start=True,
                     stop=True,
                 )
 
             def first_layer(acc, u, b, t0, t1, passes=range(PASSES)):
                 for s in passes:
-                    words = x_wide[s][:] if t0 == 0 else x_rest[:, s, PACK * (t0 - WIDE) : PACK * (t1 - WIDE)]
+                    words = x_wide[s] if t0 == 0 else x_rest[s][:, PACK * (t0 - WIDE) : PACK * (t1 - WIDE)]
                     nc.tensor.matmul_mx(
                         out=acc,
                         lhsT=w1_codes[u][:, s, 2 * P * b : 2 * P * (b + 1)].bitcast(FP4X4),
@@ -165,33 +167,18 @@ def tile_moe_sup_lin_relu2_kernel(tc, x_words, x_scales, w1_words, w1_scales, w2
                 nc.scalar.activation(relu_wide[1][:, b, :], wide[:], ACT.Relu)
             square_wide(1)
 
-            scalar_pairs = [g for g in range(PAIRS) if g not in VECTOR_PAIRS + GPSIMD_PAIRS]
-            scalar_bf = keep.tile([P, len(scalar_pairs), 2 * N * PACK], BF16, align_bytes=64, tag="relu_wide1")
-            side_bf = keep.tile([P, len(GPSIMD_PAIRS) * 2 * N * PACK], BF16, align_bytes=64)
-            side_codes = keep.tile([P, len(GPSIMD_PAIRS) * 2 * N], U32, align_bytes=64, tag="h_pairs1")
-            side_bytes = keep.tile([P, len(GPSIMD_PAIRS) * 2 * N], U8, align_bytes=64)
-            rounded = [
-                scalar_bf[:, scalar_pairs.index(g), :]
-                if g in scalar_pairs
-                else side_bf[:, GPSIMD_PAIRS.index(g) * 2 * N * PACK : (GPSIMD_PAIRS.index(g) + 1) * 2 * N * PACK]
-                if g in GPSIMD_PAIRS
-                else keep.tile([P, 2 * N * PACK], BF16, align_bytes=64, name=f"rounded{g}", tag=f"rounded{g}")[:]
-                for g in range(PAIRS)
-            ]
-            w2_codes = [keep.tile([P, 2 * N], U32, align_bytes=64, name=f"w2_codes{g}")[:] if g not in GPSIMD_PAIRS else side_codes[:, GPSIMD_PAIRS.index(g) * 2 * N : (GPSIMD_PAIRS.index(g) + 1) * 2 * N] for g in range(PAIRS)]
-            w2_bytes = [keep.tile([P, 2 * N], U8, align_bytes=64, name=f"w2_bytes{g}")[:] if g not in GPSIMD_PAIRS else side_bytes[:, GPSIMD_PAIRS.index(g) * 2 * N : (GPSIMD_PAIRS.index(g) + 1) * 2 * N] for g in range(PAIRS)]
-
             first_expert = [sum(SLOT_CHUNKS[:c]) for c in range(len(SLOT_CHUNKS))]
-            gathered = [keep.tile([P, 2, n * C], U32, name=f"gathered{c}") for c, n in enumerate(SLOT_CHUNKS)]
+            late_bf = keep.tile([P, (PAIRS - GPSIMD_PAIRS) * 2 * N * PACK], BF16, align_bytes=64, tag="relu_wide1")
+            early_bf = keep.tile([P, GPSIMD_PAIRS * 2 * N * PACK], BF16, align_bytes=64)
 
-            def gather_h(c, u):
-                entries = slice(first_expert[c] * C // PER_COLUMN, (first_expert[c] + SLOT_CHUNKS[c]) * C // PER_COLUMN)
-                nc.vector.tensor_copy(out=gathered[c][:, u, :], in_=h_pairs[u][:].bitcast(U32).indirect(offs_sb[:, entries]))
+            def rounded(e0, e1):
+                tile, base = (early_bf, 0) if e0 < 2 * GPSIMD_PAIRS else (late_bf, 2 * GPSIMD_PAIRS)
+                return tile[:, (e0 - base) * N * PACK : (e1 - base) * N * PACK]
 
-            def prepare_w2(g):
-                if g in GPSIMD_PAIRS:
+            for g in range(PAIRS):
+                if g < GPSIMD_PAIRS:
                     nc.gpsimd.tensor_scalar(
-                        rounded[g].rearrange("p (e n j) -> p e n j", e=2, j=PACK),
+                        rounded(2 * g, 2 * g + 2).rearrange("p (e n j) -> p e n j", e=2, j=PACK),
                         w2_raw[g][:].rearrange("p e (j n) -> p e n j", j=PACK),
                         1.0,
                         0.0,
@@ -199,59 +186,54 @@ def tile_moe_sup_lin_relu2_kernel(tc, x_words, x_scales, w1_words, w1_scales, w2
                         ALU.add,
                     )
                 else:
-                    copy = nc.vector.tensor_copy if g in VECTOR_PAIRS else nc.scalar.copy
-                    copy(
-                        out=rounded[g].rearrange("p (e c i j) -> p e c j i", e=2, i=4, j=PACK),
+                    nc.scalar.copy(
+                        out=rounded(2 * g, 2 * g + 2).rearrange("p (e c i j) -> p e c j i", e=2, i=4, j=PACK),
                         in_=w2_raw[g][:].rearrange("p e (j c i) -> p e c j i", j=PACK, i=4),
                     )
-                if g not in GPSIMD_PAIRS:
-                    nc.vector.quantize_mx(out=w2_codes[g].bitcast(FP8X4), scales=w2_bytes[g], in_=rounded[g])
-
-
-            early = 0
-            for g in range(early):
-                prepare_w2(g)
-            for c in range(len(SLOT_CHUNKS)):
-                gather_h(c, 0)
-            for g in range(early, PAIRS):
-                prepare_w2(g)
 
             identity = keep.tile([P, P], F32)
             make_identity(nc, identity[:])
 
+            runs = SLOTS // GATHER
+            gathered = [keep.tile([P, 2, GATHER], U32, name=f"gathered{k}") for k in range(runs)]
+            for u in range(2):
+                for k in range(runs):
+                    entries = slice(k * GATHER // PER_COLUMN, (k + 1) * GATHER // PER_COLUMN)
+                    nc.vector.tensor_copy(out=gathered[k][:, u, :], in_=h_pairs[u][:].bitcast(U32).indirect(offs_sb[:, entries]))
             slot_h = [keep.tile([P, n * C * PACK], BF16, align_bytes=64, name=f"slot_h{c}") for c, n in enumerate(SLOT_CHUNKS)]
-            for c in range(len(SLOT_CHUNKS)):
-                gather_h(c, 1)
+            for c, n in enumerate(SLOT_CHUNKS):
+                k, s0 = divmod(first_expert[c] * C, GATHER)
                 nc.scalar.copy(
                     out=slot_h[c][:].bitcast(U32).rearrange("p (s u) -> p s u", u=2),
-                    in_=gathered[c][:].rearrange("p u s -> p s u"),
+                    in_=gathered[k][:, :, s0 : s0 + n * C].rearrange("p u s -> p s u"),
                 )
-            for a, b in ((0, 2), (2, 3)):
-                nc.vector.quantize_mx(
-                    out=side_codes[:, a * 2 * N : b * 2 * N].bitcast(FP8X4),
-                    scales=side_bytes[:, a * 2 * N : b * 2 * N],
-                    in_=side_bf[:, a * 2 * N * PACK : b * 2 * N * PACK],
-                )
+            w2_codes = keep.tile([P, E * N], U32, align_bytes=64, tag="h_pairs1")
+            w2_bytes = keep.tile([P, E * N], U8, align_bytes=64)
             y = keep.tile([P, SLOTS], F32)
             for c, n in enumerate(SLOT_CHUNKS):
+                e0 = first_expert[c]
+                nc.vector.quantize_mx(
+                    out=w2_codes[:, e0 * N : (e0 + n) * N].bitcast(FP8X4),
+                    scales=w2_bytes[:, e0 * N : (e0 + n) * N],
+                    in_=rounded(e0, e0 + n),
+                )
                 h_codes = keep.tile([P, n * C], U32, align_bytes=64, name=f"h_codes{c}")
                 h_bytes = keep.tile([P, n * C], U8, align_bytes=64, name=f"h_bytes{c}")
                 nc.vector.quantize_mx(out=h_codes[:].bitcast(FP8X4), scales=h_bytes[:], in_=slot_h[c][:])
                 y_acc = y_psum.tile([P, WIDE], F32, name="y_acc")
                 for m in range(n):
-                    e = first_expert[c] + m
-                    w_cols = slice((e % 2) * N, (e % 2 + 1) * N)
+                    w_cols = slice((e0 + m) * N, (e0 + m + 1) * N)
                     slots = slice(m * C, (m + 1) * C)
                     nc.tensor.matmul_mx(
                         out=y_acc[:, slots],
-                        lhsT=w2_codes[e // 2][:, w_cols].bitcast(FP8X4),
-                        lhsT_scale=w2_bytes[e // 2][:, w_cols],
+                        lhsT=w2_codes[:, w_cols].bitcast(FP8X4),
+                        lhsT_scale=w2_bytes[:, w_cols],
                         rhs=h_codes[:, slots].bitcast(FP8X4),
                         rhs_scale=h_bytes[:, slots],
                         start=True,
                         stop=True,
                     )
-                y_cols = slice(first_expert[c] * C, (first_expert[c] + n) * C)
+                y_cols = slice(e0 * C, (e0 + n) * C)
                 if c < len(SLOT_CHUNKS) - 1:
                     nc.scalar.copy(out=y[:, y_cols], in_=y_acc[:, : n * C])
                 else:
@@ -280,13 +262,15 @@ def tile_moe_sup_lin_relu2_kernel(tc, x_words, x_scales, w1_words, w1_scales, w2
                 back = banks.tile([P, P], F32, name="bank")
                 nc.tensor.transpose(back[:], turned[:, cols], identity[:])
                 nc.scalar.copy(out=total[:, cols], in_=back[:])
-            nc.sync.dma_start(out=out[:, t0 : t0 + n], in_=total[:])
+            nc.scalar.dma_start(out=out[:, t0 : t0 + n], in_=total[:])
             t0 = t0 + n
 
-        first_term = keep.tile([P, T - t0], F32)
-        second_term = keep.tile([P, T - t0], F32)
-        last_total = keep.tile([P, T - t0], F32)
-        nc.vector.tensor_tensor(first_term[:], y[:].indirect(pos1_sb[:, t0 // PER_COLUMN :]), gate_sb[:, 0, t0:], ALU.mult)
-        nc.vector.tensor_tensor(second_term[:], y[:].indirect(pos2_sb[:, t0 // PER_COLUMN :]), gate_sb[:, 1, t0:], ALU.mult)
-        nc.vector.tensor_tensor(last_total[:], first_term[:], second_term[:], ALU.add)
-        nc.sync.dma_start(out=out[:, t0:], in_=last_total[:])
+        for c, n in enumerate((384, 128)):
+            terms = keep.tile([P, 2, n], F32, name=f"terms{c}")
+            for r in range(2):
+                entries = slice(t0 // PER_COLUMN, (t0 + n) // PER_COLUMN)
+                nc.vector.tensor_tensor(terms[:, r, :], y[:].indirect(pos_sb[r][:, entries]), gate_sb[:, r, t0 : t0 + n], ALU.mult)
+            added = keep.tile([P, n], F32, name=f"added{c}")
+            nc.vector.tensor_tensor(added[:], terms[:, 0, :], terms[:, 1, :], ALU.add)
+            nc.sync.dma_start(out=out[:, t0 : t0 + n], in_=added[:])
+            t0 = t0 + n

@@ -1,7 +1,6 @@
 from contextlib import ExitStack
 
 import concourse.mybir as mybir
-from concourse.masks import make_identity
 
 K, T, E, C, H, N = 1536, 768, 12, 128, 512, 128
 P = 128
@@ -26,9 +25,10 @@ ACT = mybir.ActivationFunctionType
 WIDE = 512
 SLOT_CHUNKS = (4, 4, 2, 2)
 GATHER = 512
-GPSIMD_PAIRS = 4
-TURNED_CHUNKS = (256,)
-WARM_PASSES = 2
+GPSIMD_PAIRS = (0, 1, 4)
+SCALAR_PAIRS = (2, 3, 5)
+WARM_PASSES = 4
+WARM_ROWS = 64
 
 
 def tile_moe_sup_lin_relu2_kernel(tc, x_words, x_scales, w1_words, w1_scales, w2, gate, offs, pos1, pos2, out):
@@ -40,14 +40,13 @@ def tile_moe_sup_lin_relu2_kernel(tc, x_words, x_scales, w1_words, w1_scales, w2
             w1_raw = keep.tile([P, PASSES, 2 * H], U8, align_bytes=64)
             w1_plane = keep.tile([P, PASSES, H], U8, align_bytes=64)
             x_plane = keep.tile([P, PASSES, T], U8, align_bytes=64)
-            x_first = keep.tile([P, PACK * T], U8, align_bytes=64)
-            x_wide = [x_first[:, : PACK * WIDE]] + [keep.tile([P, PACK * WIDE], U8, align_bytes=64, name=f"x_wide{s}")[:] for s in range(1, PASSES)]
-            x_later = keep.tile([P, PASSES - 1, PACK * (T - WIDE)], U8, align_bytes=64)
-            x_rest = [x_first[:, PACK * WIDE :]] + [x_later[:, s, :] for s in range(PASSES - 1)]
+            x_wide = [keep.tile([P, PACK * WIDE], U8, align_bytes=64, name=f"x_wide{s}")[:] for s in range(PASSES)]
+            x_later = keep.tile([P, PASSES, PACK * (T - WIDE)], U8, align_bytes=64)
+            x_rest = [x_later[:, s, :] for s in range(PASSES)]
             table_in = keep.tile([P, 8], F32)
             table_out = keep.tile([P, 8], F32)
             w1_rows = keep.tile([P, PASSES * H // 4], I32)
-            nc.gpsimd.memset(x_plane[:].bitcast(I32), 0)
+            nc.vector.memset(x_plane[:].bitcast(I32), 0)
             nc.vector.memset(table_in[:], 0.0)
             nc.vector.memset(w1_plane[:].bitcast(I32), 0)
 
@@ -61,13 +60,13 @@ def tile_moe_sup_lin_relu2_kernel(tc, x_words, x_scales, w1_words, w1_scales, w2
             nc.scalar.dma_start(out=w1_raw[:].bitcast(I32), in_=w1_words.rearrange("s p b -> p s b").bitcast(I32))
             x_rows = x_words.rearrange("s p t d -> p s (t d)")
             x_scale_rows = x_scales.rearrange("s (q r) t -> r q s t", r=4)
-            nc.scalar.dma_start(out=x_first[:].bitcast(I32), in_=x_rows[:, 0, :].bitcast(I32))
+            nc.scalar.dma_start(out=x_wide[0].bitcast(I32), in_=x_rows[:, 0, : PACK * WIDE].bitcast(I32))
             nc.scalar.activation(table_out[:], table_in[:], ACT.Square)
             for r in range(4):
                 nc.sync.dma_start(out=x_plane[r:P:32, :, :].bitcast(I32), in_=x_scale_rows[r].bitcast(I32))
             for s in range(1, PASSES):
                 nc.sync.dma_start(out=x_wide[s].bitcast(I32), in_=x_rows[:, s, : PACK * WIDE].bitcast(I32))
-            nc.sync.dma_start(out=x_later[:].bitcast(I32), in_=x_rows[:, 1:, PACK * WIDE :].bitcast(I32))
+            nc.sync.dma_start(out=x_later[:].bitcast(I32), in_=x_rows[:, :, PACK * WIDE :].bitcast(I32))
             for q in range(4):
                 rows = slice(32 * q, 32 * q + 4)
                 nc.vector.tensor_copy(out=w1_plane[rows].rearrange("p s i -> p (s i)").bitcast(I32), in_=w1_rows[rows, :])
@@ -86,7 +85,7 @@ def tile_moe_sup_lin_relu2_kernel(tc, x_words, x_scales, w1_words, w1_scales, w2
 
             offs_sb = keep.tile([P, SLOTS // PER_COLUMN], U16)
             w2_raw = [keep.tile([P, 2, PACK * N], F32, name=f"w2_raw{g}") for g in range(PAIRS)]
-            for g in range(PAIRS):
+            for g in GPSIMD_PAIRS + SCALAR_PAIRS:
                 nc.sync.dma_start(out=w2_raw[g][:], in_=w2[2 * g : 2 * g + 2].rearrange("e (p j) n -> p e (j n)", j=PACK))
                 if g == 0:
                     nc.sync.dma_start(offs_sb[:], offs)
@@ -97,19 +96,19 @@ def tile_moe_sup_lin_relu2_kernel(tc, x_words, x_scales, w1_words, w1_scales, w2
             gate_sb = keep.tile([P, 2, T], F32)
             nc.sync.dma_start(out=gate_sb[:], in_=gate.rearrange("r p t -> p r t"))
 
-            zeros = keep.tile([P, PACK * P], BF16, align_bytes=64)
-            zero_codes = keep.tile([P, P], U32, align_bytes=64)
-            zero_bytes = keep.tile([P, P], U8, align_bytes=64)
-            nc.vector.memset(zeros[:].bitcast(I32), 0)
+            zeros = keep.tile([P, PACK * WIDE], BF16, align_bytes=64)
+            zero_codes = keep.tile([P, WIDE], U32, align_bytes=64)
+            zero_bytes = keep.tile([P, WIDE], U8, align_bytes=64)
+            nc.gpsimd.memset(zeros[:].bitcast(I32), 0)
             nc.vector.quantize_mx(out=zero_codes[:].bitcast(FP8X4), scales=zero_bytes[:], in_=zeros[:])
             idle = psum.tile([P, WIDE], F32, tag="idle")
             for w in range(WARM_PASSES):
                 nc.tensor.matmul_mx(
-                    out=idle[:],
-                    lhsT=zero_codes[:].bitcast(FP8X4),
-                    lhsT_scale=zero_bytes[:],
-                    rhs=w1_raw[:, 0, :].bitcast(FP4X4),
-                    rhs_scale=w1_plane[:, 0, :],
+                    out=idle[:WARM_ROWS, :],
+                    lhsT=zero_codes[:, :WARM_ROWS].bitcast(FP8X4),
+                    lhsT_scale=zero_bytes[:, :WARM_ROWS],
+                    rhs=zero_codes[:].bitcast(FP8X4),
+                    rhs_scale=zero_bytes[:],
                     start=True,
                     stop=True,
                 )
@@ -168,15 +167,16 @@ def tile_moe_sup_lin_relu2_kernel(tc, x_words, x_scales, w1_words, w1_scales, w2
             square_wide(1)
 
             first_expert = [sum(SLOT_CHUNKS[:c]) for c in range(len(SLOT_CHUNKS))]
-            late_bf = keep.tile([P, (PAIRS - GPSIMD_PAIRS) * 2 * N * PACK], BF16, align_bytes=64, tag="relu_wide1")
-            early_bf = keep.tile([P, GPSIMD_PAIRS * 2 * N * PACK], BF16, align_bytes=64)
+            late_bf = keep.tile([P, len(SCALAR_PAIRS) * 2 * N * PACK], BF16, align_bytes=64, tag="relu_wide1")
+            early_bf = keep.tile([P, len(GPSIMD_PAIRS) * 2 * N * PACK], BF16, align_bytes=64)
 
             def rounded(e0, e1):
-                tile, base = (early_bf, 0) if e0 < 2 * GPSIMD_PAIRS else (late_bf, 2 * GPSIMD_PAIRS)
-                return tile[:, (e0 - base) * N * PACK : (e1 - base) * N * PACK]
+                tile, pairs = (early_bf, GPSIMD_PAIRS) if e0 // 2 in GPSIMD_PAIRS else (late_bf, SCALAR_PAIRS)
+                first = 2 * pairs.index(e0 // 2)
+                return tile[:, first * N * PACK : (first + e1 - e0) * N * PACK]
 
             for g in range(PAIRS):
-                if g < GPSIMD_PAIRS:
+                if g in GPSIMD_PAIRS:
                     nc.gpsimd.tensor_scalar(
                         rounded(2 * g, 2 * g + 2).rearrange("p (e n j) -> p e n j", e=2, j=PACK),
                         w2_raw[g][:].rearrange("p e (j n) -> p e n j", j=PACK),
@@ -190,9 +190,6 @@ def tile_moe_sup_lin_relu2_kernel(tc, x_words, x_scales, w1_words, w1_scales, w2
                         out=rounded(2 * g, 2 * g + 2).rearrange("p (e c i j) -> p e c j i", e=2, i=4, j=PACK),
                         in_=w2_raw[g][:].rearrange("p e (j c i) -> p e c j i", j=PACK, i=4),
                     )
-
-            identity = keep.tile([P, P], F32)
-            make_identity(nc, identity[:])
 
             runs = SLOTS // GATHER
             gathered = [keep.tile([P, 2, GATHER], U32, name=f"gathered{k}") for k in range(runs)]
@@ -239,33 +236,9 @@ def tile_moe_sup_lin_relu2_kernel(tc, x_words, x_scales, w1_words, w1_scales, w2
                 else:
                     nc.vector.tensor_copy(out=y[:, y_cols], in_=y_acc[:, : n * C])
 
-        banks = ctx.enter_context(tc.psum_pool(name="banks", bufs=8))
         pos_sb = (pos1_sb, pos2_sb)
         t0 = 0
-        for c, n in enumerate(TURNED_CHUNKS):
-            weighted = keep.tile([P, 2, n], F32, name=f"weighted{c}")
-            for r in range(2):
-                entries = slice(t0 // PER_COLUMN, (t0 + n) // PER_COLUMN)
-                nc.vector.tensor_tensor(weighted[:, r, :], y[:].indirect(pos_sb[r][:, entries]), gate_sb[:, r, t0 : t0 + n], ALU.mult)
-            turned = keep.tile([P, n], F32, name=f"turned{c}")
-            total = keep.tile([P, n], F32, name=f"total{c}")
-            for k in range(n // P):
-                cols = slice(k * P, (k + 1) * P)
-                summed = banks.tile([P, P], F32, name="bank")
-                for r in range(2):
-                    nc.tensor.matmul(
-                        summed[:], lhsT=weighted[:, r, cols], rhs=identity[:], start=(r == 0), stop=(r == 1), is_transpose=True
-                    )
-                nc.scalar.copy(out=turned[:, cols], in_=summed[:])
-            for k in range(n // P):
-                cols = slice(k * P, (k + 1) * P)
-                back = banks.tile([P, P], F32, name="bank")
-                nc.tensor.transpose(back[:], turned[:, cols], identity[:])
-                nc.scalar.copy(out=total[:, cols], in_=back[:])
-            nc.scalar.dma_start(out=out[:, t0 : t0 + n], in_=total[:])
-            t0 = t0 + n
-
-        for c, n in enumerate((384, 128)):
+        for c, n in enumerate((384, 256, 128)):
             terms = keep.tile([P, 2, n], F32, name=f"terms{c}")
             for r in range(2):
                 entries = slice(t0 // PER_COLUMN, (t0 + n) // PER_COLUMN)

@@ -23,10 +23,12 @@ ALU = mybir.AluOpType
 ACT = mybir.ActivationFunctionType
 
 WIDE = 512
-SLOT_CHUNKS = (4, 4, 2, 2)
+BLOCKS = (T - WIDE) // P
 GATHER = 512
-GPSIMD_PAIRS = (0, 1, 4)
-SCALAR_PAIRS = (2, 3, 5)
+CHUNK_PAIRS = ((0, 1), (2, 3), (4,), (5,))
+GPSIMD_PAIRS = CHUNK_PAIRS[0] + CHUNK_PAIRS[2]
+SCALAR_PAIRS = CHUNK_PAIRS[1] + CHUNK_PAIRS[3]
+STORES = (448, 192, 128)
 WARM_PASSES = 4
 WARM_ROWS = 64
 
@@ -35,215 +37,235 @@ def tile_moe_sup_lin_relu2_kernel(tc, x_words, x_scales, w1_words, w1_scales, w2
     nc = tc.nc
     with ExitStack() as ctx:
         keep = ctx.enter_context(tc.tile_pool(name="keep", bufs=1))
+        psum = ctx.enter_context(tc.psum_pool(name="psum", bufs=1))
 
-        with tc.psum_pool(name="psum", bufs=1) as psum, tc.psum_pool(name="y_psum", bufs=3) as y_psum:
-            w1_raw = keep.tile([P, PASSES, 2 * H], U8, align_bytes=64)
-            w1_plane = keep.tile([P, PASSES, H], U8, align_bytes=64)
-            x_plane = keep.tile([P, PASSES, T], U8, align_bytes=64)
-            x_wide = [keep.tile([P, PACK * WIDE], U8, align_bytes=64, name=f"x_wide{s}")[:] for s in range(PASSES)]
-            x_later = keep.tile([P, PASSES, PACK * (T - WIDE)], U8, align_bytes=64)
-            x_rest = [x_later[:, s, :] for s in range(PASSES)]
-            table_in = keep.tile([P, 8], F32)
-            table_out = keep.tile([P, 8], F32)
-            w1_rows = keep.tile([P, PASSES * H // 4], I32)
-            nc.vector.memset(x_plane[:].bitcast(I32), 0)
-            nc.vector.memset(table_in[:], 0.0)
-            nc.vector.memset(w1_plane[:].bitcast(I32), 0)
+        w1_raw = keep.tile([P, PASSES, 2 * H], U8, align_bytes=64)
+        w1_plane = keep.tile([P, PASSES, H], U8, align_bytes=64)
+        x_plane = keep.tile([P, PASSES, T], U8, align_bytes=64)
+        x_wide = [keep.tile([P, PACK * WIDE], U8, align_bytes=64, name=f"x_wide{s}") for s in range(PASSES)]
+        x_block = [keep.tile([P, PASSES, PACK * P], U8, align_bytes=64, name=f"x_block{k}") for k in range(BLOCKS)]
+        table_in = keep.tile([P, 8], F32)
+        table_out = keep.tile([P, 8], F32)
+        w1_rows = keep.tile([P, PASSES * H // 4], I32)
+        nc.vector.memset(x_plane[:].bitcast(I32), 0)
+        nc.vector.memset(table_in[:], 0.0)
+        nc.vector.memset(w1_plane[:].bitcast(I32), 0)
 
-            w1_scale_rows = w1_scales.rearrange("s (q r) i -> q r s i", r=4)
-            for q in range(4):
-                queue = nc.sync if q < 2 else nc.scalar
-                queue.dma_start(
-                    out=w1_rows[32 * q : 32 * q + 4, :].rearrange("p (s i) -> p s i", s=PASSES),
-                    in_=w1_scale_rows[q].bitcast(I32),
-                )
-            nc.scalar.dma_start(out=w1_raw[:].bitcast(I32), in_=w1_words.rearrange("s p b -> p s b").bitcast(I32))
-            x_rows = x_words.rearrange("s p t d -> p s (t d)")
-            x_scale_rows = x_scales.rearrange("s (q r) t -> r q s t", r=4)
-            nc.scalar.dma_start(out=x_wide[0].bitcast(I32), in_=x_rows[:, 0, : PACK * WIDE].bitcast(I32))
-            nc.scalar.activation(table_out[:], table_in[:], ACT.Square)
-            for r in range(4):
-                nc.sync.dma_start(out=x_plane[r:P:32, :, :].bitcast(I32), in_=x_scale_rows[r].bitcast(I32))
-            for s in range(1, PASSES):
-                nc.sync.dma_start(out=x_wide[s].bitcast(I32), in_=x_rows[:, s, : PACK * WIDE].bitcast(I32))
-            nc.sync.dma_start(out=x_later[:].bitcast(I32), in_=x_rows[:, :, PACK * WIDE :].bitcast(I32))
-            for q in range(4):
-                rows = slice(32 * q, 32 * q + 4)
-                nc.vector.tensor_copy(out=w1_plane[rows].rearrange("p s i -> p (s i)").bitcast(I32), in_=w1_rows[rows, :])
+        w1_scale_rows = w1_scales.rearrange("s (q r) i -> q r s i", r=4)
+        for q in range(4):
+            queue = nc.sync if q < 2 else nc.scalar
+            queue.dma_start(
+                out=w1_rows[32 * q : 32 * q + 4, :].rearrange("p (s i) -> p s i", s=PASSES),
+                in_=w1_scale_rows[q].bitcast(I32),
+            )
+        nc.scalar.dma_start(out=w1_raw[:].bitcast(I32), in_=w1_words.rearrange("s p b -> p s b").bitcast(I32))
+        x_rows = x_words.rearrange("s p t d -> p s (t d)")
+        x_scale_rows = x_scales.rearrange("s (q r) t -> r q s t", r=4)
+        nc.scalar.dma_start(out=x_wide[0][:].bitcast(I32), in_=x_rows[:, 0, : PACK * WIDE].bitcast(I32))
+        nc.scalar.activation(table_out[:], table_in[:], ACT.Square)
+        for r in range(4):
+            nc.sync.dma_start(out=x_plane[r:P:32, :, :].bitcast(I32), in_=x_scale_rows[r].bitcast(I32))
+        for s in range(1, PASSES):
+            nc.sync.dma_start(out=x_wide[s][:].bitcast(I32), in_=x_rows[:, s, : PACK * WIDE].bitcast(I32))
+        for k in range(BLOCKS):
+            t0 = WIDE + k * P
+            nc.sync.dma_start(out=x_block[k][:].bitcast(I32), in_=x_rows[:, :, PACK * t0 : PACK * (t0 + P)].bitcast(I32))
+        for q in range(4):
+            rows = slice(32 * q, 32 * q + 4)
+            nc.vector.tensor_copy(out=w1_plane[rows].rearrange("p s i -> p (s i)").bitcast(I32), in_=w1_rows[rows, :])
 
-            w1_codes = [keep.tile([P, PASSES, H], U8, align_bytes=64, name=f"w1_codes{u}") for u in range(2)]
-            w1_bytes = [keep.tile([P, PASSES, H // 2], U8, align_bytes=64, name=f"w1_bytes{u}") for u in range(2)]
-            for u in range(2):
-                nc.vector.tensor_copy(
-                    out=w1_bytes[u][:].rearrange("p s (b m) -> p b s m", b=2),
-                    in_=w1_plane[:].rearrange("p s (m j) -> p j s m", j=PACK)[:, 2 * u : 2 * u + 2, :, :],
-                )
-                nc.vector.tensor_copy(
-                    out=w1_codes[u][:].bitcast(U16).rearrange("p s (b m) -> p b s m", b=2),
-                    in_=w1_raw[:].bitcast(U16).rearrange("p s (m j) -> p j s m", j=PACK)[:, 2 * u : 2 * u + 2, :, :],
-                )
+        w1_codes = [keep.tile([P, PASSES, H], U8, align_bytes=64, name=f"w1_codes{u}") for u in range(2)]
+        w1_bytes = [keep.tile([P, PASSES, H // 2], U8, align_bytes=64, name=f"w1_bytes{u}") for u in range(2)]
+        for u in range(2):
+            nc.vector.tensor_copy(
+                out=w1_bytes[u][:].rearrange("p s (b m) -> p b s m", b=2),
+                in_=w1_plane[:].rearrange("p s (m j) -> p j s m", j=PACK)[:, 2 * u : 2 * u + 2, :, :],
+            )
+            nc.vector.tensor_copy(
+                out=w1_codes[u][:].bitcast(U16).rearrange("p s (b m) -> p b s m", b=2),
+                in_=w1_raw[:].bitcast(U16).rearrange("p s (m j) -> p j s m", j=PACK)[:, 2 * u : 2 * u + 2, :, :],
+            )
 
-            offs_sb = keep.tile([P, SLOTS // PER_COLUMN], U16)
-            w2_raw = [keep.tile([P, 2, PACK * N], F32, name=f"w2_raw{g}") for g in range(PAIRS)]
-            for g in GPSIMD_PAIRS + SCALAR_PAIRS:
-                nc.sync.dma_start(out=w2_raw[g][:], in_=w2[2 * g : 2 * g + 2].rearrange("e (p j) n -> p e (j n)", j=PACK))
-                if g == 0:
-                    nc.sync.dma_start(offs_sb[:], offs)
-            pos1_sb = keep.tile([P, T // PER_COLUMN], U16)
-            nc.sync.dma_start(pos1_sb[:], pos1)
-            pos2_sb = keep.tile([P, T // PER_COLUMN], U16)
-            nc.sync.dma_start(pos2_sb[:], pos2)
-            gate_sb = keep.tile([P, 2, T], F32)
-            nc.sync.dma_start(out=gate_sb[:], in_=gate.rearrange("r p t -> p r t"))
+        offs_sb = keep.tile([P, SLOTS // PER_COLUMN], U16)
+        w2_raw = [keep.tile([P, 2, PACK * N], F32, name=f"w2_raw{g}") for g in range(PAIRS)]
+        for g in GPSIMD_PAIRS + SCALAR_PAIRS:
+            nc.sync.dma_start(out=w2_raw[g][:], in_=w2[2 * g : 2 * g + 2].rearrange("e (p j) n -> p e (j n)", j=PACK))
+            if g == GPSIMD_PAIRS[0]:
+                nc.sync.dma_start(offs_sb[:], offs)
+        pos1_sb = keep.tile([P, T // PER_COLUMN], U16)
+        nc.sync.dma_start(pos1_sb[:], pos1)
+        pos2_sb = keep.tile([P, T // PER_COLUMN], U16)
+        nc.sync.dma_start(pos2_sb[:], pos2)
+        gate_sb = keep.tile([P, 2, T], F32)
+        nc.sync.dma_start(out=gate_sb[:], in_=gate.rearrange("r p t -> p r t"))
 
-            zeros = keep.tile([P, PACK * WIDE], BF16, align_bytes=64)
-            zero_codes = keep.tile([P, WIDE], U32, align_bytes=64)
-            zero_bytes = keep.tile([P, WIDE], U8, align_bytes=64)
-            nc.gpsimd.memset(zeros[:].bitcast(I32), 0)
-            nc.vector.quantize_mx(out=zero_codes[:].bitcast(FP8X4), scales=zero_bytes[:], in_=zeros[:])
-            idle = psum.tile([P, WIDE], F32, tag="idle")
-            for w in range(WARM_PASSES):
+        zeros = keep.tile([P, PACK * WIDE], BF16, align_bytes=64)
+        zero_codes = keep.tile([P, WIDE], U32, align_bytes=64)
+        zero_bytes = keep.tile([P, WIDE], U8, align_bytes=64)
+        nc.gpsimd.memset(zeros[:].bitcast(I32), 0)
+        nc.vector.quantize_mx(out=zero_codes[:].bitcast(FP8X4), scales=zero_bytes[:], in_=zeros[:])
+        idle = psum.tile([P, WIDE], F32, tag="blocks_of_half_1")
+        for w in range(WARM_PASSES):
+            nc.tensor.matmul_mx(
+                out=idle[:WARM_ROWS, :],
+                lhsT=zero_codes[:, :WARM_ROWS].bitcast(FP8X4),
+                lhsT_scale=zero_bytes[:, :WARM_ROWS],
+                rhs=zero_codes[:].bitcast(FP8X4),
+                rhs_scale=zero_bytes[:],
+                start=True,
+                stop=True,
+            )
+
+        def first_layer(acc, u, b, s, words, t0, t1):
+            nc.tensor.matmul_mx(
+                out=acc,
+                lhsT=w1_codes[u][:, s, 2 * P * b : 2 * P * (b + 1)].bitcast(FP4X4),
+                lhsT_scale=w1_bytes[u][:, s, P * b : P * (b + 1)],
+                rhs=words.bitcast(FP8X4),
+                rhs_scale=x_plane[:, s, t0:t1],
+                start=(s == 0),
+                stop=(s == PASSES - 1),
+            )
+
+        h_pairs = [keep.tile([P, 2 * T], BF16, align_bytes=64, name=f"h_pairs{u}") for u in range(2)]
+
+        def block_sums(u, k0, k1, tag):
+            t0, t1 = WIDE + k0 * P, WIDE + k1 * P
+            sums = psum.tile([P, 2, t1 - t0], F32, name=f"sums{u}{k0}", tag=tag)
+            for b in range(2):
+                for k in range(k0, k1):
+                    t = WIDE + k * P
+                    for s in range(PASSES):
+                        first_layer(sums[:, b, t - t0 : t - t0 + P], u, b, s, x_block[k][:, s, :], t, t + P)
+            relu = keep.tile([P, t1 - t0, 2], F32, name=f"relu{u}{k0}", align_bytes=64)
+            return sums[:].rearrange("p b t -> p t b"), relu[:], h_pairs[u][:, 2 * t0 : 2 * t1].rearrange("p (t b) -> p t b", b=2)
+
+        relu_wide = [keep.tile([P, 2, WIDE], F32, name=f"relu_wide{u}", tag=f"relu_wide{u}", align_bytes=64) for u in range(2)]
+
+        def square_wide(u):
+            nc.scalar.activation(
+                h_pairs[u][:, : 2 * WIDE].rearrange("p (t b) -> p t b", b=2),
+                relu_wide[u][:].rearrange("p b t -> p t b"),
+                ACT.Square,
+            )
+
+        wide = [psum.tile([P, WIDE], F32, name=f"wide0{b}", tag=f"wide{b}") for b in range(2)]
+        for s in range(PASSES):
+            for b in range(2):
+                first_layer(wide[b][:], 0, b, s, x_wide[s][:], 0, WIDE)
+        nc.vector.tensor_scalar_max(relu_wide[0][:, 0, :], wide[0][:], 0.0)
+        nc.scalar.activation(relu_wide[0][:, 1, :], wide[1][:], ACT.Relu)
+        square_wide(0)
+        blocks = [block_sums(0, k, k + 1, f"block{k}") for k in range(BLOCKS)]
+        for sums, relu, pairs in blocks:
+            nc.vector.tensor_scalar_max(relu, sums, 0.0)
+        for sums, relu, pairs in blocks:
+            nc.vector.tensor_tensor(pairs, sums, relu, ALU.mult)
+
+        sums, relu, pairs = block_sums(1, 0, BLOCKS, "blocks_of_half_1")
+        nc.scalar.activation(relu, sums, ACT.Relu)
+        nc.scalar.activation(pairs, relu, ACT.Square)
+        for b in range(2):
+            group = psum.tile([P, WIDE], F32, name=f"wide1{b}", tag=f"wide{b}")
+            for s in range(PASSES):
+                first_layer(group[:], 1, b, s, x_wide[s][:], 0, WIDE)
+            nc.scalar.activation(relu_wide[1][:, b, :], group[:], ACT.Relu)
+        square_wide(1)
+
+        gathered = [keep.tile([P, 2, GATHER], U32, name=f"gathered{k}", tag=f"gathered{k}", align_bytes=64) for k in range(SLOTS // GATHER)]
+        for u in range(2):
+            for k in range(SLOTS // GATHER):
+                entries = slice(k * GATHER // PER_COLUMN, (k + 1) * GATHER // PER_COLUMN)
+                nc.vector.tensor_copy(out=gathered[k][:, u, :], in_=h_pairs[u][:].bitcast(U32).indirect(offs_sb[:, entries]))
+
+        pair_width = 2 * N * PACK
+        gpsimd_bf = keep.tile([P, len(GPSIMD_PAIRS) * pair_width], BF16, align_bytes=64)
+        scalar_bf = keep.tile([P, len(SCALAR_PAIRS) * pair_width], BF16, align_bytes=64, tag="relu_wide1")
+
+        def rounded(pairs_of):
+            tile, share = (gpsimd_bf, GPSIMD_PAIRS) if pairs_of[0] in GPSIMD_PAIRS else (scalar_bf, SCALAR_PAIRS)
+            first = share.index(pairs_of[0])
+            return tile[:, first * pair_width : (first + len(pairs_of)) * pair_width]
+
+        for g in GPSIMD_PAIRS:
+            nc.gpsimd.tensor_scalar(
+                rounded((g,)).rearrange("p (e n j) -> p e n j", e=2, j=PACK),
+                w2_raw[g][:].rearrange("p e (j n) -> p e n j", j=PACK),
+                1.0,
+                0.0,
+                ALU.mult,
+                ALU.add,
+            )
+
+        def round_on_scalar(g):
+            nc.scalar.copy(
+                out=rounded((g,)).rearrange("p (e c i j) -> p e c j i", e=2, i=4, j=PACK),
+                in_=w2_raw[g][:].rearrange("p e (j c i) -> p e c j i", j=PACK, i=4),
+            )
+
+        slot_h = []
+        for c, pairs_of in enumerate(CHUNK_PAIRS):
+            if c < len(SCALAR_PAIRS):
+                round_on_scalar(SCALAR_PAIRS[c])
+            width = 2 * len(pairs_of) * C
+            k, s0 = divmod(2 * pairs_of[0] * C, GATHER)
+            slot_h.append(keep.tile([P, width * PACK], BF16, align_bytes=64, name=f"slot_h{c}"))
+            nc.scalar.copy(
+                out=slot_h[c][:].bitcast(U32).rearrange("p (s u) -> p s u", u=2),
+                in_=gathered[k][:, :, s0 : s0 + width].rearrange("p u s -> p s u"),
+            )
+
+        w2_codes = keep.tile([P, E * N], U32, align_bytes=64, tag="gathered0")
+        w2_bytes = keep.tile([P, E * N], U8, align_bytes=64)
+        y_banks = ("block0", "block1", "wide0", "wide1")
+        y_sums = []
+        for c, pairs_of in enumerate(CHUNK_PAIRS):
+            e0, n = 2 * pairs_of[0], 2 * len(pairs_of)
+            nc.vector.quantize_mx(
+                out=w2_codes[:, e0 * N : (e0 + n) * N].bitcast(FP8X4),
+                scales=w2_bytes[:, e0 * N : (e0 + n) * N],
+                in_=rounded(pairs_of),
+            )
+            h_codes = keep.tile([P, n * C], U32, align_bytes=64, name=f"h_codes{c}")
+            h_bytes = keep.tile([P, n * C], U8, align_bytes=64, name=f"h_bytes{c}")
+            nc.vector.quantize_mx(out=h_codes[:].bitcast(FP8X4), scales=h_bytes[:], in_=slot_h[c][:])
+            y_sums.append(psum.tile([P, n * C], F32, name=f"y_sums{c}", tag=y_banks[c]))
+            for m in range(n):
+                w_cols = slice((e0 + m) * N, (e0 + m + 1) * N)
+                slots = slice(m * C, (m + 1) * C)
                 nc.tensor.matmul_mx(
-                    out=idle[:WARM_ROWS, :],
-                    lhsT=zero_codes[:, :WARM_ROWS].bitcast(FP8X4),
-                    lhsT_scale=zero_bytes[:, :WARM_ROWS],
-                    rhs=zero_codes[:].bitcast(FP8X4),
-                    rhs_scale=zero_bytes[:],
+                    out=y_sums[c][:, slots],
+                    lhsT=w2_codes[:, w_cols].bitcast(FP8X4),
+                    lhsT_scale=w2_bytes[:, w_cols],
+                    rhs=h_codes[:, slots].bitcast(FP8X4),
+                    rhs_scale=h_bytes[:, slots],
                     start=True,
                     stop=True,
                 )
-
-            def first_layer(acc, u, b, t0, t1, passes=range(PASSES)):
-                for s in passes:
-                    words = x_wide[s] if t0 == 0 else x_rest[s][:, PACK * (t0 - WIDE) : PACK * (t1 - WIDE)]
-                    nc.tensor.matmul_mx(
-                        out=acc,
-                        lhsT=w1_codes[u][:, s, 2 * P * b : 2 * P * (b + 1)].bitcast(FP4X4),
-                        lhsT_scale=w1_bytes[u][:, s, P * b : P * (b + 1)],
-                        rhs=words.bitcast(FP8X4),
-                        rhs_scale=x_plane[:, s, t0:t1],
-                        start=(s == 0),
-                        stop=(s == PASSES - 1),
-                    )
-
-            h_pairs = [keep.tile([P, 2 * T], BF16, align_bytes=64, name=f"h_pairs{u}", tag=f"h_pairs{u}") for u in range(2)]
-            def rest_tokens(u, t0, t1, tag):
-                sums = psum.tile([P, 2, t1 - t0], F32, name=f"rest{u}_{t0}", tag=tag)
-                for b in range(2):
-                    for t in range(t0, t1, P):
-                        first_layer(sums[:, b, t - t0 : t - t0 + P], u, b, t, t + P)
-                relu = keep.tile([P, t1 - t0, 2], F32, name=f"relu_rest{u}_{t0}", align_bytes=64)
-                return sums[:].rearrange("p b t -> p t b"), relu[:], h_pairs[u][:, 2 * t0 : 2 * t1].rearrange("p (t b) -> p t b", b=2)
-
-            relu_wide = [keep.tile([P, 2, WIDE], F32, name=f"relu_wide{u}", tag=f"relu_wide{u}", align_bytes=64) for u in range(2)]
-
-            def square_wide(u):
-                nc.scalar.activation(
-                    h_pairs[u][:, : 2 * WIDE].rearrange("p (t b) -> p t b", b=2),
-                    relu_wide[u][:].rearrange("p b t -> p t b"),
-                    ACT.Square,
-                )
-
-            wide = [psum.tile([P, WIDE], F32, name=f"wide{b}", tag=f"wide{b}") for b in range(2)]
-            for s in range(PASSES):
-                for b in range(2):
-                    first_layer(wide[b][:], 0, b, 0, WIDE, [s])
-            nc.scalar.activation(relu_wide[0][:, 0, :], wide[0][:], ACT.Relu)
-            nc.vector.tensor_scalar_max(relu_wide[0][:, 1, :], wide[1][:], 0.0)
-            square_wide(0)
-            blocks = [rest_tokens(0, t0, t1, f"rest{t0}") for t0, t1 in ((WIDE, WIDE + P), (WIDE + P, T))]
-            for sums, relu, pairs in blocks:
-                nc.vector.tensor_scalar_max(relu, sums, 0.0)
-            for sums, relu, pairs in blocks:
-                nc.vector.tensor_tensor(pairs, sums, relu, ALU.mult)
-
-            sums, relu, pairs = rest_tokens(1, WIDE, T, "idle")
-            nc.scalar.activation(relu, sums, ACT.Relu)
-            nc.scalar.activation(pairs, relu, ACT.Square)
-            for b in range(2):
-                wide = psum.tile([P, WIDE], F32, name=f"wide{b}", tag=f"wide{b}")
-                first_layer(wide[:], 1, b, 0, WIDE)
-                nc.scalar.activation(relu_wide[1][:, b, :], wide[:], ACT.Relu)
-            square_wide(1)
-
-            first_expert = [sum(SLOT_CHUNKS[:c]) for c in range(len(SLOT_CHUNKS))]
-            late_bf = keep.tile([P, len(SCALAR_PAIRS) * 2 * N * PACK], BF16, align_bytes=64, tag="relu_wide1")
-            early_bf = keep.tile([P, len(GPSIMD_PAIRS) * 2 * N * PACK], BF16, align_bytes=64)
-
-            def rounded(e0, e1):
-                tile, pairs = (early_bf, GPSIMD_PAIRS) if e0 // 2 in GPSIMD_PAIRS else (late_bf, SCALAR_PAIRS)
-                first = 2 * pairs.index(e0 // 2)
-                return tile[:, first * N * PACK : (first + e1 - e0) * N * PACK]
-
-            for g in range(PAIRS):
-                if g in GPSIMD_PAIRS:
-                    nc.gpsimd.tensor_scalar(
-                        rounded(2 * g, 2 * g + 2).rearrange("p (e n j) -> p e n j", e=2, j=PACK),
-                        w2_raw[g][:].rearrange("p e (j n) -> p e n j", j=PACK),
-                        1.0,
-                        0.0,
-                        ALU.mult,
-                        ALU.add,
-                    )
-                else:
-                    nc.scalar.copy(
-                        out=rounded(2 * g, 2 * g + 2).rearrange("p (e c i j) -> p e c j i", e=2, i=4, j=PACK),
-                        in_=w2_raw[g][:].rearrange("p e (j c i) -> p e c j i", j=PACK, i=4),
-                    )
-
-            runs = SLOTS // GATHER
-            gathered = [keep.tile([P, 2, GATHER], U32, name=f"gathered{k}") for k in range(runs)]
-            for u in range(2):
-                for k in range(runs):
-                    entries = slice(k * GATHER // PER_COLUMN, (k + 1) * GATHER // PER_COLUMN)
-                    nc.vector.tensor_copy(out=gathered[k][:, u, :], in_=h_pairs[u][:].bitcast(U32).indirect(offs_sb[:, entries]))
-            slot_h = [keep.tile([P, n * C * PACK], BF16, align_bytes=64, name=f"slot_h{c}") for c, n in enumerate(SLOT_CHUNKS)]
-            for c, n in enumerate(SLOT_CHUNKS):
-                k, s0 = divmod(first_expert[c] * C, GATHER)
-                nc.scalar.copy(
-                    out=slot_h[c][:].bitcast(U32).rearrange("p (s u) -> p s u", u=2),
-                    in_=gathered[k][:, :, s0 : s0 + n * C].rearrange("p u s -> p s u"),
-                )
-            w2_codes = keep.tile([P, E * N], U32, align_bytes=64, tag="h_pairs1")
-            w2_bytes = keep.tile([P, E * N], U8, align_bytes=64)
-            y = keep.tile([P, SLOTS], F32)
-            for c, n in enumerate(SLOT_CHUNKS):
-                e0 = first_expert[c]
-                nc.vector.quantize_mx(
-                    out=w2_codes[:, e0 * N : (e0 + n) * N].bitcast(FP8X4),
-                    scales=w2_bytes[:, e0 * N : (e0 + n) * N],
-                    in_=rounded(e0, e0 + n),
-                )
-                h_codes = keep.tile([P, n * C], U32, align_bytes=64, name=f"h_codes{c}")
-                h_bytes = keep.tile([P, n * C], U8, align_bytes=64, name=f"h_bytes{c}")
-                nc.vector.quantize_mx(out=h_codes[:].bitcast(FP8X4), scales=h_bytes[:], in_=slot_h[c][:])
-                y_acc = y_psum.tile([P, WIDE], F32, name="y_acc")
-                for m in range(n):
-                    w_cols = slice((e0 + m) * N, (e0 + m + 1) * N)
-                    slots = slice(m * C, (m + 1) * C)
-                    nc.tensor.matmul_mx(
-                        out=y_acc[:, slots],
-                        lhsT=w2_codes[:, w_cols].bitcast(FP8X4),
-                        lhsT_scale=w2_bytes[:, w_cols],
-                        rhs=h_codes[:, slots].bitcast(FP8X4),
-                        rhs_scale=h_bytes[:, slots],
-                        start=True,
-                        stop=True,
-                    )
-                y_cols = slice(e0 * C, (e0 + n) * C)
-                if c < len(SLOT_CHUNKS) - 1:
-                    nc.scalar.copy(out=y[:, y_cols], in_=y_acc[:, : n * C])
-                else:
-                    nc.vector.tensor_copy(out=y[:, y_cols], in_=y_acc[:, : n * C])
+        y = keep.tile([P, SLOTS], F32)
+        for c, pairs_of in enumerate(CHUNK_PAIRS):
+            nc.scalar.copy(out=y[:, 2 * pairs_of[0] * C : 2 * (pairs_of[-1] + 1) * C], in_=y_sums[c][:])
 
         pos_sb = (pos1_sb, pos2_sb)
-        t0 = 0
-        for c, n in enumerate((384, 256, 128)):
-            terms = keep.tile([P, 2, n], F32, name=f"terms{c}")
-            for r in range(2):
-                entries = slice(t0 // PER_COLUMN, (t0 + n) // PER_COLUMN)
-                nc.vector.tensor_tensor(terms[:, r, :], y[:].indirect(pos_sb[r][:, entries]), gate_sb[:, r, t0 : t0 + n], ALU.mult)
-            added = keep.tile([P, n], F32, name=f"added{c}")
-            nc.vector.tensor_tensor(added[:], terms[:, 0, :], terms[:, 1, :], ALU.add)
-            nc.sync.dma_start(out=out[:, t0 : t0 + n], in_=added[:])
-            t0 = t0 + n
+        starts = [sum(STORES[:c]) for c in range(len(STORES))]
+        terms = [keep.tile([P, 2, n], F32, name=f"terms{c}") for c, n in enumerate(STORES)]
+
+        def weigh(c, r):
+            t0, t1 = starts[c], starts[c] + STORES[c]
+            entries = slice(t0 // PER_COLUMN, t1 // PER_COLUMN)
+            nc.vector.tensor_tensor(terms[c][:, r, :], y[:].indirect(pos_sb[r][:, entries]), gate_sb[:, r, t0:t1], ALU.mult)
+
+        def add_and_store(c):
+            total = keep.tile([P, STORES[c]], F32, name=f"total{c}")
+            nc.vector.tensor_tensor(total[:], terms[c][:, 0, :], terms[c][:, 1, :], ALU.add)
+            nc.sync.dma_start(out=out[:, starts[c] : starts[c] + STORES[c]], in_=total[:])
+
+        weigh(0, 0)
+        weigh(0, 1)
+        weigh(1, 0)
+        add_and_store(0)
+        weigh(2, 0)
+        weigh(1, 1)
+        weigh(2, 1)
+        add_and_store(1)
+        add_and_store(2)

@@ -25,9 +25,8 @@ ACT = mybir.ActivationFunctionType
 WIDE = 512
 BLOCKS = (T - WIDE) // P
 GATHER = 512
-CHUNK_PAIRS = ((0, 1), (2, 3), (4,), (5,))
-GPSIMD_PAIRS = CHUNK_PAIRS[0] + CHUNK_PAIRS[2]
-SCALAR_PAIRS = CHUNK_PAIRS[1] + CHUNK_PAIRS[3]
+W2_PARTS = (4, 4, 4)
+CHUNKS = (4, 4, 2, 1, 1)
 STORES = (448, 192, 128)
 WARM_PASSES = 4
 WARM_ROWS = 64
@@ -87,10 +86,10 @@ def tile_moe_sup_lin_relu2_kernel(tc, x_words, x_scales, w1_words, w1_scales, w2
             )
 
         offs_sb = keep.tile([P, SLOTS // PER_COLUMN], U16)
-        w2_raw = [keep.tile([P, 2, PACK * N], F32, name=f"w2_raw{g}") for g in range(PAIRS)]
-        for g in GPSIMD_PAIRS + SCALAR_PAIRS:
+        w2_raw = [keep.tile([P, 2, PACK * N], F32, name=f"w2_raw{g}", tag=f"w2_raw{g}", align_bytes=64) for g in range(PAIRS)]
+        for g in (0, 1, PAIRS - 1) + tuple(range(2, PAIRS - 1)):
             nc.sync.dma_start(out=w2_raw[g][:], in_=w2[2 * g : 2 * g + 2].rearrange("e (p j) n -> p e (j n)", j=PACK))
-            if g == GPSIMD_PAIRS[0]:
+            if g == 0:
                 nc.sync.dma_start(offs_sb[:], offs)
         pos1_sb = keep.tile([P, T // PER_COLUMN], U16)
         nc.sync.dma_start(pos1_sb[:], pos1)
@@ -127,7 +126,7 @@ def tile_moe_sup_lin_relu2_kernel(tc, x_words, x_scales, w1_words, w1_scales, w2
                 stop=(s == PASSES - 1),
             )
 
-        h_pairs = [keep.tile([P, 2 * T], BF16, align_bytes=64, name=f"h_pairs{u}") for u in range(2)]
+        h_pairs = [keep.tile([P, 2 * T], BF16, align_bytes=64, name=f"h_pairs{u}", tag=f"h_pairs{u}") for u in range(2)]
 
         def block_sums(u, k0, k1, tag):
             t0, t1 = WIDE + k0 * P, WIDE + k1 * P
@@ -179,72 +178,62 @@ def tile_moe_sup_lin_relu2_kernel(tc, x_words, x_scales, w1_words, w1_scales, w2
                 nc.vector.tensor_copy(out=gathered[k][:, u, :], in_=h_pairs[u][:].bitcast(U32).indirect(offs_sb[:, entries]))
 
         pair_width = 2 * N * PACK
-        gpsimd_bf = keep.tile([P, len(GPSIMD_PAIRS) * pair_width], BF16, align_bytes=64)
-        scalar_bf = keep.tile([P, len(SCALAR_PAIRS) * pair_width], BF16, align_bytes=64, tag="relu_wide1")
+        rounded = [keep.tile([P, 2 * pair_width], BF16, align_bytes=64, name=f"rounded{c}", tag=tag) for c, tag in enumerate(("rounded0", "rounded1", "relu_wide1"))]
 
-        def rounded(pairs_of):
-            tile, share = (gpsimd_bf, GPSIMD_PAIRS) if pairs_of[0] in GPSIMD_PAIRS else (scalar_bf, SCALAR_PAIRS)
-            first = share.index(pairs_of[0])
-            return tile[:, first * pair_width : (first + len(pairs_of)) * pair_width]
+        def pair_columns(g):
+            return rounded[g // 2][:, (g % 2) * pair_width : (g % 2 + 1) * pair_width]
 
-        for g in GPSIMD_PAIRS:
+        for g in range(PAIRS - 1):
             nc.gpsimd.tensor_scalar(
-                rounded((g,)).rearrange("p (e n j) -> p e n j", e=2, j=PACK),
+                pair_columns(g).rearrange("p (e n j) -> p e n j", e=2, j=PACK),
                 w2_raw[g][:].rearrange("p e (j n) -> p e n j", j=PACK),
                 1.0,
                 0.0,
                 ALU.mult,
                 ALU.add,
             )
+        nc.scalar.copy(
+            out=pair_columns(PAIRS - 1).rearrange("p (e c i j) -> p e c j i", e=2, i=4, j=PACK),
+            in_=w2_raw[PAIRS - 1][:].rearrange("p e (j c i) -> p e c j i", j=PACK, i=4),
+        )
 
-        def round_on_scalar(g):
+        woven = []
+        for k in range(SLOTS // GATHER):
+            woven.append(keep.tile([P, GATHER * PACK], BF16, align_bytes=64, name=f"woven{k}"))
             nc.scalar.copy(
-                out=rounded((g,)).rearrange("p (e c i j) -> p e c j i", e=2, i=4, j=PACK),
-                in_=w2_raw[g][:].rearrange("p e (j c i) -> p e c j i", j=PACK, i=4),
+                out=woven[k][:].bitcast(U32).rearrange("p (s u) -> p s u", u=2),
+                in_=gathered[k][:].rearrange("p u s -> p s u"),
             )
 
-        slot_h = []
-        for c, pairs_of in enumerate(CHUNK_PAIRS):
-            if c < len(SCALAR_PAIRS):
-                round_on_scalar(SCALAR_PAIRS[c])
-            width = 2 * len(pairs_of) * C
-            k, s0 = divmod(2 * pairs_of[0] * C, GATHER)
-            slot_h.append(keep.tile([P, width * PACK], BF16, align_bytes=64, name=f"slot_h{c}"))
-            nc.scalar.copy(
-                out=slot_h[c][:].bitcast(U32).rearrange("p (s u) -> p s u", u=2),
-                in_=gathered[k][:, :, s0 : s0 + width].rearrange("p u s -> p s u"),
-            )
-
-        w2_codes = keep.tile([P, E * N], U32, align_bytes=64, tag="gathered0")
         w2_bytes = keep.tile([P, E * N], U8, align_bytes=64)
-        y_banks = ("block0", "block1", "wide0", "wide1")
+        y_banks = ("block0", "block1", "wide0", "wide1", "blocks_of_half_1")
         y_sums = []
-        for c, pairs_of in enumerate(CHUNK_PAIRS):
-            e0, n = 2 * pairs_of[0], 2 * len(pairs_of)
-            nc.vector.quantize_mx(
-                out=w2_codes[:, e0 * N : (e0 + n) * N].bitcast(FP8X4),
-                scales=w2_bytes[:, e0 * N : (e0 + n) * N],
-                in_=rounded(pairs_of),
-            )
-            h_codes = keep.tile([P, n * C], U32, align_bytes=64, name=f"h_codes{c}")
+        e0 = 0
+        for c, n in enumerate(CHUNKS):
+            k, first = divmod(e0, 4)
+            if first == 0:
+                w2_codes = keep.tile([P, 4 * N], U32, align_bytes=64, name=f"w2_codes{k}", tag=f"gathered{k}")
+                nc.vector.quantize_mx(out=w2_codes[:].bitcast(FP8X4), scales=w2_bytes[:, e0 * N : (e0 + 4) * N], in_=rounded[k][:])
+                part_codes = keep.tile([P, 4 * C], U32, align_bytes=64, name=f"h_codes{k}", tag=f"w2_raw{min(2 * k + 1, PAIRS - 2)}")
+            h_codes = part_codes[:, first * C : (first + n) * C]
             h_bytes = keep.tile([P, n * C], U8, align_bytes=64, name=f"h_bytes{c}")
-            nc.vector.quantize_mx(out=h_codes[:].bitcast(FP8X4), scales=h_bytes[:], in_=slot_h[c][:])
+            nc.vector.quantize_mx(out=h_codes.bitcast(FP8X4), scales=h_bytes[:], in_=woven[k][:, first * C * PACK : (first + n) * C * PACK])
             y_sums.append(psum.tile([P, n * C], F32, name=f"y_sums{c}", tag=y_banks[c]))
             for m in range(n):
-                w_cols = slice((e0 + m) * N, (e0 + m + 1) * N)
                 slots = slice(m * C, (m + 1) * C)
                 nc.tensor.matmul_mx(
                     out=y_sums[c][:, slots],
-                    lhsT=w2_codes[:, w_cols].bitcast(FP8X4),
-                    lhsT_scale=w2_bytes[:, w_cols],
+                    lhsT=w2_codes[:, (first + m) * N : (first + m + 1) * N].bitcast(FP8X4),
+                    lhsT_scale=w2_bytes[:, (e0 + m) * N : (e0 + m + 1) * N],
                     rhs=h_codes[:, slots].bitcast(FP8X4),
                     rhs_scale=h_bytes[:, slots],
                     start=True,
                     stop=True,
                 )
+            e0 = e0 + n
         y = keep.tile([P, SLOTS], F32)
-        for c, pairs_of in enumerate(CHUNK_PAIRS):
-            nc.scalar.copy(out=y[:, 2 * pairs_of[0] * C : 2 * (pairs_of[-1] + 1) * C], in_=y_sums[c][:])
+        for c, n in enumerate(CHUNKS):
+            nc.scalar.copy(out=y[:, sum(CHUNKS[:c]) * C : sum(CHUNKS[: c + 1]) * C], in_=y_sums[c][:])
 
         pos_sb = (pos1_sb, pos2_sb)
         starts = [sum(STORES[:c]) for c in range(len(STORES))]

@@ -39,7 +39,8 @@ def tile_moe_sup_lin_relu2_kernel(tc, x_words, x_scales, w1_words, w1_scales, w2
         psum = ctx.enter_context(tc.psum_pool(name="psum", bufs=1))
 
         w1_raw = keep.tile([P, PASSES, 2 * H], U8, align_bytes=64)
-        w1_plane = keep.tile([P, PASSES, H], U8, align_bytes=64)
+        zeros = keep.tile([P, 2 * PACK * WIDE], U8, align_bytes=64)
+        w1_plane = zeros[:, : PASSES * H]
         x_plane = keep.tile([P, PASSES, T], U8, align_bytes=64)
         x_wide = [keep.tile([P, PACK * WIDE], U8, align_bytes=64, name=f"x_wide{s}") for s in range(PASSES)]
         x_block = [keep.tile([P, PASSES, PACK * P], U8, align_bytes=64, name=f"x_block{k}") for k in range(BLOCKS)]
@@ -48,7 +49,10 @@ def tile_moe_sup_lin_relu2_kernel(tc, x_words, x_scales, w1_words, w1_scales, w2
         w1_rows = keep.tile([P, PASSES * H // 4], I32)
         nc.vector.memset(x_plane[:].bitcast(I32), 0)
         nc.vector.memset(table_in[:], 0.0)
-        nc.vector.memset(w1_plane[:].bitcast(I32), 0)
+        nc.gpsimd.memset(zeros[:].bitcast(I32), 0)
+        zero_codes = keep.tile([P, WIDE], U32, align_bytes=64)
+        zero_bytes = keep.tile([P, WIDE], U8, align_bytes=64)
+        nc.vector.quantize_mx(out=zero_codes[:].bitcast(FP8X4), scales=zero_bytes[:], in_=zeros[:].bitcast(BF16))
 
         w1_scale_rows = w1_scales.rearrange("s (q r) i -> q r s i", r=4)
         for q in range(4):
@@ -71,23 +75,28 @@ def tile_moe_sup_lin_relu2_kernel(tc, x_words, x_scales, w1_words, w1_scales, w2
             nc.sync.dma_start(out=x_block[k][:].bitcast(I32), in_=x_rows[:, :, PACK * t0 : PACK * (t0 + P)].bitcast(I32))
         for q in range(4):
             rows = slice(32 * q, 32 * q + 4)
-            nc.vector.tensor_copy(out=w1_plane[rows].rearrange("p s i -> p (s i)").bitcast(I32), in_=w1_rows[rows, :])
+            nc.vector.tensor_copy(out=zeros[rows, : PASSES * H].bitcast(I32), in_=w1_rows[rows, :])
 
-        w1_codes = [keep.tile([P, PASSES, H], U8, align_bytes=64, name=f"w1_codes{u}") for u in range(2)]
-        w1_bytes = [keep.tile([P, PASSES, H // 2], U8, align_bytes=64, name=f"w1_bytes{u}") for u in range(2)]
-        for u in range(2):
+        plane_by_group = w1_plane.rearrange("p (s m j) -> p j s m", s=PASSES, j=PACK)
+        words_by_group = w1_raw[:].bitcast(U16).rearrange("p s (m j) -> p j s m", j=PACK)
+        w1_codes, w1_bytes = [[], []], [[], []]
+        for u, s0, s1 in [(0, s, s + 1) for s in range(PASSES)] + [(1, 0, PASSES)]:
+            codes = keep.tile([P, s1 - s0, H], U8, align_bytes=64, name=f"w1_codes{u}{s0}")
+            scales = keep.tile([P, s1 - s0, H // 2], U8, align_bytes=64, name=f"w1_bytes{u}{s0}")
             nc.vector.tensor_copy(
-                out=w1_bytes[u][:].rearrange("p s (b m) -> p b s m", b=2),
-                in_=w1_plane[:].rearrange("p s (m j) -> p j s m", j=PACK)[:, 2 * u : 2 * u + 2, :, :],
+                out=scales[:].rearrange("p s (b m) -> p b s m", b=2),
+                in_=plane_by_group[:, 2 * u : 2 * u + 2, s0:s1, :],
             )
             nc.vector.tensor_copy(
-                out=w1_codes[u][:].bitcast(U16).rearrange("p s (b m) -> p b s m", b=2),
-                in_=w1_raw[:].bitcast(U16).rearrange("p s (m j) -> p j s m", j=PACK)[:, 2 * u : 2 * u + 2, :, :],
+                out=codes[:].bitcast(U16).rearrange("p s (b m) -> p b s m", b=2),
+                in_=words_by_group[:, 2 * u : 2 * u + 2, s0:s1, :],
             )
+            w1_codes[u].extend(codes[:, s, :] for s in range(s1 - s0))
+            w1_bytes[u].extend(scales[:, s, :] for s in range(s1 - s0))
 
         offs_sb = keep.tile([P, SLOTS // PER_COLUMN], U16)
         w2_raw = [keep.tile([P, 2, PACK * N], F32, name=f"w2_raw{g}", tag=f"w2_raw{g}", align_bytes=64) for g in range(PAIRS)]
-        for g in (0, 1, PAIRS - 1) + tuple(range(2, PAIRS - 1)):
+        for g in range(PAIRS):
             nc.sync.dma_start(out=w2_raw[g][:], in_=w2[2 * g : 2 * g + 2].rearrange("e (p j) n -> p e (j n)", j=PACK))
             if g == 0:
                 nc.sync.dma_start(offs_sb[:], offs)
@@ -98,11 +107,6 @@ def tile_moe_sup_lin_relu2_kernel(tc, x_words, x_scales, w1_words, w1_scales, w2
         gate_sb = keep.tile([P, 2, T], F32)
         nc.sync.dma_start(out=gate_sb[:], in_=gate.rearrange("r p t -> p r t"))
 
-        zeros = keep.tile([P, PACK * WIDE], BF16, align_bytes=64)
-        zero_codes = keep.tile([P, WIDE], U32, align_bytes=64)
-        zero_bytes = keep.tile([P, WIDE], U8, align_bytes=64)
-        nc.gpsimd.memset(zeros[:].bitcast(I32), 0)
-        nc.vector.quantize_mx(out=zero_codes[:].bitcast(FP8X4), scales=zero_bytes[:], in_=zeros[:])
         idle = psum.tile([P, WIDE], F32, tag="blocks_of_half_1")
         for w in range(WARM_PASSES):
             nc.tensor.matmul_mx(
@@ -118,8 +122,8 @@ def tile_moe_sup_lin_relu2_kernel(tc, x_words, x_scales, w1_words, w1_scales, w2
         def first_layer(acc, u, b, s, words, t0, t1):
             nc.tensor.matmul_mx(
                 out=acc,
-                lhsT=w1_codes[u][:, s, 2 * P * b : 2 * P * (b + 1)].bitcast(FP4X4),
-                lhsT_scale=w1_bytes[u][:, s, P * b : P * (b + 1)],
+                lhsT=w1_codes[u][s][:, 2 * P * b : 2 * P * (b + 1)].bitcast(FP4X4),
+                lhsT_scale=w1_bytes[u][s][:, P * b : P * (b + 1)],
                 rhs=words.bitcast(FP8X4),
                 rhs_scale=x_plane[:, s, t0:t1],
                 start=(s == 0),
@@ -136,17 +140,13 @@ def tile_moe_sup_lin_relu2_kernel(tc, x_words, x_scales, w1_words, w1_scales, w2
                     t = WIDE + k * P
                     for s in range(PASSES):
                         first_layer(sums[:, b, t - t0 : t - t0 + P], u, b, s, x_block[k][:, s, :], t, t + P)
-            relu = keep.tile([P, t1 - t0, 2], F32, name=f"relu{u}{k0}", align_bytes=64)
+            relu = keep.tile([P, t1 - t0, 2], F32, name=f"relu{u}{k0}", tag=f"relu{u}{k0}", align_bytes=64)
             return sums[:].rearrange("p b t -> p t b"), relu[:], h_pairs[u][:, 2 * t0 : 2 * t1].rearrange("p (t b) -> p t b", b=2)
 
         relu_wide = [keep.tile([P, 2, WIDE], F32, name=f"relu_wide{u}", tag=f"relu_wide{u}", align_bytes=64) for u in range(2)]
 
-        def square_wide(u):
-            nc.scalar.activation(
-                h_pairs[u][:, : 2 * WIDE].rearrange("p (t b) -> p t b", b=2),
-                relu_wide[u][:].rearrange("p b t -> p t b"),
-                ACT.Square,
-            )
+        def wide_views(u, t0, t1):
+            return relu_wide[u][:, :, t0:t1].rearrange("p b t -> p t b"), h_pairs[u][:, 2 * t0 : 2 * t1].rearrange("p (t b) -> p t b", b=2)
 
         wide = [psum.tile([P, WIDE], F32, name=f"wide0{b}", tag=f"wide{b}") for b in range(2)]
         for s in range(PASSES):
@@ -154,22 +154,26 @@ def tile_moe_sup_lin_relu2_kernel(tc, x_words, x_scales, w1_words, w1_scales, w2
                 first_layer(wide[b][:], 0, b, s, x_wide[s][:], 0, WIDE)
         nc.vector.tensor_scalar_max(relu_wide[0][:, 0, :], wide[0][:], 0.0)
         nc.scalar.activation(relu_wide[0][:, 1, :], wide[1][:], ACT.Relu)
-        square_wide(0)
+        relu, pairs = wide_views(0, 0, WIDE)
+        nc.scalar.activation(pairs, relu, ACT.Square)
         blocks = [block_sums(0, k, k + 1, f"block{k}") for k in range(BLOCKS)]
         for sums, relu, pairs in blocks:
             nc.vector.tensor_scalar_max(relu, sums, 0.0)
-        for sums, relu, pairs in blocks:
-            nc.vector.tensor_tensor(pairs, sums, relu, ALU.mult)
+        sums, relu, pairs = blocks[0]
+        nc.gpsimd.tensor_tensor(pairs, relu, relu, ALU.mult)
+        sums, relu, pairs = blocks[1]
+        nc.vector.tensor_tensor(pairs, sums, relu, ALU.mult)
 
         sums, relu, pairs = block_sums(1, 0, BLOCKS, "blocks_of_half_1")
         nc.scalar.activation(relu, sums, ACT.Relu)
-        nc.scalar.activation(pairs, relu, ACT.Square)
+        nc.gpsimd.tensor_tensor(pairs, relu, relu, ALU.mult)
         for b in range(2):
             group = psum.tile([P, WIDE], F32, name=f"wide1{b}", tag=f"wide{b}")
             for s in range(PASSES):
                 first_layer(group[:], 1, b, s, x_wide[s][:], 0, WIDE)
             nc.scalar.activation(relu_wide[1][:, b, :], group[:], ACT.Relu)
-        square_wide(1)
+        relu, pairs = wide_views(1, 0, WIDE)
+        nc.scalar.activation(pairs, relu, ACT.Square)
 
         gathered = [keep.tile([P, 2, GATHER], U32, name=f"gathered{k}", tag=f"gathered{k}", align_bytes=64) for k in range(SLOTS // GATHER)]
         for u in range(2):
@@ -178,12 +182,12 @@ def tile_moe_sup_lin_relu2_kernel(tc, x_words, x_scales, w1_words, w1_scales, w2
                 nc.vector.tensor_copy(out=gathered[k][:, u, :], in_=h_pairs[u][:].bitcast(U32).indirect(offs_sb[:, entries]))
 
         pair_width = 2 * N * PACK
-        rounded = [keep.tile([P, 2 * pair_width], BF16, align_bytes=64, name=f"rounded{c}", tag=tag) for c, tag in enumerate(("rounded0", "rounded1", "relu_wide1"))]
+        rounded = [keep.tile([P, 2 * pair_width], BF16, align_bytes=64, name=f"rounded{c}", tag=tag) for c, tag in enumerate(("relu00", "relu_wide1", "rounded2"))]
 
         def pair_columns(g):
             return rounded[g // 2][:, (g % 2) * pair_width : (g % 2 + 1) * pair_width]
 
-        for g in range(PAIRS - 1):
+        for g in (0, 1, 4, 5):
             nc.gpsimd.tensor_scalar(
                 pair_columns(g).rearrange("p (e n j) -> p e n j", e=2, j=PACK),
                 w2_raw[g][:].rearrange("p e (j n) -> p e n j", j=PACK),
@@ -192,10 +196,11 @@ def tile_moe_sup_lin_relu2_kernel(tc, x_words, x_scales, w1_words, w1_scales, w2
                 ALU.mult,
                 ALU.add,
             )
-        nc.scalar.copy(
-            out=pair_columns(PAIRS - 1).rearrange("p (e c i j) -> p e c j i", e=2, i=4, j=PACK),
-            in_=w2_raw[PAIRS - 1][:].rearrange("p e (j c i) -> p e c j i", j=PACK, i=4),
-        )
+        for g in (2, 3):
+            nc.scalar.copy(
+                out=pair_columns(g).rearrange("p (e c i j) -> p e c j i", e=2, i=4, j=PACK),
+                in_=w2_raw[g][:].rearrange("p e (j c i) -> p e c j i", j=PACK, i=4),
+            )
 
         woven = []
         for k in range(SLOTS // GATHER):
@@ -212,9 +217,9 @@ def tile_moe_sup_lin_relu2_kernel(tc, x_words, x_scales, w1_words, w1_scales, w2
         for c, n in enumerate(CHUNKS):
             k, first = divmod(e0, 4)
             if first == 0:
-                w2_codes = keep.tile([P, 4 * N], U32, align_bytes=64, name=f"w2_codes{k}", tag=f"gathered{k}")
+                w2_codes = keep.tile([P, 4 * N], U32, align_bytes=64, name=f"w2_codes{k}", tag=("w2_raw3", "gathered1", "gathered2")[k])
                 nc.vector.quantize_mx(out=w2_codes[:].bitcast(FP8X4), scales=w2_bytes[:, e0 * N : (e0 + 4) * N], in_=rounded[k][:])
-                part_codes = keep.tile([P, 4 * C], U32, align_bytes=64, name=f"h_codes{k}", tag=f"w2_raw{min(2 * k + 1, PAIRS - 2)}")
+                part_codes = keep.tile([P, 4 * C], U32, align_bytes=64, name=f"h_codes{k}", tag=("h_codes0", "h_codes1", "w2_raw5")[k])
             h_codes = part_codes[:, first * C : (first + n) * C]
             h_bytes = keep.tile([P, n * C], U8, align_bytes=64, name=f"h_bytes{c}")
             nc.vector.quantize_mx(out=h_codes.bitcast(FP8X4), scales=h_bytes[:], in_=woven[k][:, first * C * PACK : (first + n) * C * PACK])

@@ -43,7 +43,9 @@ def tile_moe_sup_lin_relu2_kernel(tc, x_words, x_scales, w1_words, w1_scales, w2
         w1_plane = zeros[:, : PASSES * H]
         x_plane = keep.tile([P, PASSES, T], U8, align_bytes=64)
         x_wide = [keep.tile([P, PACK * WIDE], U8, align_bytes=64, name=f"x_wide{s}") for s in range(PASSES)]
-        x_block = [keep.tile([P, PASSES, PACK * P], U8, align_bytes=64, name=f"x_block{k}") for k in range(BLOCKS)]
+        x_early = keep.tile([P, PASSES - 1, PACK * (T - WIDE)], U8, align_bytes=64)
+        x_late = keep.tile([P, PACK * (T - WIDE)], U8, align_bytes=64)
+        x_narrow = [x_early[:, s, :] for s in range(PASSES - 1)] + [x_late[:]]
         table_in = keep.tile([P, 8], F32)
         table_out = keep.tile([P, 8], F32)
         w1_rows = keep.tile([P, PASSES * H // 4], I32)
@@ -70,9 +72,8 @@ def tile_moe_sup_lin_relu2_kernel(tc, x_words, x_scales, w1_words, w1_scales, w2
             nc.sync.dma_start(out=x_plane[r:P:32, :, :].bitcast(I32), in_=x_scale_rows[r].bitcast(I32))
         for s in range(1, PASSES):
             nc.sync.dma_start(out=x_wide[s][:].bitcast(I32), in_=x_rows[:, s, : PACK * WIDE].bitcast(I32))
-        for k in range(BLOCKS):
-            t0 = WIDE + k * P
-            nc.sync.dma_start(out=x_block[k][:].bitcast(I32), in_=x_rows[:, :, PACK * t0 : PACK * (t0 + P)].bitcast(I32))
+        nc.sync.dma_start(out=x_early[:].bitcast(I32), in_=x_rows[:, : PASSES - 1, PACK * WIDE :].bitcast(I32))
+        nc.sync.dma_start(out=x_late[:].bitcast(I32), in_=x_rows[:, PASSES - 1, PACK * WIDE :].bitcast(I32))
         for q in range(4):
             rows = slice(32 * q, 32 * q + 4)
             nc.vector.tensor_copy(out=zeros[rows, : PASSES * H].bitcast(I32), in_=w1_rows[rows, :])
@@ -139,7 +140,7 @@ def tile_moe_sup_lin_relu2_kernel(tc, x_words, x_scales, w1_words, w1_scales, w2
                 for k in range(k0, k1):
                     t = WIDE + k * P
                     for s in range(PASSES):
-                        first_layer(sums[:, b, t - t0 : t - t0 + P], u, b, s, x_block[k][:, s, :], t, t + P)
+                        first_layer(sums[:, b, t - t0 : t - t0 + P], u, b, s, x_narrow[s][:, PACK * k * P : PACK * (k + 1) * P], t, t + P)
             relu = keep.tile([P, t1 - t0, 2], F32, name=f"relu{u}{k0}", tag=f"relu{u}{k0}", align_bytes=64)
             return sums[:].rearrange("p b t -> p t b"), relu[:], h_pairs[u][:, 2 * t0 : 2 * t1].rearrange("p (t b) -> p t b", b=2)
 
@@ -156,19 +157,24 @@ def tile_moe_sup_lin_relu2_kernel(tc, x_words, x_scales, w1_words, w1_scales, w2
         nc.scalar.activation(relu_wide[0][:, 1, :], wide[1][:], ACT.Relu)
         relu, pairs = wide_views(0, 0, WIDE)
         nc.scalar.activation(pairs, relu, ACT.Square)
-        blocks = [block_sums(0, k, k + 1, f"block{k}") for k in range(BLOCKS)]
-        for sums, relu, pairs in blocks:
-            nc.vector.tensor_scalar_max(relu, sums, 0.0)
-        sums, relu, pairs = blocks[0]
-        nc.gpsimd.tensor_tensor(pairs, relu, relu, ALU.mult)
-        sums, relu, pairs = blocks[1]
-        nc.vector.tensor_tensor(pairs, sums, relu, ALU.mult)
+        relu_block = [keep.tile([P, 2, P], F32, name=f"relu_block{k}", tag=f"relu_block{k}", align_bytes=64) for k in range(BLOCKS)]
+        for k in range(BLOCKS):
+            t = WIDE + k * P
+            for b in range(2):
+                sums = psum.tile([P, P], F32, name=f"block{k}{b}", tag=f"block{k}{b}")
+                for s in range(PASSES):
+                    first_layer(sums[:], 0, b, s, x_narrow[s][:, PACK * k * P : PACK * (k + 1) * P], t, t + P)
+                nc.vector.tensor_scalar_max(relu_block[k][:, b, :], sums[:], 0.0)
+        for k, engine in enumerate((nc.gpsimd, nc.vector)):
+            t = WIDE + k * P
+            relu = relu_block[k][:].rearrange("p b t -> p t b")
+            engine.tensor_tensor(h_pairs[0][:, 2 * t : 2 * (t + P)].rearrange("p (t b) -> p t b", b=2), relu, relu, ALU.mult)
 
-        sums, relu, pairs = block_sums(1, 0, BLOCKS, "blocks_of_half_1")
+        sums, relu, pairs = block_sums(1, 0, BLOCKS, "wide0")
         nc.scalar.activation(relu, sums, ACT.Relu)
         nc.gpsimd.tensor_tensor(pairs, relu, relu, ALU.mult)
         for b in range(2):
-            group = psum.tile([P, WIDE], F32, name=f"wide1{b}", tag=f"wide{b}")
+            group = psum.tile([P, WIDE], F32, name=f"wide1{b}", tag=("wide1", "block00")[b])
             for s in range(PASSES):
                 first_layer(group[:], 1, b, s, x_wide[s][:], 0, WIDE)
             nc.scalar.activation(relu_wide[1][:, b, :], group[:], ACT.Relu)
@@ -182,7 +188,7 @@ def tile_moe_sup_lin_relu2_kernel(tc, x_words, x_scales, w1_words, w1_scales, w2
                 nc.vector.tensor_copy(out=gathered[k][:, u, :], in_=h_pairs[u][:].bitcast(U32).indirect(offs_sb[:, entries]))
 
         pair_width = 2 * N * PACK
-        rounded = [keep.tile([P, 2 * pair_width], BF16, align_bytes=64, name=f"rounded{c}", tag=tag) for c, tag in enumerate(("relu00", "relu_wide1", "rounded2"))]
+        rounded = [keep.tile([P, 2 * pair_width], BF16, align_bytes=64, name=f"rounded{c}", tag=tag) for c, tag in enumerate(("relu_block0", "relu_wide1", "rounded2"))]
 
         def pair_columns(g):
             return rounded[g // 2][:, (g % 2) * pair_width : (g % 2 + 1) * pair_width]
@@ -211,7 +217,7 @@ def tile_moe_sup_lin_relu2_kernel(tc, x_words, x_scales, w1_words, w1_scales, w2
             )
 
         w2_bytes = keep.tile([P, E * N], U8, align_bytes=64)
-        y_banks = ("block0", "block1", "wide0", "wide1", "blocks_of_half_1")
+        y_banks = ("block01", "block10", "block11", "wide0", "blocks_of_half_1")
         y_sums = []
         e0 = 0
         for c, n in enumerate(CHUNKS):

@@ -165,14 +165,14 @@ def tile_moe_sup_lin_relu2_kernel(tc, x_words, x_scales, w1_words, w1_scales, w2
                 for s in range(PASSES):
                     first_layer(sums[:], 0, b, s, x_narrow[s][:, PACK * k * P : PACK * (k + 1) * P], t, t + P)
                 nc.vector.tensor_scalar_max(relu_block[k][:, b, :], sums[:], 0.0)
-        for k, engine in enumerate((nc.gpsimd, nc.vector)):
+        for k in range(BLOCKS):
             t = WIDE + k * P
             relu = relu_block[k][:].rearrange("p b t -> p t b")
-            engine.tensor_tensor(h_pairs[0][:, 2 * t : 2 * (t + P)].rearrange("p (t b) -> p t b", b=2), relu, relu, ALU.mult)
+            nc.vector.tensor_tensor(h_pairs[0][:, 2 * t : 2 * (t + P)].rearrange("p (t b) -> p t b", b=2), relu, relu, ALU.mult)
 
         sums, relu, pairs = block_sums(1, 0, BLOCKS, "wide0")
         nc.scalar.activation(relu, sums, ACT.Relu)
-        nc.gpsimd.tensor_tensor(pairs, relu, relu, ALU.mult)
+        nc.scalar.activation(pairs, relu, ACT.Square)
         for b in range(2):
             group = psum.tile([P, WIDE], F32, name=f"wide1{b}", tag=("wide1", "block00")[b])
             for s in range(PASSES):
@@ -188,7 +188,7 @@ def tile_moe_sup_lin_relu2_kernel(tc, x_words, x_scales, w1_words, w1_scales, w2
                 nc.vector.tensor_copy(out=gathered[k][:, u, :], in_=h_pairs[u][:].bitcast(U32).indirect(offs_sb[:, entries]))
 
         pair_width = 2 * N * PACK
-        rounded = [keep.tile([P, 2 * pair_width], BF16, align_bytes=64, name=f"rounded{c}", tag=tag) for c, tag in enumerate(("relu_block0", "relu_wide1", "rounded2"))]
+        rounded = [keep.tile([P, 2 * pair_width], BF16, align_bytes=64, name=f"rounded{c}", tag=tag) for c, tag in enumerate(("relu_block1", "relu_wide1", "rounded2"))]
 
         def pair_columns(g):
             return rounded[g // 2][:, (g % 2) * pair_width : (g % 2 + 1) * pair_width]
@@ -223,7 +223,7 @@ def tile_moe_sup_lin_relu2_kernel(tc, x_words, x_scales, w1_words, w1_scales, w2
         for c, n in enumerate(CHUNKS):
             k, first = divmod(e0, 4)
             if first == 0:
-                w2_codes = keep.tile([P, 4 * N], U32, align_bytes=64, name=f"w2_codes{k}", tag=("w2_raw3", "gathered1", "gathered2")[k])
+                w2_codes = keep.tile([P, 4 * N], U32, align_bytes=64, name=f"w2_codes{k}", tag=("w2_raw3", "w2_codes1", "gathered1")[k])
                 nc.vector.quantize_mx(out=w2_codes[:].bitcast(FP8X4), scales=w2_bytes[:, e0 * N : (e0 + 4) * N], in_=rounded[k][:])
                 part_codes = keep.tile([P, 4 * C], U32, align_bytes=64, name=f"h_codes{k}", tag=("h_codes0", "h_codes1", "w2_raw5")[k])
             h_codes = part_codes[:, first * C : (first + n) * C]

@@ -96,11 +96,11 @@ def tile_moe_sup_lin_relu2_kernel(tc, x_words, x_scales, w1_words, w1_scales, w2
             w1_bytes[u].extend(scales[:, s, :] for s in range(s1 - s0))
 
         offs_sb = keep.tile([P, SLOTS // PER_COLUMN], U16)
-        w2_raw = [keep.tile([P, 2, PACK * N], F32, name=f"w2_raw{g}", tag=f"w2_raw{g}", align_bytes=64) for g in range(PAIRS)]
-        for g in range(PAIRS):
-            nc.sync.dma_start(out=w2_raw[g][:], in_=w2[2 * g : 2 * g + 2].rearrange("e (p j) n -> p e (j n)", j=PACK))
-            if g == 0:
-                nc.sync.dma_start(offs_sb[:], offs)
+        nc.sync.dma_start(offs_sb[:], offs)
+        w2_raw = {}
+        for e0, e1 in ((0, 2), (2, 4), (8, 11), (4, 6), (6, 8), (11, 12)):
+            w2_raw[e0] = keep.tile([P, e1 - e0, PACK * N], F32, name=f"w2_raw{e0}", tag=f"w2_raw{e0}", align_bytes=64)
+            nc.sync.dma_start(out=w2_raw[e0][:], in_=w2[e0:e1].rearrange("e (p j) n -> p e (j n)", j=PACK))
         pos1_sb = keep.tile([P, T // PER_COLUMN], U16)
         nc.sync.dma_start(pos1_sb[:], pos1)
         pos2_sb = keep.tile([P, T // PER_COLUMN], U16)
@@ -108,7 +108,7 @@ def tile_moe_sup_lin_relu2_kernel(tc, x_words, x_scales, w1_words, w1_scales, w2
         gate_sb = keep.tile([P, 2, T], F32)
         nc.sync.dma_start(out=gate_sb[:], in_=gate.rearrange("r p t -> p r t"))
 
-        idle = psum.tile([P, WIDE], F32, tag="blocks_of_half_1")
+        idle = psum.tile([P, WIDE], F32, tag="warm_up")
         for w in range(WARM_PASSES):
             nc.tensor.matmul_mx(
                 out=idle[:WARM_ROWS, :],
@@ -120,29 +120,18 @@ def tile_moe_sup_lin_relu2_kernel(tc, x_words, x_scales, w1_words, w1_scales, w2
                 stop=True,
             )
 
-        def first_layer(acc, u, b, s, words, t0, t1):
+        def first_layer(acc, u, b, s, words, t0, t1, first=0):
             nc.tensor.matmul_mx(
                 out=acc,
                 lhsT=w1_codes[u][s][:, 2 * P * b : 2 * P * (b + 1)].bitcast(FP4X4),
                 lhsT_scale=w1_bytes[u][s][:, P * b : P * (b + 1)],
                 rhs=words.bitcast(FP8X4),
                 rhs_scale=x_plane[:, s, t0:t1],
-                start=(s == 0),
-                stop=(s == PASSES - 1),
+                start=(s == first),
+                stop=(s == (first - 1) % PASSES),
             )
 
         h_pairs = [keep.tile([P, 2 * T], BF16, align_bytes=64, name=f"h_pairs{u}", tag=f"h_pairs{u}") for u in range(2)]
-
-        def block_sums(u, k0, k1, tag):
-            t0, t1 = WIDE + k0 * P, WIDE + k1 * P
-            sums = psum.tile([P, 2, t1 - t0], F32, name=f"sums{u}{k0}", tag=tag)
-            for b in range(2):
-                for k in range(k0, k1):
-                    t = WIDE + k * P
-                    for s in range(PASSES):
-                        first_layer(sums[:, b, t - t0 : t - t0 + P], u, b, s, x_narrow[s][:, PACK * k * P : PACK * (k + 1) * P], t, t + P)
-            relu = keep.tile([P, t1 - t0, 2], F32, name=f"relu{u}{k0}", tag=f"relu{u}{k0}", align_bytes=64)
-            return sums[:].rearrange("p b t -> p t b"), relu[:], h_pairs[u][:, 2 * t0 : 2 * t1].rearrange("p (t b) -> p t b", b=2)
 
         relu_wide = [keep.tile([P, 2, WIDE], F32, name=f"relu_wide{u}", tag=f"relu_wide{u}", align_bytes=64) for u in range(2)]
 
@@ -154,32 +143,45 @@ def tile_moe_sup_lin_relu2_kernel(tc, x_words, x_scales, w1_words, w1_scales, w2
             for b in range(2):
                 first_layer(wide[b][:], 0, b, s, x_wide[s][:], 0, WIDE)
         nc.vector.tensor_scalar_max(relu_wide[0][:, 0, :], wide[0][:], 0.0)
-        nc.scalar.activation(relu_wide[0][:, 1, :], wide[1][:], ACT.Relu)
-        relu, pairs = wide_views(0, 0, WIDE)
-        nc.scalar.activation(pairs, relu, ACT.Square)
+        for t0 in range(0, WIDE, WIDE // 2):
+            nc.scalar.activation(relu_wide[0][:, 1, t0 : t0 + WIDE // 2], wide[1][:, t0 : t0 + WIDE // 2], ACT.Relu)
+        for t0 in range(0, WIDE, WIDE // 2):
+            relu, pairs = wide_views(0, t0, t0 + WIDE // 2)
+            nc.scalar.activation(pairs, relu, ACT.Square)
         relu_block = [keep.tile([P, 2, P], F32, name=f"relu_block{k}", tag=f"relu_block{k}", align_bytes=64) for k in range(BLOCKS)]
         for k in range(BLOCKS):
             t = WIDE + k * P
+            sums = psum.tile([P, 2, P], F32, name=f"block{k}", tag=f"block{k}")
             for b in range(2):
-                sums = psum.tile([P, P], F32, name=f"block{k}{b}", tag=f"block{k}{b}")
                 for s in range(PASSES):
-                    first_layer(sums[:], 0, b, s, x_narrow[s][:, PACK * k * P : PACK * (k + 1) * P], t, t + P)
-                nc.vector.tensor_scalar_max(relu_block[k][:, b, :], sums[:], 0.0)
+                    first_layer(sums[:, b, :], 0, b, s, x_narrow[s][:, PACK * k * P : PACK * (k + 1) * P], t, t + P)
+            nc.vector.tensor_scalar_max(relu_block[k][:], sums[:], 0.0)
         for k in range(BLOCKS):
             t = WIDE + k * P
             relu = relu_block[k][:].rearrange("p b t -> p t b")
             nc.vector.tensor_tensor(h_pairs[0][:, 2 * t : 2 * (t + P)].rearrange("p (t b) -> p t b", b=2), relu, relu, ALU.mult)
 
-        sums, relu, pairs = block_sums(1, 0, BLOCKS, "wide0")
-        nc.scalar.activation(relu, sums, ACT.Relu)
+        def block_relu(k, tag):
+            t = WIDE + k * P
+            sums = psum.tile([P, 2, P], F32, name=f"sums{k}", tag=tag)
+            for b in range(2):
+                for s in (2, 0, 1):
+                    first_layer(sums[:, b, :], 1, b, s, x_narrow[s][:, PACK * k * P : PACK * (k + 1) * P], t, t + P, first=2)
+            relu = keep.tile([P, P, 2], F32, name=f"relu1{k}", align_bytes=64)
+            nc.scalar.activation(relu[:], sums[:].rearrange("p b t -> p t b"), ACT.Relu)
+            return relu[:], h_pairs[1][:, 2 * t : 2 * (t + P)].rearrange("p (t b) -> p t b", b=2)
+
+        relu, pairs = block_relu(0, "warm_up")
         nc.scalar.activation(pairs, relu, ACT.Square)
         for b in range(2):
-            group = psum.tile([P, WIDE], F32, name=f"wide1{b}", tag=("wide1", "block00")[b])
+            group = psum.tile([P, WIDE], F32, name=f"wide1{b}", tag=f"block{b}")
             for s in range(PASSES):
                 first_layer(group[:], 1, b, s, x_wide[s][:], 0, WIDE)
             nc.scalar.activation(relu_wide[1][:, b, :], group[:], ACT.Relu)
+        last_relu, last_pairs = block_relu(1, "spare")
         relu, pairs = wide_views(1, 0, WIDE)
         nc.scalar.activation(pairs, relu, ACT.Square)
+        nc.scalar.activation(last_pairs, last_relu, ACT.Square)
 
         gathered = [keep.tile([P, 2, GATHER], U32, name=f"gathered{k}", tag=f"gathered{k}", align_bytes=64) for k in range(SLOTS // GATHER)]
         for u in range(2):
@@ -188,25 +190,24 @@ def tile_moe_sup_lin_relu2_kernel(tc, x_words, x_scales, w1_words, w1_scales, w2
                 nc.vector.tensor_copy(out=gathered[k][:, u, :], in_=h_pairs[u][:].bitcast(U32).indirect(offs_sb[:, entries]))
 
         pair_width = 2 * N * PACK
-        rounded = [keep.tile([P, 2 * pair_width], BF16, align_bytes=64, name=f"rounded{c}", tag=tag) for c, tag in enumerate(("relu_block1", "relu_wide1", "rounded2"))]
+        rounded = [keep.tile([P, 2 * pair_width], BF16, align_bytes=64, name=f"rounded{c}", tag=tag) for c, tag in enumerate(("relu_block1", "relu_block1", "relu_wide1"))]
 
         def pair_columns(g):
             return rounded[g // 2][:, (g % 2) * pair_width : (g % 2 + 1) * pair_width]
 
-        for g in (0, 1, 4, 5):
+        for g in (0, 1, 2, 3):
             nc.gpsimd.tensor_scalar(
                 pair_columns(g).rearrange("p (e n j) -> p e n j", e=2, j=PACK),
-                w2_raw[g][:].rearrange("p e (j n) -> p e n j", j=PACK),
+                w2_raw[2 * g][:].rearrange("p e (j n) -> p e n j", j=PACK),
                 1.0,
                 0.0,
                 ALU.mult,
                 ALU.add,
             )
-        for g in (2, 3):
-            nc.scalar.copy(
-                out=pair_columns(g).rearrange("p (e c i j) -> p e c j i", e=2, i=4, j=PACK),
-                in_=w2_raw[g][:].rearrange("p e (j c i) -> p e c j i", j=PACK, i=4),
-            )
+        nc.scalar.copy(
+            out=rounded[2][:, : 3 * N * PACK].rearrange("p (e c i j) -> p e c j i", e=3, i=4, j=PACK),
+            in_=w2_raw[8][:].rearrange("p e (j c i) -> p e c j i", j=PACK, i=4),
+        )
 
         woven = []
         for k in range(SLOTS // GATHER):
@@ -216,25 +217,38 @@ def tile_moe_sup_lin_relu2_kernel(tc, x_words, x_scales, w1_words, w1_scales, w2
                 in_=gathered[k][:].rearrange("p u s -> p s u"),
             )
 
+        nc.scalar.copy(
+            out=rounded[2][:, 3 * N * PACK :].rearrange("p (c i j) -> p c j i", i=4, j=PACK),
+            in_=w2_raw[11][:, 0, :].rearrange("p (j c i) -> p c j i", j=PACK, i=4),
+        )
+
         w2_bytes = keep.tile([P, E * N], U8, align_bytes=64)
-        y_banks = ("block01", "block10", "block11", "wide0", "blocks_of_half_1")
+        y_banks = ("wide0", "wide1", "y2", "y3", "warm_up")
+        w2_tags = ("w2_codes0", "w2_codes1", "gathered1", "gathered2", "w2_codes4")
         y_sums = []
         e0 = 0
         for c, n in enumerate(CHUNKS):
             k, first = divmod(e0, 4)
-            if first == 0:
-                w2_codes = keep.tile([P, 4 * N], U32, align_bytes=64, name=f"w2_codes{k}", tag=("w2_raw3", "w2_codes1", "gathered1")[k])
-                nc.vector.quantize_mx(out=w2_codes[:].bitcast(FP8X4), scales=w2_bytes[:, e0 * N : (e0 + 4) * N], in_=rounded[k][:])
-                part_codes = keep.tile([P, 4 * C], U32, align_bytes=64, name=f"h_codes{k}", tag=("h_codes0", "h_codes1", "w2_raw5")[k])
-            h_codes = part_codes[:, first * C : (first + n) * C]
-            h_bytes = keep.tile([P, n * C], U8, align_bytes=64, name=f"h_bytes{c}")
-            nc.vector.quantize_mx(out=h_codes.bitcast(FP8X4), scales=h_bytes[:], in_=woven[k][:, first * C * PACK : (first + n) * C * PACK])
+            if first == 0 and c == 2:
+                h_codes = keep.tile([P, 4 * C], U32, align_bytes=64, name=f"h_codes{k}")
+                h_bytes = keep.tile([P, 4 * C], U8, align_bytes=64, name=f"h_bytes{k}")
+                nc.vector.quantize_mx(out=h_codes[:].bitcast(FP8X4), scales=h_bytes[:], in_=woven[k][:])
+            w2_codes = keep.tile([P, n * N], U32, align_bytes=64, name=f"w2_codes{c}", tag=w2_tags[c])
+            nc.vector.quantize_mx(
+                out=w2_codes[:].bitcast(FP8X4),
+                scales=w2_bytes[:, e0 * N : (e0 + n) * N],
+                in_=rounded[k][:, first * N * PACK : (first + n) * N * PACK],
+            )
+            if first == 0 and c < 2:
+                h_codes = keep.tile([P, 4 * C], U32, align_bytes=64, name=f"h_codes{k}")
+                h_bytes = keep.tile([P, 4 * C], U8, align_bytes=64, name=f"h_bytes{k}")
+                nc.vector.quantize_mx(out=h_codes[:].bitcast(FP8X4), scales=h_bytes[:], in_=woven[k][:])
             y_sums.append(psum.tile([P, n * C], F32, name=f"y_sums{c}", tag=y_banks[c]))
             for m in range(n):
-                slots = slice(m * C, (m + 1) * C)
+                slots = slice((first + m) * C, (first + m + 1) * C)
                 nc.tensor.matmul_mx(
-                    out=y_sums[c][:, slots],
-                    lhsT=w2_codes[:, (first + m) * N : (first + m + 1) * N].bitcast(FP8X4),
+                    out=y_sums[c][:, m * C : (m + 1) * C],
+                    lhsT=w2_codes[:, m * N : (m + 1) * N].bitcast(FP8X4),
                     lhsT_scale=w2_bytes[:, (e0 + m) * N : (e0 + m + 1) * N],
                     rhs=h_codes[:, slots].bitcast(FP8X4),
                     rhs_scale=h_bytes[:, slots],
@@ -242,9 +256,12 @@ def tile_moe_sup_lin_relu2_kernel(tc, x_words, x_scales, w1_words, w1_scales, w2
                     stop=True,
                 )
             e0 = e0 + n
-        y = keep.tile([P, SLOTS], F32)
+        y = keep.tile([P, SLOTS], F32, tag="w2_raw11", align_bytes=64)
         for c, n in enumerate(CHUNKS):
-            nc.scalar.copy(out=y[:, sum(CHUNKS[:c]) * C : sum(CHUNKS[: c + 1]) * C], in_=y_sums[c][:])
+            if c == 3:
+                nc.vector.tensor_copy(out=y[:, sum(CHUNKS[:c]) * C : sum(CHUNKS[: c + 1]) * C], in_=y_sums[c][:])
+            else:
+                nc.scalar.copy(out=y[:, sum(CHUNKS[:c]) * C : sum(CHUNKS[: c + 1]) * C], in_=y_sums[c][:])
 
         pos_sb = (pos1_sb, pos2_sb)
         starts = [sum(STORES[:c]) for c in range(len(STORES))]

@@ -145,21 +145,27 @@ def tile_moe_sup_lin_relu2_kernel(tc, x_words, x_scales, w1_words, w1_scales, w2
         nc.vector.tensor_scalar_max(relu_wide[0][:, 0, :], wide[0][:], 0.0)
         for t0 in range(0, WIDE, WIDE // 2):
             nc.scalar.activation(relu_wide[0][:, 1, t0 : t0 + WIDE // 2], wide[1][:, t0 : t0 + WIDE // 2], ACT.Relu)
-        for t0 in range(0, WIDE, WIDE // 2):
-            relu, pairs = wide_views(0, t0, t0 + WIDE // 2)
+        relu, pairs = wide_views(0, 0, P)
+        nc.vector.tensor_tensor(pairs, relu, relu, ALU.mult)
+        for t0, t1 in ((P, WIDE // 2), (WIDE // 2, WIDE)):
+            relu, pairs = wide_views(0, t0, t1)
             nc.scalar.activation(pairs, relu, ACT.Square)
         relu_block = [keep.tile([P, 2, P], F32, name=f"relu_block{k}", tag=f"relu_block{k}", align_bytes=64) for k in range(BLOCKS)]
         for k in range(BLOCKS):
             t = WIDE + k * P
-            sums = psum.tile([P, 2, P], F32, name=f"block{k}", tag=f"block{k}")
             for b in range(2):
+                sums = psum.tile([P, P], F32, name=f"block{k}{b}", tag=f"block{k}{b}")
                 for s in range(PASSES):
-                    first_layer(sums[:, b, :], 0, b, s, x_narrow[s][:, PACK * k * P : PACK * (k + 1) * P], t, t + P)
-            nc.vector.tensor_scalar_max(relu_block[k][:], sums[:], 0.0)
+                    first_layer(sums[:], 0, b, s, x_narrow[s][:, PACK * k * P : PACK * (k + 1) * P], t, t + P)
+                nc.vector.tensor_scalar_max(relu_block[k][:, b, :], sums[:], 0.0)
         for k in range(BLOCKS):
             t = WIDE + k * P
             relu = relu_block[k][:].rearrange("p b t -> p t b")
-            nc.vector.tensor_tensor(h_pairs[0][:, 2 * t : 2 * (t + P)].rearrange("p (t b) -> p t b", b=2), relu, relu, ALU.mult)
+            pairs = h_pairs[0][:, 2 * t : 2 * (t + P)].rearrange("p (t b) -> p t b", b=2)
+            if k == 0:
+                nc.vector.tensor_tensor(pairs, relu, relu, ALU.mult)
+            else:
+                nc.scalar.activation(pairs, relu, ACT.Square)
 
         def block_relu(k, tag):
             t = WIDE + k * P
@@ -167,14 +173,14 @@ def tile_moe_sup_lin_relu2_kernel(tc, x_words, x_scales, w1_words, w1_scales, w2
             for b in range(2):
                 for s in (2, 0, 1):
                     first_layer(sums[:, b, :], 1, b, s, x_narrow[s][:, PACK * k * P : PACK * (k + 1) * P], t, t + P, first=2)
-            relu = keep.tile([P, P, 2], F32, name=f"relu1{k}", align_bytes=64)
+            relu = keep.tile([P, P, 2], F32, name=f"relu1{k}", tag=("relu_block1", "relu11")[k], align_bytes=64)
             nc.scalar.activation(relu[:], sums[:].rearrange("p b t -> p t b"), ACT.Relu)
             return relu[:], h_pairs[1][:, 2 * t : 2 * (t + P)].rearrange("p (t b) -> p t b", b=2)
 
         relu, pairs = block_relu(0, "warm_up")
         nc.scalar.activation(pairs, relu, ACT.Square)
         for b in range(2):
-            group = psum.tile([P, WIDE], F32, name=f"wide1{b}", tag=f"block{b}")
+            group = psum.tile([P, WIDE], F32, name=f"wide1{b}", tag=f"block0{b}")
             for s in range(PASSES):
                 first_layer(group[:], 1, b, s, x_wide[s][:], 0, WIDE)
             nc.scalar.activation(relu_wide[1][:, b, :], group[:], ACT.Relu)
@@ -190,7 +196,7 @@ def tile_moe_sup_lin_relu2_kernel(tc, x_words, x_scales, w1_words, w1_scales, w2
                 nc.vector.tensor_copy(out=gathered[k][:, u, :], in_=h_pairs[u][:].bitcast(U32).indirect(offs_sb[:, entries]))
 
         pair_width = 2 * N * PACK
-        rounded = [keep.tile([P, 2 * pair_width], BF16, align_bytes=64, name=f"rounded{c}", tag=tag) for c, tag in enumerate(("relu_block1", "relu_block1", "relu_wide1"))]
+        rounded = [keep.tile([P, 2 * pair_width], BF16, align_bytes=64, name=f"rounded{c}", tag=tag) for c, tag in enumerate(("relu_block0", "relu_block0", "relu_wide1"))]
 
         def pair_columns(g):
             return rounded[g // 2][:, (g % 2) * pair_width : (g % 2 + 1) * pair_width]
@@ -223,7 +229,7 @@ def tile_moe_sup_lin_relu2_kernel(tc, x_words, x_scales, w1_words, w1_scales, w2
         )
 
         w2_bytes = keep.tile([P, E * N], U8, align_bytes=64)
-        y_banks = ("wide0", "wide1", "y2", "y3", "warm_up")
+        y_banks = ("wide0", "wide1", "block10", "block11", "warm_up")
         w2_tags = ("w2_codes0", "w2_codes1", "gathered1", "gathered2", "w2_codes4")
         y_sums = []
         e0 = 0

@@ -28,8 +28,6 @@ GATHER = 512
 W2_PARTS = (4, 4, 4)
 CHUNKS = (4, 4, 2, 1, 1)
 STORES = (448, 192, 128)
-WARM_PASSES = 4
-WARM_ROWS = 64
 
 
 def tile_moe_sup_lin_relu2_kernel(tc, x_words, x_scales, w1_words, w1_scales, w2, gate, offs, pos1, pos2, out):
@@ -39,7 +37,7 @@ def tile_moe_sup_lin_relu2_kernel(tc, x_words, x_scales, w1_words, w1_scales, w2
         psum = ctx.enter_context(tc.psum_pool(name="psum", bufs=1))
 
         w1_raw = keep.tile([P, PASSES, 2 * H], U8, align_bytes=64)
-        zeros = keep.tile([P, 2 * PACK * WIDE], U8, align_bytes=64)
+        zeros = keep.tile([P, PASSES * H], U8, align_bytes=64)
         w1_plane = zeros[:, : PASSES * H]
         x_plane = keep.tile([P, PASSES, T], U8, align_bytes=64)
         x_wide = [keep.tile([P, PACK * WIDE], U8, align_bytes=64, name=f"x_wide{s}") for s in range(PASSES)]
@@ -52,9 +50,6 @@ def tile_moe_sup_lin_relu2_kernel(tc, x_words, x_scales, w1_words, w1_scales, w2
         nc.vector.memset(x_plane[:].bitcast(I32), 0)
         nc.vector.memset(table_in[:], 0.0)
         nc.gpsimd.memset(zeros[:].bitcast(I32), 0)
-        zero_codes = keep.tile([P, WIDE], U32, align_bytes=64)
-        zero_bytes = keep.tile([P, WIDE], U8, align_bytes=64)
-        nc.vector.quantize_mx(out=zero_codes[:].bitcast(FP8X4), scales=zero_bytes[:], in_=zeros[:].bitcast(BF16))
 
         w1_scale_rows = w1_scales.rearrange("s (q r) i -> q r s i", r=4)
         for q in range(4):
@@ -107,18 +102,6 @@ def tile_moe_sup_lin_relu2_kernel(tc, x_words, x_scales, w1_words, w1_scales, w2
         nc.sync.dma_start(pos2_sb[:], pos2)
         gate_sb = keep.tile([P, 2, T], F32)
         nc.sync.dma_start(out=gate_sb[:], in_=gate.rearrange("r p t -> p r t"))
-
-        idle = psum.tile([P, WIDE], F32, tag="warm_up")
-        for w in range(WARM_PASSES):
-            nc.tensor.matmul_mx(
-                out=idle[:WARM_ROWS, :],
-                lhsT=zero_codes[:, :WARM_ROWS].bitcast(FP8X4),
-                lhsT_scale=zero_bytes[:, :WARM_ROWS],
-                rhs=zero_codes[:].bitcast(FP8X4),
-                rhs_scale=zero_bytes[:],
-                start=True,
-                stop=True,
-            )
 
         def first_layer(acc, u, b, s, words, t0, t1, first=0):
             nc.tensor.matmul_mx(

@@ -23,11 +23,13 @@ ALU = mybir.AluOpType
 ACT = mybir.ActivationFunctionType
 
 WIDE = 512
-BLOCKS = (T - WIDE) // P
+BLOCK = T - WIDE
+WARM_PASSES = 3
+WARM_ROWS = 32
 GATHER = 512
 W2_PARTS = (4, 4, 4)
 CHUNKS = (4, 4, 2, 1, 1)
-STORES = (448, 192, 128)
+STORES = (224, 256, 192, 96)
 
 
 def tile_moe_sup_lin_relu2_kernel(tc, x_words, x_scales, w1_words, w1_scales, w2, gate, offs, pos1, pos2, out):
@@ -37,56 +39,49 @@ def tile_moe_sup_lin_relu2_kernel(tc, x_words, x_scales, w1_words, w1_scales, w2
         psum = ctx.enter_context(tc.psum_pool(name="psum", bufs=1))
 
         w1_raw = keep.tile([P, PASSES, 2 * H], U8, align_bytes=64)
-        zeros = keep.tile([P, PASSES * H], U8, align_bytes=64)
-        w1_plane = zeros[:, : PASSES * H]
+        w1_plane = keep.tile([P, PASSES * H], U8, align_bytes=64)
         x_plane = keep.tile([P, PASSES, T], U8, align_bytes=64)
-        x_wide = [keep.tile([P, PACK * WIDE], U8, align_bytes=64, name=f"x_wide{s}") for s in range(PASSES)]
-        x_early = keep.tile([P, PASSES - 1, PACK * (T - WIDE)], U8, align_bytes=64)
-        x_late = keep.tile([P, PACK * (T - WIDE)], U8, align_bytes=64)
-        x_narrow = [x_early[:, s, :] for s in range(PASSES - 1)] + [x_late[:]]
+        x_first = keep.tile([P, PASSES - 1, PACK * BLOCK], U8, align_bytes=64)
+        x_rest = keep.tile([P, PASSES, PACK * T], U8, align_bytes=64)
         table_in = keep.tile([P, 8], F32)
         table_out = keep.tile([P, 8], F32)
-        w1_rows = keep.tile([P, PASSES * H // 4], I32)
+        nc.gpsimd.memset(w1_plane[:].bitcast(I32), 0)
         nc.vector.memset(x_plane[:].bitcast(I32), 0)
         nc.vector.memset(table_in[:], 0.0)
-        nc.gpsimd.memset(zeros[:].bitcast(I32), 0)
 
+        x_rows = x_words.rearrange("s p t d -> p s (t d)")
+        w1_rows = w1_words.rearrange("s p b -> p s b")
         w1_scale_rows = w1_scales.rearrange("s (q r) i -> q r s i", r=4)
+        x_scale_rows = x_scales.rearrange("s (q r) t -> r q s t", r=4)
+        nc.scalar.dma_start(out=x_first[:].bitcast(I32), in_=x_rows[:, : PASSES - 1, : PACK * BLOCK].bitcast(I32))
         for q in range(4):
             queue = nc.sync if q < 2 else nc.scalar
             queue.dma_start(
-                out=w1_rows[32 * q : 32 * q + 4, :].rearrange("p (s i) -> p s i", s=PASSES),
+                out=w1_plane[32 * q : 32 * q + 4, :].bitcast(I32).rearrange("p (s i) -> p s i", s=PASSES),
                 in_=w1_scale_rows[q].bitcast(I32),
             )
-        nc.scalar.dma_start(out=w1_raw[:].bitcast(I32), in_=w1_words.rearrange("s p b -> p s b").bitcast(I32))
-        x_rows = x_words.rearrange("s p t d -> p s (t d)")
-        x_scale_rows = x_scales.rearrange("s (q r) t -> r q s t", r=4)
-        nc.scalar.dma_start(out=x_wide[0][:].bitcast(I32), in_=x_rows[:, 0, : PACK * WIDE].bitcast(I32))
+        nc.scalar.dma_start(out=w1_raw[:].bitcast(I32), in_=w1_rows.bitcast(I32))
         nc.scalar.activation(table_out[:], table_in[:], ACT.Square)
         for r in range(4):
             nc.sync.dma_start(out=x_plane[r:P:32, :, :].bitcast(I32), in_=x_scale_rows[r].bitcast(I32))
-        for s in range(1, PASSES):
-            nc.sync.dma_start(out=x_wide[s][:].bitcast(I32), in_=x_rows[:, s, : PACK * WIDE].bitcast(I32))
-        nc.sync.dma_start(out=x_early[:].bitcast(I32), in_=x_rows[:, : PASSES - 1, PACK * WIDE :].bitcast(I32))
-        nc.sync.dma_start(out=x_late[:].bitcast(I32), in_=x_rows[:, PASSES - 1, PACK * WIDE :].bitcast(I32))
-        for q in range(4):
-            rows = slice(32 * q, 32 * q + 4)
-            nc.vector.tensor_copy(out=zeros[rows, : PASSES * H].bitcast(I32), in_=w1_rows[rows, :])
+        for s0, s1, t0, t1 in ((2, 3, 0, 2 * BLOCK), (0, 2, BLOCK, 2 * BLOCK), (0, 3, 2 * BLOCK, T)):
+            nc.sync.dma_start(
+                out=x_rest[:, s0:s1, PACK * t0 : PACK * t1].bitcast(I32),
+                in_=x_rows[:, s0:s1, PACK * t0 : PACK * t1].bitcast(I32),
+            )
 
-        plane_by_group = w1_plane.rearrange("p (s m j) -> p j s m", s=PASSES, j=PACK)
+        plane_by_group = w1_plane[:].rearrange("p (s m j) -> p j s m", s=PASSES, j=PACK)
         words_by_group = w1_raw[:].bitcast(U16).rearrange("p s (m j) -> p j s m", j=PACK)
         w1_codes, w1_bytes = [[], []], [[], []]
-        for u, s0, s1 in [(0, s, s + 1) for s in range(PASSES)] + [(1, 0, PASSES)]:
+        for u, s0, s1 in ((0, 0, 1), (0, 1, 2), (0, 2, 3), (1, 0, 3)):
             codes = keep.tile([P, s1 - s0, H], U8, align_bytes=64, name=f"w1_codes{u}{s0}")
             scales = keep.tile([P, s1 - s0, H // 2], U8, align_bytes=64, name=f"w1_bytes{u}{s0}")
             nc.vector.tensor_copy(
                 out=scales[:].rearrange("p s (b m) -> p b s m", b=2),
                 in_=plane_by_group[:, 2 * u : 2 * u + 2, s0:s1, :],
             )
-            nc.vector.tensor_copy(
-                out=codes[:].bitcast(U16).rearrange("p s (b m) -> p b s m", b=2),
-                in_=words_by_group[:, 2 * u : 2 * u + 2, s0:s1, :],
-            )
+            words = words_by_group[:, 2 * u : 2 * u + 2, s0:s1, :]
+            nc.scalar.copy(out=codes[:].bitcast(U16).rearrange("p s (b m) -> p b s m", b=2), in_=words)
             w1_codes[u].extend(codes[:, s, :] for s in range(s1 - s0))
             w1_bytes[u].extend(scales[:, s, :] for s in range(s1 - s0))
 
@@ -103,74 +98,68 @@ def tile_moe_sup_lin_relu2_kernel(tc, x_words, x_scales, w1_words, w1_scales, w2
         gate_sb = keep.tile([P, 2, T], F32)
         nc.sync.dma_start(out=gate_sb[:], in_=gate.rearrange("r p t -> p r t"))
 
-        def first_layer(acc, u, b, s, words, t0, t1, first=0):
+        idle = psum.tile([P, WIDE], F32, tag="warm_up")
+        first_words = x_first[:].rearrange("p s c -> p (s c)")
+        for w in range(WARM_PASSES):
+            nc.tensor.matmul_mx(
+                out=idle[:WARM_ROWS, :],
+                lhsT=first_words[:, : PACK * WARM_ROWS].bitcast(FP8X4),
+                lhsT_scale=w1_plane[:, :WARM_ROWS],
+                rhs=first_words[:, : PACK * WIDE].bitcast(FP8X4),
+                rhs_scale=w1_plane[:, :WIDE],
+                start=True,
+                stop=True,
+            )
+
+        def first_layer(acc, u, b, s, t0, t1):
+            words = (x_first if t1 <= BLOCK and s < PASSES - 1 else x_rest)[:, s, PACK * t0 : PACK * t1]
             nc.tensor.matmul_mx(
                 out=acc,
                 lhsT=w1_codes[u][s][:, 2 * P * b : 2 * P * (b + 1)].bitcast(FP4X4),
                 lhsT_scale=w1_bytes[u][s][:, P * b : P * (b + 1)],
                 rhs=words.bitcast(FP8X4),
                 rhs_scale=x_plane[:, s, t0:t1],
-                start=(s == first),
-                stop=(s == (first - 1) % PASSES),
+                start=(s == 0),
+                stop=(s == PASSES - 1),
             )
 
         h_pairs = [keep.tile([P, 2 * T], BF16, align_bytes=64, name=f"h_pairs{u}", tag=f"h_pairs{u}") for u in range(2)]
 
-        relu_wide = [keep.tile([P, 2, WIDE], F32, name=f"relu_wide{u}", tag=f"relu_wide{u}", align_bytes=64) for u in range(2)]
+        def views(relu, u, t0, c0, c1):
+            pairs = h_pairs[u][:, 2 * (t0 + c0) : 2 * (t0 + c1)]
+            return relu[:, :, c0:c1].rearrange("p b t -> p t b"), pairs.rearrange("p (t b) -> p t b", b=2)
 
-        def wide_views(u, t0, t1):
-            return relu_wide[u][:, :, t0:t1].rearrange("p b t -> p t b"), h_pairs[u][:, 2 * t0 : 2 * t1].rearrange("p (t b) -> p t b", b=2)
+        for k in range(T // BLOCK):
+            t = k * BLOCK
+            sums = [psum.tile([P, BLOCK], F32, name=f"sums0{k}{b}", tag=f"bank{k}{b}") for b in range(2)]
+            order = [(s, b) for s in range(PASSES) for b in range(2)] if k == 0 else [(s, b) for b in range(2) for s in range(PASSES)]
+            for s, b in order:
+                first_layer(sums[b][:], 0, b, s, t, t + BLOCK)
+            relu = keep.tile([P, 2, BLOCK], F32, name=f"relu0{k}", tag=f"relu0{k}", align_bytes=64)
+            nc.vector.tensor_scalar_max(relu[:, 0, :], sums[0][:], 0.0)
+            nc.scalar.activation(relu[:, 1, :], sums[1][:], ACT.Relu)
+            values, pairs = views(relu, 0, t, 0, BLOCK // 2)
+            nc.vector.tensor_tensor(pairs, values, values, ALU.mult)
+            values, pairs = views(relu, 0, t, BLOCK // 2, BLOCK)
+            nc.scalar.activation(pairs, values, ACT.Square)
 
-        wide = [psum.tile([P, WIDE], F32, name=f"wide0{b}", tag=f"wide{b}") for b in range(2)]
-        for s in range(PASSES):
-            for b in range(2):
-                first_layer(wide[b][:], 0, b, s, x_wide[s][:], 0, WIDE)
-        nc.vector.tensor_scalar_max(relu_wide[0][:, 0, :], wide[0][:], 0.0)
-        for t0 in range(0, WIDE, WIDE // 2):
-            nc.scalar.activation(relu_wide[0][:, 1, t0 : t0 + WIDE // 2], wide[1][:, t0 : t0 + WIDE // 2], ACT.Relu)
-        relu, pairs = wide_views(0, 0, P)
-        nc.vector.tensor_tensor(pairs, relu, relu, ALU.mult)
-        for t0, t1 in ((P, WIDE // 2), (WIDE // 2, WIDE)):
-            relu, pairs = wide_views(0, t0, t1)
-            nc.scalar.activation(pairs, relu, ACT.Square)
-        relu_block = [keep.tile([P, 2, P], F32, name=f"relu_block{k}", tag=f"relu_block{k}", align_bytes=64) for k in range(BLOCKS)]
-        for k in range(BLOCKS):
-            t = WIDE + k * P
-            for b in range(2):
-                sums = psum.tile([P, P], F32, name=f"block{k}{b}", tag=f"block{k}{b}")
-                for s in range(PASSES):
-                    first_layer(sums[:], 0, b, s, x_narrow[s][:, PACK * k * P : PACK * (k + 1) * P], t, t + P)
-                nc.vector.tensor_scalar_max(relu_block[k][:, b, :], sums[:], 0.0)
-        for k in range(BLOCKS):
-            t = WIDE + k * P
-            relu = relu_block[k][:].rearrange("p b t -> p t b")
-            pairs = h_pairs[0][:, 2 * t : 2 * (t + P)].rearrange("p (t b) -> p t b", b=2)
-            if k == 0:
-                nc.vector.tensor_tensor(pairs, relu, relu, ALU.mult)
-            else:
-                nc.scalar.activation(pairs, relu, ACT.Square)
-
-        def block_relu(k, tag):
-            t = WIDE + k * P
-            sums = psum.tile([P, 2, P], F32, name=f"sums{k}", tag=tag)
-            for b in range(2):
-                for s in (2, 0, 1):
-                    first_layer(sums[:, b, :], 1, b, s, x_narrow[s][:, PACK * k * P : PACK * (k + 1) * P], t, t + P, first=2)
-            relu = keep.tile([P, P, 2], F32, name=f"relu1{k}", tag=("relu_block1", "relu11")[k], align_bytes=64)
-            nc.scalar.activation(relu[:], sums[:].rearrange("p b t -> p t b"), ACT.Relu)
-            return relu[:], h_pairs[1][:, 2 * t : 2 * (t + P)].rearrange("p (t b) -> p t b", b=2)
-
-        relu, pairs = block_relu(0, "warm_up")
-        nc.scalar.activation(pairs, relu, ACT.Square)
+        relu_wide = keep.tile([P, 2, WIDE], F32, align_bytes=64)
         for b in range(2):
-            group = psum.tile([P, WIDE], F32, name=f"wide1{b}", tag=f"block0{b}")
+            group = psum.tile([P, WIDE], F32, name=f"wide1{b}", tag=("spare", "warm_up")[b])
             for s in range(PASSES):
-                first_layer(group[:], 1, b, s, x_wide[s][:], 0, WIDE)
-            nc.scalar.activation(relu_wide[1][:, b, :], group[:], ACT.Relu)
-        last_relu, last_pairs = block_relu(1, "spare")
-        relu, pairs = wide_views(1, 0, WIDE)
-        nc.scalar.activation(pairs, relu, ACT.Square)
-        nc.scalar.activation(last_pairs, last_relu, ACT.Square)
+                first_layer(group[:], 1, b, s, BLOCK, T)
+            nc.scalar.activation(relu_wide[:, b, :], group[:], ACT.Relu)
+        sums = psum.tile([P, 2, BLOCK], F32, name="sums1", tag="bank20")
+        for b in range(2):
+            for s in range(PASSES):
+                first_layer(sums[:, b, :], 1, b, s, 0, BLOCK)
+        relu_last = keep.tile([P, BLOCK, 2], F32, tag="relu_last", align_bytes=64)
+        values, pairs = views(relu_wide, 1, BLOCK, 0, WIDE // 2)
+        nc.scalar.activation(pairs, values, ACT.Square)
+        nc.scalar.activation(relu_last[:], sums[:].rearrange("p b t -> p t b"), ACT.Relu)
+        values, pairs = views(relu_wide, 1, BLOCK, WIDE // 2, WIDE)
+        nc.scalar.activation(pairs, values, ACT.Square)
+        nc.scalar.activation(h_pairs[1][:, : 2 * BLOCK].rearrange("p (t b) -> p t b", b=2), relu_last[:], ACT.Square)
 
         gathered = [keep.tile([P, 2, GATHER], U32, name=f"gathered{k}", tag=f"gathered{k}", align_bytes=64) for k in range(SLOTS // GATHER)]
         for u in range(2):
@@ -179,7 +168,7 @@ def tile_moe_sup_lin_relu2_kernel(tc, x_words, x_scales, w1_words, w1_scales, w2
                 nc.vector.tensor_copy(out=gathered[k][:, u, :], in_=h_pairs[u][:].bitcast(U32).indirect(offs_sb[:, entries]))
 
         pair_width = 2 * N * PACK
-        rounded = [keep.tile([P, 2 * pair_width], BF16, align_bytes=64, name=f"rounded{c}", tag=tag) for c, tag in enumerate(("relu_block0", "relu_block0", "relu_wide1"))]
+        rounded = [keep.tile([P, 2 * pair_width], BF16, align_bytes=64, name=f"rounded{c}", tag=tag) for c, tag in enumerate(("relu02", "relu02", "relu_last"))]
 
         def pair_columns(g):
             return rounded[g // 2][:, (g % 2) * pair_width : (g % 2 + 1) * pair_width]
@@ -212,7 +201,7 @@ def tile_moe_sup_lin_relu2_kernel(tc, x_words, x_scales, w1_words, w1_scales, w2
         )
 
         w2_bytes = keep.tile([P, E * N], U8, align_bytes=64)
-        y_banks = ("wide0", "wide1", "block10", "block11", "warm_up")
+        y_banks = ("bank00", "bank01", "bank10", "bank11", "bank21")
         w2_tags = ("w2_codes0", "w2_codes1", "gathered1", "gathered2", "w2_codes4")
         y_sums = []
         e0 = 0
@@ -255,23 +244,29 @@ def tile_moe_sup_lin_relu2_kernel(tc, x_words, x_scales, w1_words, w1_scales, w2
         pos_sb = (pos1_sb, pos2_sb)
         starts = [sum(STORES[:c]) for c in range(len(STORES))]
         terms = [keep.tile([P, 2, n], F32, name=f"terms{c}") for c, n in enumerate(STORES)]
+        picked = [keep.tile([P, 2, n], F32, name=f"picked{c}") for c, n in enumerate(STORES) if c > 0]
 
-        def weigh(c, r):
-            t0, t1 = starts[c], starts[c] + STORES[c]
-            entries = slice(t0 // PER_COLUMN, t1 // PER_COLUMN)
-            nc.vector.tensor_tensor(terms[c][:, r, :], y[:].indirect(pos_sb[r][:, entries]), gate_sb[:, r, t0:t1], ALU.mult)
+        def columns(c, r):
+            entries = slice(starts[c] // PER_COLUMN, (starts[c] + STORES[c]) // PER_COLUMN)
+            return y[:].indirect(pos_sb[r][:, entries])
+
+        def weigh(c):
+            nc.vector.tensor_tensor(terms[c][:], picked[c - 1][:], gate_sb[:, :, starts[c] : starts[c] + STORES[c]], ALU.mult)
 
         def add_and_store(c):
             total = keep.tile([P, STORES[c]], F32, name=f"total{c}")
             nc.vector.tensor_tensor(total[:], terms[c][:, 0, :], terms[c][:, 1, :], ALU.add)
             nc.sync.dma_start(out=out[:, starts[c] : starts[c] + STORES[c]], in_=total[:])
 
-        weigh(0, 0)
-        weigh(0, 1)
-        weigh(1, 0)
+        for r in range(2):
+            nc.vector.tensor_tensor(terms[0][:, r, :], columns(0, r), gate_sb[:, r, : STORES[0]], ALU.mult)
+        for c in range(1, len(STORES)):
+            for r in range(2):
+                nc.scalar.activation(picked[c - 1][:, r, :], columns(c, r), ACT.Copy)
+        weigh(1)
         add_and_store(0)
-        weigh(2, 0)
-        weigh(1, 1)
-        weigh(2, 1)
         add_and_store(1)
+        weigh(2)
+        weigh(3)
         add_and_store(2)
+        add_and_store(3)

@@ -24,7 +24,7 @@ ACT = mybir.ActivationFunctionType
 
 WIDE = 512
 BLOCK = T - WIDE
-WARM_PASSES = 3
+WARM_PASSES = 2
 WARM_ROWS = 32
 GATHER = 512
 W2_PARTS = (4, 4, 4)
@@ -41,34 +41,40 @@ def tile_moe_sup_lin_relu2_kernel(tc, x_words, x_scales, w1_words, w1_scales, w2
         w1_raw = keep.tile([P, PASSES, 2 * H], U8, align_bytes=64)
         w1_plane = keep.tile([P, PASSES * H], U8, align_bytes=64)
         x_plane = keep.tile([P, PASSES, T], U8, align_bytes=64)
-        x_first = keep.tile([P, PASSES - 1, PACK * BLOCK], U8, align_bytes=64)
+        x_landed = keep.tile([P, PASSES, T // 4], I32)
         x_rest = keep.tile([P, PASSES, PACK * T], U8, align_bytes=64)
         table_in = keep.tile([P, 8], F32)
         table_out = keep.tile([P, 8], F32)
-        nc.gpsimd.memset(w1_plane[:].bitcast(I32), 0)
+        nc.vector.memset(w1_plane[:].bitcast(I32), 0)
         nc.vector.memset(x_plane[:].bitcast(I32), 0)
         nc.vector.memset(table_in[:], 0.0)
 
         x_rows = x_words.rearrange("s p t d -> p s (t d)")
         w1_rows = w1_words.rearrange("s p b -> p s b")
         w1_scale_rows = w1_scales.rearrange("s (q r) i -> q r s i", r=4)
-        x_scale_rows = x_scales.rearrange("s (q r) t -> r q s t", r=4)
-        nc.scalar.dma_start(out=x_first[:].bitcast(I32), in_=x_rows[:, : PASSES - 1, : PACK * BLOCK].bitcast(I32))
+        x_scale_rows = x_scales.rearrange("s (q r) t -> q r s t", r=4)
+        for q, queue in ((0, nc.sync), (2, nc.scalar)):
+            queue.dma_start(out=x_landed[32 * q : 32 * q + 4], in_=x_scale_rows[q].bitcast(I32))
+        nc.sync.dma_start(out=x_rest[:, 0, : PACK * WIDE].bitcast(I32), in_=x_rows[:, 0, : PACK * WIDE].bitcast(I32))
         for q in range(4):
             queue = nc.sync if q < 2 else nc.scalar
             queue.dma_start(
                 out=w1_plane[32 * q : 32 * q + 4, :].bitcast(I32).rearrange("p (s i) -> p s i", s=PASSES),
                 in_=w1_scale_rows[q].bitcast(I32),
             )
-        nc.scalar.dma_start(out=w1_raw[:].bitcast(I32), in_=w1_rows.bitcast(I32))
+        nc.sync.dma_start(out=w1_raw[:].bitcast(I32), in_=w1_rows.bitcast(I32))
         nc.scalar.activation(table_out[:], table_in[:], ACT.Square)
-        for r in range(4):
-            nc.sync.dma_start(out=x_plane[r:P:32, :, :].bitcast(I32), in_=x_scale_rows[r].bitcast(I32))
-        for s0, s1, t0, t1 in ((2, 3, 0, 2 * BLOCK), (0, 2, BLOCK, 2 * BLOCK), (0, 3, 2 * BLOCK, T)):
+        for q in (1, 3):
+            nc.sync.dma_start(out=x_plane[32 * q : 32 * q + 4].bitcast(I32), in_=x_scale_rows[q].bitcast(I32))
+        for s0, s1, t0, t1 in ((1, 3, 0, BLOCK), (1, 3, BLOCK, 2 * BLOCK), (0, 2, 2 * BLOCK, T), (2, 3, 2 * BLOCK, T)):
             nc.sync.dma_start(
                 out=x_rest[:, s0:s1, PACK * t0 : PACK * t1].bitcast(I32),
                 in_=x_rows[:, s0:s1, PACK * t0 : PACK * t1].bitcast(I32),
             )
+
+        for q in (0, 2):
+            rows = slice(32 * q, 32 * q + 4)
+            nc.vector.tensor_copy(out=x_plane[rows].bitcast(I32), in_=x_landed[rows])
 
         plane_by_group = w1_plane[:].rearrange("p (s m j) -> p j s m", s=PASSES, j=PACK)
         words_by_group = w1_raw[:].bitcast(U16).rearrange("p s (m j) -> p j s m", j=PACK)
@@ -81,7 +87,10 @@ def tile_moe_sup_lin_relu2_kernel(tc, x_words, x_scales, w1_words, w1_scales, w2
                 in_=plane_by_group[:, 2 * u : 2 * u + 2, s0:s1, :],
             )
             words = words_by_group[:, 2 * u : 2 * u + 2, s0:s1, :]
-            nc.scalar.copy(out=codes[:].bitcast(U16).rearrange("p s (b m) -> p b s m", b=2), in_=words)
+            if (u, s0) == (0, 0):
+                nc.vector.tensor_copy(out=codes[:].bitcast(U16).rearrange("p s (b m) -> p b s m", b=2), in_=words)
+            else:
+                nc.scalar.copy(out=codes[:].bitcast(U16).rearrange("p s (b m) -> p b s m", b=2), in_=words)
             w1_codes[u].extend(codes[:, s, :] for s in range(s1 - s0))
             w1_bytes[u].extend(scales[:, s, :] for s in range(s1 - s0))
 
@@ -99,28 +108,28 @@ def tile_moe_sup_lin_relu2_kernel(tc, x_words, x_scales, w1_words, w1_scales, w2
         nc.sync.dma_start(out=gate_sb[:], in_=gate.rearrange("r p t -> p r t"))
 
         idle = psum.tile([P, WIDE], F32, tag="warm_up")
-        first_words = x_first[:].rearrange("p s c -> p (s c)")
+        first_words = x_rest[:, 0, : PACK * WIDE]
         for w in range(WARM_PASSES):
             nc.tensor.matmul_mx(
                 out=idle[:WARM_ROWS, :],
                 lhsT=first_words[:, : PACK * WARM_ROWS].bitcast(FP8X4),
                 lhsT_scale=w1_plane[:, :WARM_ROWS],
-                rhs=first_words[:, : PACK * WIDE].bitcast(FP8X4),
+                rhs=first_words.bitcast(FP8X4),
                 rhs_scale=w1_plane[:, :WIDE],
                 start=True,
                 stop=True,
             )
 
-        def first_layer(acc, u, b, s, t0, t1):
-            words = (x_first if t1 <= BLOCK and s < PASSES - 1 else x_rest)[:, s, PACK * t0 : PACK * t1]
+        def first_layer(acc, u, b, s, t0, t1, first=0):
+            words = x_rest[:, s, PACK * t0 : PACK * t1]
             nc.tensor.matmul_mx(
                 out=acc,
                 lhsT=w1_codes[u][s][:, 2 * P * b : 2 * P * (b + 1)].bitcast(FP4X4),
                 lhsT_scale=w1_bytes[u][s][:, P * b : P * (b + 1)],
                 rhs=words.bitcast(FP8X4),
                 rhs_scale=x_plane[:, s, t0:t1],
-                start=(s == 0),
-                stop=(s == PASSES - 1),
+                start=(s == first),
+                stop=(s == (first - 1) % PASSES),
             )
 
         h_pairs = [keep.tile([P, 2 * T], BF16, align_bytes=64, name=f"h_pairs{u}", tag=f"h_pairs{u}") for u in range(2)]
@@ -129,12 +138,16 @@ def tile_moe_sup_lin_relu2_kernel(tc, x_words, x_scales, w1_words, w1_scales, w2
             pairs = h_pairs[u][:, 2 * (t0 + c0) : 2 * (t0 + c1)]
             return relu[:, :, c0:c1].rearrange("p b t -> p t b"), pairs.rearrange("p (t b) -> p t b", b=2)
 
+        banks = [[psum.tile([P, BLOCK], F32, name=f"sums0{k}{b}", tag=f"bank{k}{b}") for b in range(2)] for k in range(T // BLOCK)]
+        for k in range(WIDE // BLOCK):
+            for b in range(2):
+                first_layer(banks[k][b][:], 0, b, 0, k * BLOCK, (k + 1) * BLOCK)
         for k in range(T // BLOCK):
             t = k * BLOCK
-            sums = [psum.tile([P, BLOCK], F32, name=f"sums0{k}{b}", tag=f"bank{k}{b}") for b in range(2)]
-            order = [(s, b) for s in range(PASSES) for b in range(2)] if k == 0 else [(s, b) for b in range(2) for s in range(PASSES)]
-            for s, b in order:
-                first_layer(sums[b][:], 0, b, s, t, t + BLOCK)
+            sums = banks[k]
+            for s in range(1 if t < WIDE else 0, PASSES):
+                for b in range(2):
+                    first_layer(sums[b][:], 0, b, s, t, t + BLOCK)
             relu = keep.tile([P, 2, BLOCK], F32, name=f"relu0{k}", tag=f"relu0{k}", align_bytes=64)
             nc.vector.tensor_scalar_max(relu[:, 0, :], sums[0][:], 0.0)
             nc.scalar.activation(relu[:, 1, :], sums[1][:], ACT.Relu)
@@ -143,23 +156,24 @@ def tile_moe_sup_lin_relu2_kernel(tc, x_words, x_scales, w1_words, w1_scales, w2
             values, pairs = views(relu, 0, t, BLOCK // 2, BLOCK)
             nc.scalar.activation(pairs, values, ACT.Square)
 
-        relu_wide = keep.tile([P, 2, WIDE], F32, align_bytes=64)
+        sums = psum.tile([P, 2, BLOCK], F32, name="sums1", tag="spare")
         for b in range(2):
-            group = psum.tile([P, WIDE], F32, name=f"wide1{b}", tag=("spare", "warm_up")[b])
-            for s in range(PASSES):
-                first_layer(group[:], 1, b, s, BLOCK, T)
-            nc.scalar.activation(relu_wide[:, b, :], group[:], ACT.Relu)
-        sums = psum.tile([P, 2, BLOCK], F32, name="sums1", tag="bank20")
+            for s in (2, 0, 1):
+                first_layer(sums[:, b, :], 1, b, s, WIDE, T, first=2)
+        relu_narrow = keep.tile([P, BLOCK, 2], F32, align_bytes=64)
+        nc.scalar.activation(relu_narrow[:], sums[:].rearrange("p b t -> p t b"), ACT.Relu)
+        nc.scalar.activation(h_pairs[1][:, 2 * WIDE :].rearrange("p (t b) -> p t b", b=2), relu_narrow[:], ACT.Square)
+        relu_wide = keep.tile([P, 2, WIDE], F32, tag="relu_last", align_bytes=64)
         for b in range(2):
+            group = psum.tile([P, WIDE], F32, name=f"wide1{b}", tag=f"bank2{b}")
             for s in range(PASSES):
-                first_layer(sums[:, b, :], 1, b, s, 0, BLOCK)
-        relu_last = keep.tile([P, BLOCK, 2], F32, tag="relu_last", align_bytes=64)
-        values, pairs = views(relu_wide, 1, BLOCK, 0, WIDE // 2)
-        nc.scalar.activation(pairs, values, ACT.Square)
-        nc.scalar.activation(relu_last[:], sums[:].rearrange("p b t -> p t b"), ACT.Relu)
-        values, pairs = views(relu_wide, 1, BLOCK, WIDE // 2, WIDE)
-        nc.scalar.activation(pairs, values, ACT.Square)
-        nc.scalar.activation(h_pairs[1][:, : 2 * BLOCK].rearrange("p (t b) -> p t b", b=2), relu_last[:], ACT.Square)
+                first_layer(group[:], 1, b, s, 0, WIDE)
+            for t0 in range(0, WIDE, WIDE if b == 0 else BLOCK):
+                t1 = t0 + (WIDE if b == 0 else BLOCK)
+                nc.scalar.activation(relu_wide[:, b, t0:t1], group[:, t0:t1], ACT.Relu)
+        for t0 in range(0, WIDE, BLOCK):
+            values, pairs = views(relu_wide, 1, 0, t0, t0 + BLOCK)
+            nc.scalar.activation(pairs, values, ACT.Square)
 
         gathered = [keep.tile([P, 2, GATHER], U32, name=f"gathered{k}", tag=f"gathered{k}", align_bytes=64) for k in range(SLOTS // GATHER)]
         for u in range(2):
@@ -201,7 +215,7 @@ def tile_moe_sup_lin_relu2_kernel(tc, x_words, x_scales, w1_words, w1_scales, w2
         )
 
         w2_bytes = keep.tile([P, E * N], U8, align_bytes=64)
-        y_banks = ("bank00", "bank01", "bank10", "bank11", "bank21")
+        y_banks = ("bank00", "bank01", "bank10", "bank11", "warm_up")
         w2_tags = ("w2_codes0", "w2_codes1", "gathered1", "gathered2", "w2_codes4")
         y_sums = []
         e0 = 0
@@ -263,8 +277,8 @@ def tile_moe_sup_lin_relu2_kernel(tc, x_words, x_scales, w1_words, w1_scales, w2
         for c in range(1, len(STORES)):
             for r in range(2):
                 nc.scalar.activation(picked[c - 1][:, r, :], columns(c, r), ACT.Copy)
-        weigh(1)
         add_and_store(0)
+        weigh(1)
         add_and_store(1)
         weigh(2)
         weigh(3)

@@ -29,7 +29,7 @@ WARM_ROWS = 32
 GATHER = 512
 W2_PARTS = (4, 4, 4)
 CHUNKS = (4, 4, 2, 1, 1)
-STORES = (224, 256, 192, 96)
+STORES = (320, 192, 160, 96)
 
 
 def tile_moe_sup_lin_relu2_kernel(tc, x_words, x_scales, w1_words, w1_scales, w2, gate, offs, pos1, pos2, out):
@@ -66,7 +66,7 @@ def tile_moe_sup_lin_relu2_kernel(tc, x_words, x_scales, w1_words, w1_scales, w2
         nc.scalar.activation(table_out[:], table_in[:], ACT.Square)
         for q in (1, 3):
             nc.sync.dma_start(out=x_plane[32 * q : 32 * q + 4].bitcast(I32), in_=x_scale_rows[q].bitcast(I32))
-        for s0, s1, t0, t1 in ((1, 3, 0, BLOCK), (1, 3, BLOCK, 2 * BLOCK), (0, 2, 2 * BLOCK, T), (2, 3, 2 * BLOCK, T)):
+        for s0, s1, t0, t1 in ((1, 2, 0, WIDE), (2, 3, 0, WIDE), (0, 2, 2 * BLOCK, T), (2, 3, 2 * BLOCK, T)):
             nc.sync.dma_start(
                 out=x_rest[:, s0:s1, PACK * t0 : PACK * t1].bitcast(I32),
                 in_=x_rows[:, s0:s1, PACK * t0 : PACK * t1].bitcast(I32),
@@ -139,22 +139,33 @@ def tile_moe_sup_lin_relu2_kernel(tc, x_words, x_scales, w1_words, w1_scales, w2
             return relu[:, :, c0:c1].rearrange("p b t -> p t b"), pairs.rearrange("p (t b) -> p t b", b=2)
 
         banks = [[psum.tile([P, BLOCK], F32, name=f"sums0{k}{b}", tag=f"bank{k}{b}") for b in range(2)] for k in range(T // BLOCK)]
-        for k in range(WIDE // BLOCK):
-            for b in range(2):
-                first_layer(banks[k][b][:], 0, b, 0, k * BLOCK, (k + 1) * BLOCK)
-        for k in range(T // BLOCK):
-            t = k * BLOCK
-            sums = banks[k]
-            for s in range(1 if t < WIDE else 0, PASSES):
+        for s in range(PASSES - 1):
+            for k in range(WIDE // BLOCK):
                 for b in range(2):
-                    first_layer(sums[b][:], 0, b, s, t, t + BLOCK)
-            relu = keep.tile([P, 2, BLOCK], F32, name=f"relu0{k}", tag=f"relu0{k}", align_bytes=64)
-            nc.vector.tensor_scalar_max(relu[:, 0, :], sums[0][:], 0.0)
-            nc.scalar.activation(relu[:, 1, :], sums[1][:], ACT.Relu)
-            values, pairs = views(relu, 0, t, 0, BLOCK // 2)
+                    first_layer(banks[k][b][:], 0, b, s, k * BLOCK, (k + 1) * BLOCK)
+        relu_early = keep.tile([P, 2, WIDE], F32, align_bytes=64)
+        relu_late = keep.tile([P, 2, BLOCK], F32, tag="relu02", align_bytes=64)
+
+        def sums_and_relu(k, relu):
+            t = k * BLOCK
+            for s in range(PASSES - 1 if t < WIDE else 0, PASSES):
+                for b in range(2):
+                    first_layer(banks[k][b][:], 0, b, s, t, t + BLOCK)
+            nc.vector.tensor_scalar_max(relu[:, 0, :], banks[k][0][:], 0.0)
+            nc.scalar.activation(relu[:, 1, :], banks[k][1][:], ACT.Relu)
+
+        def squares(relu, t0, c0):
+            values, pairs = views(relu, 0, t0, c0, c0 + BLOCK // 2)
             nc.vector.tensor_tensor(pairs, values, values, ALU.mult)
-            values, pairs = views(relu, 0, t, BLOCK // 2, BLOCK)
+            values, pairs = views(relu, 0, t0, c0 + BLOCK // 2, c0 + BLOCK)
             nc.scalar.activation(pairs, values, ACT.Square)
+
+        for k in range(2):
+            sums_and_relu(k, relu_early[:, :, k * BLOCK : (k + 1) * BLOCK])
+        for k in range(2):
+            squares(relu_early, 0, k * BLOCK)
+        sums_and_relu(2, relu_late[:])
+        squares(relu_late, WIDE, 0)
 
         sums = psum.tile([P, 2, BLOCK], F32, name="sums1", tag="spare")
         for b in range(2):

@@ -113,9 +113,9 @@ def tile_moe_sup_lin_relu2_kernel(tc, x_words, x_scales, w1_words, w1_scales, w2
             nc.tensor.matmul_mx(
                 out=idle[:WARM_ROWS, :],
                 lhsT=first_words[:, : PACK * WARM_ROWS].bitcast(FP8X4),
-                lhsT_scale=w1_plane[:, :WARM_ROWS],
+                lhsT_scale=first_words[:, :WARM_ROWS],
                 rhs=first_words.bitcast(FP8X4),
-                rhs_scale=w1_plane[:, :WIDE],
+                rhs_scale=first_words[:, :WIDE],
                 start=True,
                 stop=True,
             )
@@ -154,10 +154,10 @@ def tile_moe_sup_lin_relu2_kernel(tc, x_words, x_scales, w1_words, w1_scales, w2
             nc.vector.tensor_scalar_max(relu[:, 0, :], banks[k][0][:], 0.0)
             nc.scalar.activation(relu[:, 1, :], banks[k][1][:], ACT.Relu)
 
-        def squares(relu, t0, c0):
-            values, pairs = views(relu, 0, t0, c0, c0 + BLOCK // 2)
+        def squares(relu, t0, c0, share=BLOCK // 2):
+            values, pairs = views(relu, 0, t0, c0, c0 + share)
             nc.vector.tensor_tensor(pairs, values, values, ALU.mult)
-            values, pairs = views(relu, 0, t0, c0 + BLOCK // 2, c0 + BLOCK)
+            values, pairs = views(relu, 0, t0, c0 + share, c0 + BLOCK)
             nc.scalar.activation(pairs, values, ACT.Square)
 
         for k in range(2):
@@ -165,26 +165,17 @@ def tile_moe_sup_lin_relu2_kernel(tc, x_words, x_scales, w1_words, w1_scales, w2
         for k in range(2):
             squares(relu_early, 0, k * BLOCK)
         sums_and_relu(2, relu_late[:])
-        squares(relu_late, WIDE, 0)
+        squares(relu_late, WIDE, 0, share=112)
 
-        sums = psum.tile([P, 2, BLOCK], F32, name="sums1", tag="spare")
-        for b in range(2):
-            for s in (2, 0, 1):
-                first_layer(sums[:, b, :], 1, b, s, WIDE, T, first=2)
-        relu_narrow = keep.tile([P, BLOCK, 2], F32, align_bytes=64)
-        nc.scalar.activation(relu_narrow[:], sums[:].rearrange("p b t -> p t b"), ACT.Relu)
-        nc.scalar.activation(h_pairs[1][:, 2 * WIDE :].rearrange("p (t b) -> p t b", b=2), relu_narrow[:], ACT.Square)
-        relu_wide = keep.tile([P, 2, WIDE], F32, tag="relu_last", align_bytes=64)
-        for b in range(2):
-            group = psum.tile([P, WIDE], F32, name=f"wide1{b}", tag=f"bank2{b}")
-            for s in range(PASSES):
-                first_layer(group[:], 1, b, s, 0, WIDE)
-            for t0 in range(0, WIDE, WIDE if b == 0 else BLOCK):
-                t1 = t0 + (WIDE if b == 0 else BLOCK)
-                nc.scalar.activation(relu_wide[:, b, t0:t1], group[:, t0:t1], ACT.Relu)
-        for t0 in range(0, WIDE, BLOCK):
-            values, pairs = views(relu_wide, 1, 0, t0, t0 + BLOCK)
-            nc.scalar.activation(pairs, values, ACT.Square)
+        for k, tag, first in ((2, "spare", 2), (0, "bank20", 0), (1, "bank21", 0)):
+            sums = psum.tile([P, 2, BLOCK], F32, name=f"sums1{k}", tag=tag)
+            for b in range(2):
+                for s in range(PASSES):
+                    first_layer(sums[:, b, :], 1, b, (first + s) % PASSES, k * BLOCK, (k + 1) * BLOCK, first=first)
+            relu = keep.tile([P, BLOCK, 2], F32, align_bytes=64, name=f"relu1{k}", tag="relu_last" if k == 1 else f"relu1{k}")
+            nc.scalar.activation(relu[:], sums[:].rearrange("p b t -> p t b"), ACT.Relu)
+            pairs = h_pairs[1][:, 2 * k * BLOCK : 2 * (k + 1) * BLOCK].rearrange("p (t b) -> p t b", b=2)
+            nc.scalar.activation(pairs, relu[:], ACT.Square)
 
         gathered = [keep.tile([P, 2, GATHER], U32, name=f"gathered{k}", tag=f"gathered{k}", align_bytes=64) for k in range(SLOTS // GATHER)]
         for u in range(2):
@@ -288,10 +279,7 @@ def tile_moe_sup_lin_relu2_kernel(tc, x_words, x_scales, w1_words, w1_scales, w2
         for c in range(1, len(STORES)):
             for r in range(2):
                 nc.scalar.activation(picked[c - 1][:, r, :], columns(c, r), ACT.Copy)
-        add_and_store(0)
-        weigh(1)
-        add_and_store(1)
-        weigh(2)
-        weigh(3)
-        add_and_store(2)
-        add_and_store(3)
+        for c in range(1, len(STORES)):
+            weigh(c)
+            add_and_store(c - 1)
+        add_and_store(len(STORES) - 1)

@@ -24,7 +24,7 @@ ACT = mybir.ActivationFunctionType
 
 WIDE = 512
 BLOCK = T - WIDE
-WARM_PASSES = 2
+WARM_WIDTHS = (512, 512, 128)
 WARM_ROWS = 32
 GATHER = 512
 W2_PARTS = (4, 4, 4)
@@ -109,13 +109,13 @@ def tile_moe_sup_lin_relu2_kernel(tc, x_words, x_scales, w1_words, w1_scales, w2
 
         idle = psum.tile([P, WIDE], F32, tag="warm_up")
         first_words = x_rest[:, 0, : PACK * WIDE]
-        for w in range(WARM_PASSES):
+        for width in WARM_WIDTHS:
             nc.tensor.matmul_mx(
-                out=idle[:WARM_ROWS, :],
+                out=idle[:WARM_ROWS, :width],
                 lhsT=first_words[:, : PACK * WARM_ROWS].bitcast(FP8X4),
                 lhsT_scale=first_words[:, :WARM_ROWS],
-                rhs=first_words.bitcast(FP8X4),
-                rhs_scale=first_words[:, :WIDE],
+                rhs=first_words[:, : PACK * width].bitcast(FP8X4),
+                rhs_scale=first_words[:, :width],
                 start=True,
                 stop=True,
             )

@@ -9,6 +9,7 @@ PASSES = K // (P * PACK)
 SLOTS = E * C
 PAIRS = E // 2
 PER_COLUMN = 16
+LINE = 256
 FLOPS = 2 * K * H * T + 2 * H * N * SLOTS
 
 F32 = mybir.dt.float32
@@ -38,11 +39,11 @@ def tile_moe_sup_lin_relu2_kernel(tc, x_words, x_scales, w1_words, w1_scales, w2
         keep = ctx.enter_context(tc.tile_pool(name="keep", bufs=1))
         psum = ctx.enter_context(tc.psum_pool(name="psum", bufs=1))
 
-        w1_raw = keep.tile([P, PASSES, 2 * H], U8, align_bytes=64)
-        w1_plane = keep.tile([P, PASSES * H], U8, align_bytes=64)
-        x_plane = keep.tile([P, PASSES, T], U8, align_bytes=64)
-        x_landed = keep.tile([P, PASSES, T // 4], I32)
-        x_rest = keep.tile([P, PASSES, PACK * T], U8, align_bytes=64)
+        w1_raw = keep.tile([P, PASSES, 2 * H], U8, align_bytes=LINE)
+        w1_plane = keep.tile([P, PASSES * H], U8, align_bytes=LINE)
+        x_plane = keep.tile([P, PASSES, T], U8, align_bytes=LINE)
+        x_landed = keep.tile([P, PASSES, T // 4], I32, align_bytes=LINE)
+        x_rest = keep.tile([P, PASSES, PACK * T], U8, align_bytes=LINE)
         table_in = keep.tile([P, 8], F32)
         table_out = keep.tile([P, 8], F32)
         nc.vector.memset(w1_plane[:].bitcast(I32), 0)
@@ -80,8 +81,8 @@ def tile_moe_sup_lin_relu2_kernel(tc, x_words, x_scales, w1_words, w1_scales, w2
         words_by_group = w1_raw[:].bitcast(U16).rearrange("p s (m j) -> p j s m", j=PACK)
         w1_codes, w1_bytes = [[], []], [[], []]
         for u, s0, s1 in ((0, 0, 1), (0, 1, 2), (0, 2, 3), (1, 0, 3)):
-            codes = keep.tile([P, s1 - s0, H], U8, align_bytes=64, name=f"w1_codes{u}{s0}")
-            scales = keep.tile([P, s1 - s0, H // 2], U8, align_bytes=64, name=f"w1_bytes{u}{s0}")
+            codes = keep.tile([P, s1 - s0, H], U8, align_bytes=LINE, name=f"w1_codes{u}{s0}")
+            scales = keep.tile([P, s1 - s0, H // 2], U8, align_bytes=LINE, name=f"w1_bytes{u}{s0}")
             nc.vector.tensor_copy(
                 out=scales[:].rearrange("p s (b m) -> p b s m", b=2),
                 in_=plane_by_group[:, 2 * u : 2 * u + 2, s0:s1, :],
@@ -98,13 +99,13 @@ def tile_moe_sup_lin_relu2_kernel(tc, x_words, x_scales, w1_words, w1_scales, w2
         nc.sync.dma_start(offs_sb[:], offs)
         w2_raw = {}
         for e0, e1 in ((0, 2), (2, 4), (8, 11), (4, 6), (6, 8), (11, 12)):
-            w2_raw[e0] = keep.tile([P, e1 - e0, PACK * N], F32, name=f"w2_raw{e0}", tag=f"w2_raw{e0}", align_bytes=64)
+            w2_raw[e0] = keep.tile([P, e1 - e0, PACK * N], F32, name=f"w2_raw{e0}", tag=f"w2_raw{e0}", align_bytes=LINE)
             nc.sync.dma_start(out=w2_raw[e0][:], in_=w2[e0:e1].rearrange("e (p j) n -> p e (j n)", j=PACK))
         pos1_sb = keep.tile([P, T // PER_COLUMN], U16)
         nc.sync.dma_start(pos1_sb[:], pos1)
         pos2_sb = keep.tile([P, T // PER_COLUMN], U16)
         nc.sync.dma_start(pos2_sb[:], pos2)
-        gate_sb = keep.tile([P, 2, T], F32)
+        gate_sb = keep.tile([P, 2, T], F32, align_bytes=LINE)
         nc.sync.dma_start(out=gate_sb[:], in_=gate.rearrange("r p t -> p r t"))
 
         idle = psum.tile([P, WIDE], F32, tag="warm_up")
@@ -132,7 +133,7 @@ def tile_moe_sup_lin_relu2_kernel(tc, x_words, x_scales, w1_words, w1_scales, w2
                 stop=(s == (first - 1) % PASSES),
             )
 
-        h_pairs = [keep.tile([P, 2 * T], BF16, align_bytes=64, name=f"h_pairs{u}", tag=f"h_pairs{u}") for u in range(2)]
+        h_pairs = [keep.tile([P, 2 * T], BF16, align_bytes=LINE, name=f"h_pairs{u}", tag=f"h_pairs{u}") for u in range(2)]
 
         def views(relu, u, t0, c0, c1):
             pairs = h_pairs[u][:, 2 * (t0 + c0) : 2 * (t0 + c1)]
@@ -143,8 +144,8 @@ def tile_moe_sup_lin_relu2_kernel(tc, x_words, x_scales, w1_words, w1_scales, w2
             for k in range(WIDE // BLOCK):
                 for b in range(2):
                     first_layer(banks[k][b][:], 0, b, s, k * BLOCK, (k + 1) * BLOCK)
-        relu_early = keep.tile([P, 2, WIDE], F32, align_bytes=64)
-        relu_late = keep.tile([P, 2, BLOCK], F32, tag="relu02", align_bytes=64)
+        relu_early = keep.tile([P, 2, WIDE], F32, align_bytes=LINE)
+        relu_late = keep.tile([P, 2, BLOCK], F32, tag="relu02", align_bytes=LINE)
 
         def sums_and_relu(k, relu):
             t = k * BLOCK
@@ -172,19 +173,19 @@ def tile_moe_sup_lin_relu2_kernel(tc, x_words, x_scales, w1_words, w1_scales, w2
             for b in range(2):
                 for s in range(PASSES):
                     first_layer(sums[:, b, :], 1, b, (first + s) % PASSES, k * BLOCK, (k + 1) * BLOCK, first=first)
-            relu = keep.tile([P, BLOCK, 2], F32, align_bytes=64, name=f"relu1{k}", tag="relu_last" if k == 1 else f"relu1{k}")
+            relu = keep.tile([P, BLOCK, 2], F32, align_bytes=LINE, name=f"relu1{k}", tag="relu_last" if k == 1 else f"relu1{k}")
             nc.scalar.activation(relu[:], sums[:].rearrange("p b t -> p t b"), ACT.Relu)
             pairs = h_pairs[1][:, 2 * k * BLOCK : 2 * (k + 1) * BLOCK].rearrange("p (t b) -> p t b", b=2)
             nc.scalar.activation(pairs, relu[:], ACT.Square)
 
-        gathered = [keep.tile([P, 2, GATHER], U32, name=f"gathered{k}", tag=f"gathered{k}", align_bytes=64) for k in range(SLOTS // GATHER)]
+        gathered = [keep.tile([P, 2, GATHER], U32, name=f"gathered{k}", tag=f"gathered{k}", align_bytes=LINE) for k in range(SLOTS // GATHER)]
         for u in range(2):
             for k in range(SLOTS // GATHER):
                 entries = slice(k * GATHER // PER_COLUMN, (k + 1) * GATHER // PER_COLUMN)
                 nc.vector.tensor_copy(out=gathered[k][:, u, :], in_=h_pairs[u][:].bitcast(U32).indirect(offs_sb[:, entries]))
 
         pair_width = 2 * N * PACK
-        rounded = [keep.tile([P, 2 * pair_width], BF16, align_bytes=64, name=f"rounded{c}", tag=tag) for c, tag in enumerate(("relu02", "relu02", "relu_last"))]
+        rounded = [keep.tile([P, 2 * pair_width], BF16, align_bytes=LINE, name=f"rounded{c}", tag=tag) for c, tag in enumerate(("relu02", "relu02", "relu_last"))]
 
         def pair_columns(g):
             return rounded[g // 2][:, (g % 2) * pair_width : (g % 2 + 1) * pair_width]
@@ -205,7 +206,7 @@ def tile_moe_sup_lin_relu2_kernel(tc, x_words, x_scales, w1_words, w1_scales, w2
 
         woven = []
         for k in range(SLOTS // GATHER):
-            woven.append(keep.tile([P, GATHER * PACK], BF16, align_bytes=64, name=f"woven{k}"))
+            woven.append(keep.tile([P, GATHER * PACK], BF16, align_bytes=LINE, name=f"woven{k}"))
             nc.scalar.copy(
                 out=woven[k][:].bitcast(U32).rearrange("p (s u) -> p s u", u=2),
                 in_=gathered[k][:].rearrange("p u s -> p s u"),
@@ -216,7 +217,7 @@ def tile_moe_sup_lin_relu2_kernel(tc, x_words, x_scales, w1_words, w1_scales, w2
             in_=w2_raw[11][:, 0, :].rearrange("p (j c i) -> p c j i", j=PACK, i=4),
         )
 
-        w2_bytes = keep.tile([P, E * N], U8, align_bytes=64)
+        w2_bytes = keep.tile([P, E * N], U8, align_bytes=LINE)
         y_banks = ("bank00", "bank01", "bank10", "bank11", "warm_up")
         w2_tags = ("w2_codes0", "w2_codes1", "gathered1", "gathered2", "w2_codes4")
         y_sums = []
@@ -224,18 +225,18 @@ def tile_moe_sup_lin_relu2_kernel(tc, x_words, x_scales, w1_words, w1_scales, w2
         for c, n in enumerate(CHUNKS):
             k, first = divmod(e0, 4)
             if first == 0 and c == 2:
-                h_codes = keep.tile([P, 4 * C], U32, align_bytes=64, name=f"h_codes{k}")
-                h_bytes = keep.tile([P, 4 * C], U8, align_bytes=64, name=f"h_bytes{k}")
+                h_codes = keep.tile([P, 4 * C], U32, align_bytes=LINE, name=f"h_codes{k}")
+                h_bytes = keep.tile([P, 4 * C], U8, align_bytes=LINE, name=f"h_bytes{k}")
                 nc.vector.quantize_mx(out=h_codes[:].bitcast(FP8X4), scales=h_bytes[:], in_=woven[k][:])
-            w2_codes = keep.tile([P, n * N], U32, align_bytes=64, name=f"w2_codes{c}", tag=w2_tags[c])
+            w2_codes = keep.tile([P, n * N], U32, align_bytes=LINE, name=f"w2_codes{c}", tag=w2_tags[c])
             nc.vector.quantize_mx(
                 out=w2_codes[:].bitcast(FP8X4),
                 scales=w2_bytes[:, e0 * N : (e0 + n) * N],
                 in_=rounded[k][:, first * N * PACK : (first + n) * N * PACK],
             )
             if first == 0 and c < 2:
-                h_codes = keep.tile([P, 4 * C], U32, align_bytes=64, name=f"h_codes{k}")
-                h_bytes = keep.tile([P, 4 * C], U8, align_bytes=64, name=f"h_bytes{k}")
+                h_codes = keep.tile([P, 4 * C], U32, align_bytes=LINE, name=f"h_codes{k}")
+                h_bytes = keep.tile([P, 4 * C], U8, align_bytes=LINE, name=f"h_bytes{k}")
                 nc.vector.quantize_mx(out=h_codes[:].bitcast(FP8X4), scales=h_bytes[:], in_=woven[k][:])
             y_sums.append(psum.tile([P, n * C], F32, name=f"y_sums{c}", tag=y_banks[c]))
             for m in range(n):
@@ -250,7 +251,7 @@ def tile_moe_sup_lin_relu2_kernel(tc, x_words, x_scales, w1_words, w1_scales, w2
                     stop=True,
                 )
             e0 = e0 + n
-        y = keep.tile([P, SLOTS], F32, tag="w2_raw11", align_bytes=64)
+        y = keep.tile([P, SLOTS], F32, tag="w2_raw11", align_bytes=LINE)
         for c, n in enumerate(CHUNKS):
             if c == 3:
                 nc.vector.tensor_copy(out=y[:, sum(CHUNKS[:c]) * C : sum(CHUNKS[: c + 1]) * C], in_=y_sums[c][:])
@@ -270,7 +271,7 @@ def tile_moe_sup_lin_relu2_kernel(tc, x_words, x_scales, w1_words, w1_scales, w2
             nc.vector.tensor_tensor(terms[c][:], picked[c - 1][:], gate_sb[:, :, starts[c] : starts[c] + STORES[c]], ALU.mult)
 
         def add_and_store(c):
-            total = keep.tile([P, STORES[c]], F32, name=f"total{c}")
+            total = keep.tile([P, STORES[c]], F32, name=f"total{c}", align_bytes=LINE)
             nc.vector.tensor_tensor(total[:], terms[c][:, 0, :], terms[c][:, 1, :], ALU.add)
             nc.sync.dma_start(out=out[:, starts[c] : starts[c] + STORES[c]], in_=total[:])
 

@@ -25,8 +25,7 @@ ACT = mybir.ActivationFunctionType
 
 WIDE = 512
 BLOCK = T - WIDE
-WARM_WIDTHS = (512, 512, 128)
-WARM_ROWS = 32
+WARM_PASSES = ((128, 256), (128, 256), (128, 256), (128, 256), (32, 128))
 GATHER = 512
 W2_PARTS = (4, 4, 4)
 CHUNKS = (4, 4, 2, 1, 1)
@@ -56,7 +55,7 @@ def tile_moe_sup_lin_relu2_kernel(tc, x_words, x_scales, w1_words, w1_scales, w2
         x_scale_rows = x_scales.rearrange("s (q r) t -> q r s t", r=4)
         for q, queue in ((0, nc.sync), (2, nc.scalar)):
             queue.dma_start(out=x_landed[32 * q : 32 * q + 4], in_=x_scale_rows[q].bitcast(I32))
-        nc.sync.dma_start(out=x_rest[:, 0, : PACK * WIDE].bitcast(I32), in_=x_rows[:, 0, : PACK * WIDE].bitcast(I32))
+        nc.sync.dma_start(out=x_rest[:, 0, : PACK * BLOCK].bitcast(I32), in_=x_rows[:, 0, : PACK * BLOCK].bitcast(I32))
         for q in range(4):
             queue = nc.sync if q < 2 else nc.scalar
             queue.dma_start(
@@ -67,7 +66,7 @@ def tile_moe_sup_lin_relu2_kernel(tc, x_words, x_scales, w1_words, w1_scales, w2
         nc.scalar.activation(table_out[:], table_in[:], ACT.Square)
         for q in (1, 3):
             nc.sync.dma_start(out=x_plane[32 * q : 32 * q + 4].bitcast(I32), in_=x_scale_rows[q].bitcast(I32))
-        for s0, s1, t0, t1 in ((1, 2, 0, WIDE), (2, 3, 0, WIDE), (0, 2, 2 * BLOCK, T), (2, 3, 2 * BLOCK, T)):
+        for s0, s1, t0, t1 in ((0, 1, BLOCK, WIDE), (1, 2, 0, WIDE), (2, 3, 0, WIDE), (0, 1, WIDE, T), (1, 2, WIDE, T), (2, 3, WIDE, T)):
             nc.sync.dma_start(
                 out=x_rest[:, s0:s1, PACK * t0 : PACK * t1].bitcast(I32),
                 in_=x_rows[:, s0:s1, PACK * t0 : PACK * t1].bitcast(I32),
@@ -109,12 +108,12 @@ def tile_moe_sup_lin_relu2_kernel(tc, x_words, x_scales, w1_words, w1_scales, w2
         nc.sync.dma_start(out=gate_sb[:], in_=gate.rearrange("r p t -> p r t"))
 
         idle = psum.tile([P, WIDE], F32, tag="warm_up")
-        first_words = x_rest[:, 0, : PACK * WIDE]
-        for width in WARM_WIDTHS:
+        first_words = x_rest[:, 0, : PACK * BLOCK]
+        for rows, width in WARM_PASSES:
             nc.tensor.matmul_mx(
-                out=idle[:WARM_ROWS, :width],
-                lhsT=first_words[:, : PACK * WARM_ROWS].bitcast(FP8X4),
-                lhsT_scale=first_words[:, :WARM_ROWS],
+                out=idle[:rows, :width],
+                lhsT=first_words[:, : PACK * rows].bitcast(FP8X4),
+                lhsT_scale=first_words[:, :rows],
                 rhs=first_words[:, : PACK * width].bitcast(FP8X4),
                 rhs_scale=first_words[:, :width],
                 start=True,

@@ -66,7 +66,7 @@ def tile_moe_sup_lin_relu2_kernel(tc, x_words, x_scales, w1_words, w1_scales, w2
         nc.scalar.activation(table_out[:], table_in[:], ACT.Square)
         for q in (1, 3):
             nc.sync.dma_start(out=x_plane[32 * q : 32 * q + 4].bitcast(I32), in_=x_scale_rows[q].bitcast(I32))
-        for s0, s1, t0, t1 in ((0, 1, BLOCK, WIDE), (1, 2, 0, WIDE), (2, 3, 0, WIDE), (0, 1, WIDE, T), (1, 2, WIDE, T), (2, 3, WIDE, T)):
+        for s0, s1, t0, t1 in [(s, s + 1, t, t + BLOCK) for t in range(0, T, BLOCK) for s in range(PASSES)][1:]:
             nc.sync.dma_start(
                 out=x_rest[:, s0:s1, PACK * t0 : PACK * t1].bitcast(I32),
                 in_=x_rows[:, s0:s1, PACK * t0 : PACK * t1].bitcast(I32),
@@ -87,7 +87,7 @@ def tile_moe_sup_lin_relu2_kernel(tc, x_words, x_scales, w1_words, w1_scales, w2
                 in_=plane_by_group[:, 2 * u : 2 * u + 2, s0:s1, :],
             )
             words = words_by_group[:, 2 * u : 2 * u + 2, s0:s1, :]
-            if (u, s0) == (0, 0):
+            if u == 0:
                 nc.vector.tensor_copy(out=codes[:].bitcast(U16).rearrange("p s (b m) -> p b s m", b=2), in_=words)
             else:
                 nc.scalar.copy(out=codes[:].bitcast(U16).rearrange("p s (b m) -> p b s m", b=2), in_=words)
@@ -139,16 +139,12 @@ def tile_moe_sup_lin_relu2_kernel(tc, x_words, x_scales, w1_words, w1_scales, w2
             return relu[:, :, c0:c1].rearrange("p b t -> p t b"), pairs.rearrange("p (t b) -> p t b", b=2)
 
         banks = [[psum.tile([P, BLOCK], F32, name=f"sums0{k}{b}", tag=f"bank{k}{b}") for b in range(2)] for k in range(T // BLOCK)]
-        for s in range(PASSES - 1):
-            for k in range(WIDE // BLOCK):
-                for b in range(2):
-                    first_layer(banks[k][b][:], 0, b, s, k * BLOCK, (k + 1) * BLOCK)
         relu_early = keep.tile([P, 2, WIDE], F32, align_bytes=LINE)
         relu_late = keep.tile([P, 2, BLOCK], F32, tag="relu02", align_bytes=LINE)
 
         def sums_and_relu(k, relu):
             t = k * BLOCK
-            for s in range(PASSES - 1 if t < WIDE else 0, PASSES):
+            for s in range(PASSES):
                 for b in range(2):
                     first_layer(banks[k][b][:], 0, b, s, t, t + BLOCK)
             nc.vector.tensor_scalar_max(relu[:, 0, :], banks[k][0][:], 0.0)
@@ -162,7 +158,6 @@ def tile_moe_sup_lin_relu2_kernel(tc, x_words, x_scales, w1_words, w1_scales, w2
 
         for k in range(2):
             sums_and_relu(k, relu_early[:, :, k * BLOCK : (k + 1) * BLOCK])
-        for k in range(2):
             squares(relu_early, 0, k * BLOCK)
         sums_and_relu(2, relu_late[:])
         squares(relu_late, WIDE, 0, share=112)

@@ -81,9 +81,9 @@ def tile_moe_sup_lin_relu2_kernel(tc, x_words, x_scales, w1_words, w1_scales, w2
         w1_codes, w1_bytes = [[], []], [[], []]
         for u, s0, s1 in ((0, 0, 1), (0, 1, 2), (0, 2, 3), (1, 0, 3)):
             codes = keep.tile([P, s1 - s0, H], U8, align_bytes=LINE, name=f"w1_codes{u}{s0}")
-            scales = keep.tile([P, s1 - s0, H // 2], U8, align_bytes=LINE, name=f"w1_bytes{u}{s0}")
+            scales = keep.tile([P, s1 - s0, 2, LINE], U8, align_bytes=LINE, name=f"w1_bytes{u}{s0}")
             nc.vector.tensor_copy(
-                out=scales[:].rearrange("p s (b m) -> p b s m", b=2),
+                out=scales[:, :, :, :P].rearrange("p s b m -> p b s m"),
                 in_=plane_by_group[:, 2 * u : 2 * u + 2, s0:s1, :],
             )
             words = words_by_group[:, 2 * u : 2 * u + 2, s0:s1, :]
@@ -92,7 +92,7 @@ def tile_moe_sup_lin_relu2_kernel(tc, x_words, x_scales, w1_words, w1_scales, w2
             else:
                 nc.scalar.copy(out=codes[:].bitcast(U16).rearrange("p s (b m) -> p b s m", b=2), in_=words)
             w1_codes[u].extend(codes[:, s, :] for s in range(s1 - s0))
-            w1_bytes[u].extend(scales[:, s, :] for s in range(s1 - s0))
+            w1_bytes[u].extend(scales[:, s] for s in range(s1 - s0))
 
         offs_sb = keep.tile([P, SLOTS // PER_COLUMN], U16)
         nc.sync.dma_start(offs_sb[:], offs)
@@ -125,7 +125,7 @@ def tile_moe_sup_lin_relu2_kernel(tc, x_words, x_scales, w1_words, w1_scales, w2
             nc.tensor.matmul_mx(
                 out=acc,
                 lhsT=w1_codes[u][s][:, 2 * P * b : 2 * P * (b + 1)].bitcast(FP4X4),
-                lhsT_scale=w1_bytes[u][s][:, P * b : P * (b + 1)],
+                lhsT_scale=w1_bytes[u][s][:, b, :P],
                 rhs=words.bitcast(FP8X4),
                 rhs_scale=x_plane[:, s, t0:t1],
                 start=(s == first),

from contextlib import ExitStack

import concourse.mybir as mybir

K, T, E, C, H, N = 1536, 768, 12, 128, 512, 128
P = 128
PACK = 4
PASSES = K // (P * PACK)
SLOTS = E * C
PAIRS = E // 2
PER_COLUMN = 16
LINE = 256
FLOPS = 2 * K * H * T + 2 * H * N * SLOTS

F32 = mybir.dt.float32
BF16 = mybir.dt.bfloat16
I32 = mybir.dt.int32
U32 = mybir.dt.uint32
U16 = mybir.dt.uint16
U8 = mybir.dt.uint8
FP8X4 = mybir.dt.float8_e4m3fn_x4
FP4X4 = mybir.dt.float4_e2m1fn_x4
ALU = mybir.AluOpType
ACT = mybir.ActivationFunctionType

WIDE = 512
BLOCK = T - WIDE
WARM_PASSES = ((128, 256), (128, 256), (128, 256), (128, 256), (32, 128))
GATHER = 512
W2_PARTS = (4, 4, 4)
CHUNKS = (4, 4, 2, 1, 1)
STORES = (320, 192, 160, 96)


def tile_moe_sup_lin_relu2_kernel(tc, x_words, x_scales, w1_words, w1_scales, w2, gate, offs, pos1, pos2, out):
    nc = tc.nc
    with ExitStack() as ctx:
        keep = ctx.enter_context(tc.tile_pool(name="keep", bufs=1))
        psum = ctx.enter_context(tc.psum_pool(name="psum", bufs=1))

        w1_raw = keep.tile([P, PASSES, 2 * H], U8, align_bytes=LINE)
        w1_plane = keep.tile([P, PASSES * H], U8, align_bytes=LINE)
        x_plane = keep.tile([P, PASSES, T], U8, align_bytes=LINE)
        x_landed = keep.tile([P, PASSES, T // 4], I32, align_bytes=LINE)
        x_rest = keep.tile([P, PASSES, PACK * T], U8, align_bytes=LINE)
        table_in = keep.tile([P, 8], F32)
        table_out = keep.tile([P, 8], F32)
        nc.vector.memset(w1_plane[:].bitcast(I32), 0)
        nc.vector.memset(x_plane[:].bitcast(I32), 0)
        nc.vector.memset(table_in[:], 0.0)

        x_rows = x_words.rearrange("s p t d -> p s (t d)")
        w1_rows = w1_words.rearrange("s p b -> p s b")
        w1_scale_rows = w1_scales.rearrange("s (q r) i -> q r s i", r=4)
        x_scale_rows = x_scales.rearrange("s (q r) t -> q r s t", r=4)
        for q, queue in ((0, nc.sync), (2, nc.scalar)):
            queue.dma_start(out=x_landed[32 * q : 32 * q + 4], in_=x_scale_rows[q].bitcast(I32))
        nc.sync.dma_start(out=x_rest[:, 0, : PACK * BLOCK].bitcast(I32), in_=x_rows[:, 0, : PACK * BLOCK].bitcast(I32))
        for q in range(4):
            queue = nc.sync if q < 2 else nc.scalar
            queue.dma_start(
                out=w1_plane[32 * q : 32 * q + 4, :].bitcast(I32).rearrange("p (s i) -> p s i", s=PASSES),
                in_=w1_scale_rows[q].bitcast(I32),
            )
        nc.sync.dma_start(out=w1_raw[:].bitcast(I32), in_=w1_rows.bitcast(I32))
        nc.scalar.activation(table_out[:], table_in[:], ACT.Square)
        for q in (1, 3):
            nc.sync.dma_start(out=x_plane[32 * q : 32 * q + 4].bitcast(I32), in_=x_scale_rows[q].bitcast(I32))
        for s0, s1, t0, t1 in [(s, s + 1, t, t + BLOCK) for t in range(0, T, BLOCK) for s in range(PASSES)][1:]:
            nc.sync.dma_start(
                out=x_rest[:, s0:s1, PACK * t0 : PACK * t1].bitcast(I32),
                in_=x_rows[:, s0:s1, PACK * t0 : PACK * t1].bitcast(I32),
            )

        for q in (0, 2):
            rows = slice(32 * q, 32 * q + 4)
            nc.vector.tensor_copy(out=x_plane[rows].bitcast(I32), in_=x_landed[rows])

        plane_by_group = w1_plane[:].rearrange("p (s m j) -> p j s m", s=PASSES, j=PACK)
        words_by_group = w1_raw[:].bitcast(U16).rearrange("p s (m j) -> p j s m", j=PACK)
        w1_codes, w1_bytes = [[], []], [[], []]
        for u, s0, s1 in ((0, 0, 1), (0, 1, 2), (0, 2, 3), (1, 0, 3)):
            codes = keep.tile([P, s1 - s0, H], U8, align_bytes=LINE, name=f"w1_codes{u}{s0}")
            scales = keep.tile([P, s1 - s0, 2, LINE], U8, align_bytes=LINE, name=f"w1_bytes{u}{s0}")
            nc.vector.tensor_copy(
                out=scales[:, :, :, :P].rearrange("p s b m -> p b s m"),
                in_=plane_by_group[:, 2 * u : 2 * u + 2, s0:s1, :],
            )
            words = words_by_group[:, 2 * u : 2 * u + 2, s0:s1, :]
            if u == 0:
                nc.vector.tensor_copy(out=codes[:].bitcast(U16).rearrange("p s (b m) -> p b s m", b=2), in_=words)
            else:
                nc.scalar.copy(out=codes[:].bitcast(U16).rearrange("p s (b m) -> p b s m", b=2), in_=words)
            w1_codes[u].extend(codes[:, s, :] for s in range(s1 - s0))
            w1_bytes[u].extend(scales[:, s] for s in range(s1 - s0))

        offs_sb = keep.tile([P, SLOTS // PER_COLUMN], U16)
        nc.sync.dma_start(offs_sb[:], offs)
        w2_raw = {}
        for e0, e1 in ((0, 2), (2, 4), (8, 11), (4, 6), (6, 8), (11, 12)):
            w2_raw[e0] = keep.tile([P, e1 - e0, PACK * N], F32, name=f"w2_raw{e0}", tag=f"w2_raw{e0}", align_bytes=LINE)
            nc.sync.dma_start(out=w2_raw[e0][:], in_=w2[e0:e1].rearrange("e (p j) n -> p e (j n)", j=PACK))
        pos1_sb = keep.tile([P, T // PER_COLUMN], U16)
        nc.sync.dma_start(pos1_sb[:], pos1)
        pos2_sb = keep.tile([P, T // PER_COLUMN], U16)
        nc.sync.dma_start(pos2_sb[:], pos2)
        gate_sb = keep.tile([P, 2, T], F32, align_bytes=LINE)
        nc.sync.dma_start(out=gate_sb[:], in_=gate.rearrange("r p t -> p r t"))

        idle = psum.tile([P, WIDE], F32, tag="warm_up")
        first_words = x_rest[:, 0, : PACK * BLOCK]
        for rows, width in WARM_PASSES:
            nc.tensor.matmul_mx(
                out=idle[:rows, :width],
                lhsT=first_words[:, : PACK * rows].bitcast(FP8X4),
                lhsT_scale=first_words[:, :rows],
                rhs=first_words[:, : PACK * width].bitcast(FP8X4),
                rhs_scale=first_words[:, :width],
                start=True,
                stop=True,
            )

        def first_layer(acc, u, b, s, t0, t1, first=0):
            words = x_rest[:, s, PACK * t0 : PACK * t1]
            nc.tensor.matmul_mx(
                out=acc,
                lhsT=w1_codes[u][s][:, 2 * P * b : 2 * P * (b + 1)].bitcast(FP4X4),
                lhsT_scale=w1_bytes[u][s][:, b, :P],
                rhs=words.bitcast(FP8X4),
                rhs_scale=x_plane[:, s, t0:t1],
                start=(s == first),
                stop=(s == (first - 1) % PASSES),
            )

        h_pairs = [keep.tile([P, 2 * T], BF16, align_bytes=LINE, name=f"h_pairs{u}", tag=f"h_pairs{u}") for u in range(2)]

        def views(relu, u, t0, c0, c1):
            pairs = h_pairs[u][:, 2 * (t0 + c0) : 2 * (t0 + c1)]
            return relu[:, :, c0:c1].rearrange("p b t -> p t b"), pairs.rearrange("p (t b) -> p t b", b=2)

        banks = [[psum.tile([P, BLOCK], F32, name=f"sums0{k}{b}", tag=f"bank{k}{b}") for b in range(2)] for k in range(T // BLOCK)]
        relu_early = keep.tile([P, 2, WIDE], F32, align_bytes=LINE)
        relu_late = keep.tile([P, 2, BLOCK], F32, tag="relu02", align_bytes=LINE)

        def sums_and_relu(k, relu):
            t = k * BLOCK
            for s in range(PASSES):
                for b in range(2):
                    first_layer(banks[k][b][:], 0, b, s, t, t + BLOCK)
            nc.vector.tensor_scalar_max(relu[:, 0, :], banks[k][0][:], 0.0)
            nc.scalar.activation(relu[:, 1, :], banks[k][1][:], ACT.Relu)

        def squares(relu, t0, c0, share=BLOCK // 2):
            values, pairs = views(relu, 0, t0, c0, c0 + share)
            nc.vector.tensor_tensor(pairs, values, values, ALU.mult)
            values, pairs = views(relu, 0, t0, c0 + share, c0 + BLOCK)
            nc.scalar.activation(pairs, values, ACT.Square)

        for k in range(2):
            sums_and_relu(k, relu_early[:, :, k * BLOCK : (k + 1) * BLOCK])
            squares(relu_early, 0, k * BLOCK)
        sums_and_relu(2, relu_late[:])
        squares(relu_late, WIDE, 0, share=112)

        for k, tag, first in ((2, "spare", 2), (0, "bank20", 0), (1, "bank21", 0)):
            sums = psum.tile([P, 2, BLOCK], F32, name=f"sums1{k}", tag=tag)
            for b in range(2):
                for s in range(PASSES):
                    first_layer(sums[:, b, :], 1, b, (first + s) % PASSES, k * BLOCK, (k + 1) * BLOCK, first=first)
            relu = keep.tile([P, BLOCK, 2], F32, align_bytes=LINE, name=f"relu1{k}", tag="relu_last" if k == 1 else f"relu1{k}")
            nc.scalar.activation(relu[:], sums[:].rearrange("p b t -> p t b"), ACT.Relu)
            pairs = h_pairs[1][:, 2 * k * BLOCK : 2 * (k + 1) * BLOCK].rearrange("p (t b) -> p t b", b=2)
            nc.scalar.activation(pairs, relu[:], ACT.Square)

        gathered = [keep.tile([P, 2, GATHER], U32, name=f"gathered{k}", tag=f"gathered{k}", align_bytes=LINE) for k in range(SLOTS // GATHER)]
        for u in range(2):
            for k in range(SLOTS // GATHER):
                entries = slice(k * GATHER // PER_COLUMN, (k + 1) * GATHER // PER_COLUMN)
                nc.vector.tensor_copy(out=gathered[k][:, u, :], in_=h_pairs[u][:].bitcast(U32).indirect(offs_sb[:, entries]))

        pair_width = 2 * N * PACK
        rounded = [keep.tile([P, 2 * pair_width], BF16, align_bytes=LINE, name=f"rounded{c}", tag=tag) for c, tag in enumerate(("relu02", "relu02", "relu_last"))]

        def pair_columns(g):
            return rounded[g // 2][:, (g % 2) * pair_width : (g % 2 + 1) * pair_width]

        for g in (0, 1, 2, 3):
            nc.gpsimd.tensor_scalar(
                pair_columns(g).rearrange("p (e n j) -> p e n j", e=2, j=PACK),
                w2_raw[2 * g][:].rearrange("p e (j n) -> p e n j", j=PACK),
                1.0,
                0.0,
                ALU.mult,
                ALU.add,
            )
        nc.scalar.copy(
            out=rounded[2][:, : 3 * N * PACK].rearrange("p (e c i j) -> p e c j i", e=3, i=4, j=PACK),
            in_=w2_raw[8][:].rearrange("p e (j c i) -> p e c j i", j=PACK, i=4),
        )

        woven = []
        for k in range(SLOTS // GATHER):
            woven.append(keep.tile([P, GATHER * PACK], BF16, align_bytes=LINE, name=f"woven{k}"))
            nc.scalar.copy(
                out=woven[k][:].bitcast(U32).rearrange("p (s u) -> p s u", u=2),
                in_=gathered[k][:].rearrange("p u s -> p s u"),
            )

        nc.scalar.copy(
            out=rounded[2][:, 3 * N * PACK :].rearrange("p (c i j) -> p c j i", i=4, j=PACK),
            in_=w2_raw[11][:, 0, :].rearrange("p (j c i) -> p c j i", j=PACK, i=4),
        )

        w2_bytes = keep.tile([P, E * N], U8, align_bytes=LINE)
        y_banks = ("bank00", "bank01", "bank10", "bank11", "warm_up")
        w2_tags = ("w2_codes0", "w2_codes1", "gathered1", "gathered2", "w2_codes4")
        y_sums = []
        e0 = 0
        for c, n in enumerate(CHUNKS):
            k, first = divmod(e0, 4)
            if first == 0 and c == 2:
                h_codes = keep.tile([P, 4 * C], U32, align_bytes=LINE, name=f"h_codes{k}")
                h_bytes = keep.tile([P, 4 * C], U8, align_bytes=LINE, name=f"h_bytes{k}")
                nc.vector.quantize_mx(out=h_codes[:].bitcast(FP8X4), scales=h_bytes[:], in_=woven[k][:])
            w2_codes = keep.tile([P, n * N], U32, align_bytes=LINE, name=f"w2_codes{c}", tag=w2_tags[c])
            nc.vector.quantize_mx(
                out=w2_codes[:].bitcast(FP8X4),
                scales=w2_bytes[:, e0 * N : (e0 + n) * N],
                in_=rounded[k][:, first * N * PACK : (first + n) * N * PACK],
            )
            if first == 0 and c < 2:
                h_codes = keep.tile([P, 4 * C], U32, align_bytes=LINE, name=f"h_codes{k}")
                h_bytes = keep.tile([P, 4 * C], U8, align_bytes=LINE, name=f"h_bytes{k}")
                nc.vector.quantize_mx(out=h_codes[:].bitcast(FP8X4), scales=h_bytes[:], in_=woven[k][:])
            y_sums.append(psum.tile([P, n * C], F32, name=f"y_sums{c}", tag=y_banks[c]))
            for m in range(n):
                slots = slice((first + m) * C, (first + m + 1) * C)
                nc.tensor.matmul_mx(
                    out=y_sums[c][:, m * C : (m + 1) * C],
                    lhsT=w2_codes[:, m * N : (m + 1) * N].bitcast(FP8X4),
                    lhsT_scale=w2_bytes[:, (e0 + m) * N : (e0 + m + 1) * N],
                    rhs=h_codes[:, slots].bitcast(FP8X4),
                    rhs_scale=h_bytes[:, slots],
                    start=True,
                    stop=True,
                )
            e0 = e0 + n
        y = keep.tile([P, SLOTS], F32, tag="w2_raw11", align_bytes=LINE)
        for c, n in enumerate(CHUNKS):
            if c == 3:
                nc.vector.tensor_copy(out=y[:, sum(CHUNKS[:c]) * C : sum(CHUNKS[: c + 1]) * C], in_=y_sums[c][:])
            else:
                nc.scalar.copy(out=y[:, sum(CHUNKS[:c]) * C : sum(CHUNKS[: c + 1]) * C], in_=y_sums[c][:])

        pos_sb = (pos1_sb, pos2_sb)
        starts = [sum(STORES[:c]) for c in range(len(STORES))]
        terms = [keep.tile([P, 2, n], F32, name=f"terms{c}") for c, n in enumerate(STORES)]
        picked = [keep.tile([P, 2, n], F32, name=f"picked{c}") for c, n in enumerate(STORES) if c > 0]

        def columns(c, r):
            entries = slice(starts[c] // PER_COLUMN, (starts[c] + STORES[c]) // PER_COLUMN)
            return y[:].indirect(pos_sb[r][:, entries])

        def weigh(c):
            nc.vector.tensor_tensor(terms[c][:], picked[c - 1][:], gate_sb[:, :, starts[c] : starts[c] + STORES[c]], ALU.mult)

        def add_and_store(c):
            total = keep.tile([P, STORES[c]], F32, name=f"total{c}", align_bytes=LINE)
            nc.vector.tensor_tensor(total[:], terms[c][:, 0, :], terms[c][:, 1, :], ALU.add)
            nc.sync.dma_start(out=out[:, starts[c] : starts[c] + STORES[c]], in_=total[:])

        for r in range(2):
            nc.vector.tensor_tensor(terms[0][:, r, :], columns(0, r), gate_sb[:, r, : STORES[0]], ALU.mult)
        for c in range(1, len(STORES)):
            for r in range(2):
                nc.scalar.activation(picked[c - 1][:, r, :], columns(c, r), ACT.Copy)
        for c in range(1, len(STORES)):
            weigh(c)
            add_and_store(c - 1)
        add_and_store(len(STORES) - 1)
